import numpy as np, ml_dtypes
CORES = [2,6,10,14,18,22,26,30]
N = 8
import mx_ref
BF = ml_dtypes.bfloat16
def gentries(a):
    return np.ascontiguousarray(a.reshape(8, 16, -1).transpose(0, 2, 1)).reshape(8, -1)
def gtable(e):
    e = np.asarray(e); return np.ascontiguousarray(e.reshape(8, -1, 16).transpose(0, 2, 1)).reshape(128, -1).astype(np.int32)
def gcols(t, e):
    v = np.concatenate([t.reshape(8, 16, -1, 4), np.zeros((8, 16, 1, 4), BF)], axis=2)
    return np.ascontiguousarray(np.stack([v[g][:, e[g]] for g in range(8)])).reshape(128, -1)
def tile(rs):
    return np.stack(rs, axis=2).reshape(128, -1).astype(BF)
def pick(q, e):
    c = np.concatenate([q[0].reshape(128, -1, 4), np.zeros((128, 1, 4), np.uint8)], axis=1); s = np.concatenate([q[1], np.ones((16, 1), np.uint8)], axis=1)
    return (np.ascontiguousarray(c[:, e].reshape(128, -1)), np.ascontiguousarray(s[:, e]))
def join(*qs):
    return (np.concatenate([q[0] for q in qs], axis=1), np.concatenate([q[1] for q in qs], axis=1))
def put(q, e, v):
    c, s = q[0].reshape(128, -1, 4).copy(), q[1].copy(); c[:, e] = v[0].reshape(128, -1, 4); s[:, e] = v[1]
    return (c.reshape(128, -1), s)
def pk(c, s):
    return (np.ascontiguousarray(c), mx_ref.live(s))
def emit(q):
    return q[0], q[1]
def packed(v, rng):
    q = [mx_ref.quantize(np.ascontiguousarray(v[r])) for r in range(N)]
    return np.stack([a for a, b in q]), np.stack([mx_ref.plane(b, rng) for a, b in q])
def values_of_codes():
    e, c = np.zeros((128, 128, 4), np.float32), np.zeros((128, 2, 4), np.uint8)
    e[np.arange(128), np.arange(128), 0] = 1
    c[:127, :, 0] = np.arange(256).reshape(2, 128).T[:127]
    return mx_ref.matmul(mx_ref.quantize(e.reshape(128, 512).astype(BF)), (c.reshape(128, 8), np.full((16, 2), 127, np.uint8))).T.reshape(-1).astype(np.float64)
CODE_VALUE, SCALE_VALUE = values_of_codes(), 2.0 ** (np.arange(256) - 127.0)
def decode(q):
    return (CODE_VALUE[q[0]].reshape(16, 8, -1, 4) * SCALE_VALUE[q[1]][:, None, :, None] + 0.0).reshape(128, -1).astype(np.float32)
def f(rng, *shape):
    return mx_ref.flush((rng.standard_normal(shape, dtype=np.float32) * np.exp2(rng.integers(-2, 3, shape[:-1] + (1,)))).astype(BF))
def wide(rng, *shape, cols=0):
    v = rng.standard_normal(shape, dtype=np.float32) * np.exp2(rng.integers(-12, 13, shape)).astype(np.float32)
    if cols: v *= np.repeat(np.exp2(rng.integers(-cols, cols + 1, shape[:-2] + (1, shape[-1] // 4))) * (rng.random(shape[:-2] + (1, shape[-1] // 4)) > 0.0625), 4, axis=-1).astype(np.float32)
    return mx_ref.flush(v.astype(BF))
C, HALF, E = 256, 128, 192
MASK = [1, 2, 4]
TIMES = 8
def register(b):
    a = 2 * np.arange(HALF)
    return np.concatenate([a + b, a + 1 - b], axis=-1)
def lowest(s):
    low, to = np.broadcast_to(np.arange(C), s.shape), s
    for i in range(TIMES):
        low = np.minimum(low, np.take_along_axis(low, to, axis=-1))
        to = np.take_along_axis(to, to, axis=-1)
    return low
def joined(s):
    low, c = lowest(s), np.arange(HALF)
    a, b = low[..., :HALF], low[..., HALF:]
    swap = (a != b) & ((a == c) & (c > 0) | (b == c + HALF))
    return np.concatenate([np.where(swap, s[..., HALF:], s[..., :HALF]), np.where(swap, s[..., :HALF], s[..., HALF:])], axis=-1)
def numbers_of(rng):
    return {"x": np.array(f(rng, N, 128, 4 * C)), "u": np.array(f(rng, N, 128, 512)), "v": np.array(f(rng, N, 128, 512))}
def orders(rng):
    return rng.permuted(np.tile(np.arange(C), (N, 8, 1)), axis=2)
def stored(k):
    return {"kl": np.stack([gtable(k[r]) for r in range(N)])}
def layers(rng):
    return np.array(f(rng, N, 128, 2048)).reshape(N, 8, 16, 4, 8, 16, 4)
def weights(rng, w):
    c, p = packed(np.ascontiguousarray(w).reshape(N, 128, 2048), rng)
    return {"wc": c, "ws": p}
def setup_inputs(rng):
    return {**numbers_of(rng), **stored(orders(rng)), **weights(rng, layers(rng))}
def setup_inputs_ties(rng):
    d = numbers_of(rng)
    o = rng.permutation(N)
    k = rng.integers(-1, 2, (N, 8, C)).astype(np.float32)
    k[o[1]] = 1
    x = d["x"].reshape(N, 8, 16, C, 4)
    x[:, :, 0] = 0
    x[:, :, 0, :, 0] = k.astype(BF)
    a = np.exp2(rng.integers(-3, 4, (8, 1)).astype(np.float64))
    j = rng.integers(3, 7, (8, 4, 6))
    j[:, :, 0] = 6
    q = (9 + 2 * rng.integers(0, 4, (8, 4, 6))) * 0.125 * np.exp2(-j.astype(np.float64))
    x[:, :, 8:] = 0
    x[:, :, 8, :, 0] = (-3.0 * a).astype(np.float32).astype(BF)
    x[:, :, 10, :, 0] = (-0.140625 * a).astype(np.float32).astype(BF)
    x[:, :, 10, :, 1] = (-0.125 * a).astype(np.float32).astype(BF)
    c = np.ones(N, np.float32)
    c[o[0]] = 0
    c[o[2]] = -1
    u = d["u"].reshape(N, 128, 128, 4)
    u[:, :, ::16] = 0
    for h in range(0, 128, 16): u[:, h, h, 0] = c.astype(BF)
    w = layers(rng)
    w[:, :, 0] = 0
    w[:, :, :, :, :, 0] = 0
    w[:, :, :, :, :, 8:] = 0
    for g in range(8): w[:, g, 10, 0, g, 8, 0] = -224.0
    for n, i in enumerate((9, 11, 12, 13, 14, 15)):
        x[:, :, i] = (q[:, :, n] * a * -0.0078125)[:, None].astype(np.float32).astype(BF)
        for g in range(8): w[:, g, 10, :, g, i, 1] = (-q[g, :, n]).astype(np.float32).astype(BF)
    return {"x": x.reshape(N, 128, 4 * C), "u": u.reshape(N, 128, 512), "v": d["v"], **stored(orders(rng)), **weights(rng, w)}
def setup_inputs_near(rng):
    d = numbers_of(rng)
    o = rng.permutation(N) % 4
    k = np.where((o == 1) | (o == 2), 1.0, 2.0 ** -30).astype(np.float32)
    x = d["x"].astype(np.float32).reshape(N, 8, 16, C, 4)
    x[:, :, :8] = 0
    s = rng.integers(-1, 2, (N, 8, C)) * k[:, None, None]
    s[o == 3] = 0
    x[:, :, 0, :, 0] = 1.125 * s
    x[:, :, 1, :, 0] = -1.25 * s
    x[:, :, 7, :, 0] = 2.0 ** -30
    w = layers(rng)
    w[:, :, :8] = 0
    w[:, :, :, :, :, :8] = 0
    for r in range(N):
        if o[r] == 3:
            x[r, :, 4, :, 0] = rng.choice([-1.0, 1.0], (8, C)) * 2.0 ** -30
            for g in range(8):
                w[r, g, 4, 0, g, 0, 0] = 1.125 * 2.0 ** -8
                w[r, g, 4, 0, g, 1, 0] = -1.25 * 2.0 ** -8
                w[r, g, 7, 0, g, 6, 0] = 2.0 ** 5
        at = [0, C - 1, int(rng.integers(C)), int(rng.integers(C))]
        for g, j in zip(rng.permutation(8)[:4], at): x[r, g, 0, j, 0] = 2.0 ** 30 * rng.choice([-1.0, 1.0])
    u = d["u"].reshape(N, 128, 128, 4)
    u[:, :, ::16] = 0
    for h in range(0, 128, 16):
        u[:, h, h, 0] = (1.125 * k).astype(np.float32).astype(BF)
        u[:, h + 1, h, 0] = k.astype(BF)
    return {"x": x.reshape(N, 128, 4 * C).astype(BF), "u": u.reshape(N, 128, 512), "v": d["v"], **stored(orders(rng)), **weights(rng, w)}
def setup_inputs_long(rng):
    d = numbers_of(rng)
    k = orders(rng)
    b = rng.integers(0, 2, (N, 8, HALF))
    for c in rng.permutation(HALF):
        low = lowest(register(b))
        b[..., c] ^= (low[..., c] != low[..., c + HALF]).astype(np.int64)
    last = HALF - 1 - (HALF - 1) // 2
    way = [last >> i for i in range(last.bit_length() - 1, -1, -1)]
    for r in range(N):
        t = rng.permutation(8)
        for g in t[2:4]: b[r, g, rng.integers(1, HALF)] ^= 1
        b[r, t[4], 0] ^= 1
        for g in t[5:]: b[r, g] = rng.integers(0, 2, HALF)
        for g in t[5:7]:
            b[r, g, HALF - 1] = 0
            for i, j in zip(way, way[1:]): b[r, g, HALF - 1 - i] = j & 1
            b[r, g, HALF - 1 - last] = 1 - (HALF - 1) % 2
    s = np.zeros((N, 8, C))
    np.put_along_axis(s, k, np.concatenate([b, rng.integers(0, 2, (N, 8, HALF))], axis=2) * 2.0 - 1.0, axis=2)
    x = d["x"].reshape(N, 8, 16, C, 4)
    x[:, :, 0] = 0
    x[:, :, 0, :, 0] = (s * np.exp2(rng.integers(-3, 4, (N, 8, C)).astype(np.float64))).astype(np.float32).astype(BF)
    u = d["u"].reshape(N, 128, 128, 4)
    u[:, :, ::16] = 0
    for h in range(0, 128, 16): u[:, h, h, 0] = 1
    w = layers(rng)
    w[:, :, :, :, :, 0] = (w[:, :, :, :, :, 0].astype(np.float32) * 4).astype(BF)
    return {"x": x.reshape(N, 128, 4 * C), "u": u.reshape(N, 128, 512), "v": d["v"], **stored(k), **weights(rng, w)}
def setup_inputs_ends(rng):
    d = numbers_of(rng)
    o, e = rng.permutation(N) % 4, rng.permutation(N) % 4
    k = orders(rng)
    x = np.zeros((N, 8, 16, C, 4))
    u = d["u"].astype(np.float32).reshape(N, 128, 128, 4)
    v = np.zeros((N, 128, 512))
    w = np.zeros((N, 128, 4, 128, 4), np.float32)
    i = np.arange(128)[np.arange(128) % 16 < 15]
    j = np.arange(14, 128, 16)
    up, down = np.arange(C), np.arange(C)[::-1]
    for r in range(N):
        if e[r] == 0: k[r] = up
        if e[r] == 1: k[r] = down
        if e[r] == 2: k[r] = np.where(rng.permutation(8)[:, None] < 4, up, down)
        h = rng.permutation(8)
        c = np.where(h < 2, 0.0, h % 2 * 2.0 - 1.0)[None, :, None]
        much = (0.9 + 0.1 * rng.random((8, 16, C, 4))) * 2.0 ** 29
        if o[r] == 0: x[r] = -much
        if o[r] == 1: x[r] = much * rng.choice([-1.0, 1.0], (1, 1, C, 1))
        if o[r] == 2: x[r] = -(1.0 + 0.125 * rng.integers(0, 8, (8, 16, C, 4))) * 2.0 ** -30
        if o[r] == 3: x[r] = d["x"][r].astype(np.float32).reshape(8, 16, C, 4)[:, :, :1]
        x[r, :, 15] = 2.0 ** -30
        if o[r] < 2:
            u[r, :, ::16] = c * (0.9 + 0.1 * rng.random((128, 8, 4))) * 2.0 ** 30
            v[r] = (0.9 + 0.1 * rng.random((128, 512))) * 2.0 ** 30
        else:
            v[r] = (1.0 + 0.125 * rng.integers(0, 8, (128, 512))) * 2.0 ** -30
        if o[r] == 2: u[r, :, ::16] = c * (1.0 + 0.125 * rng.integers(0, 8, (128, 8, 4))) * 2.0 ** -30
        if o[r] == 3: u[r, :, ::16] *= np.abs(c).astype(np.float32)
        n = np.array([1.0, 2.0, 4.0])[rng.permutation(8) % 3]
        for b in range(4):
            if o[r] != 2: w[r, i, b, i, b] = -n[i // 16]
            else:
                w[r, i, b, i, b] = -2.0 ** -8
                w[r, j, b, j, b] = 0.0
                w[r, j + 1, b, j, b] = 2.0 ** 8
                w[r, j - 8, b, j - 8, b] = 0.0
                w[r, j + 1, b, j - 8, b] = 2.0 ** 5
    v = v * rng.choice([-1.0, 1.0], (N, 128, 512))
    return {"x": x.astype(np.float32).reshape(N, 128, 4 * C).astype(BF), "u": u.reshape(N, 128, 512).astype(BF), "v": v.astype(np.float32).astype(BF), **stored(k), **weights(rng, w.astype(BF))}
def setup_inputs_spread(rng):
    d = setup_inputs(rng)
    d["x"] = wide(rng, N, 128, 4 * C, cols=6)
    return d
def check_inputs(d):
    b = []
    for k in ("x", "u", "v"):
        a = np.abs(d[k].astype(np.float32))
        if not (np.isfinite(a).all() and ((a == 0) | (a >= 2.0 ** -30) & (a <= 2.0 ** 30)).all()): b.append("a value of " + k)
    none, least, most = [emit(mx_ref.quantize(np.full((128, 16), k, np.float32).astype(BF)))[1][0, 0] for k in (0.0, 2.0 ** -8, 2.0 ** 8)]
    for r in range(N):
        if not (np.sort(gentries(d["kl"][r]), axis=1) == np.arange(C)).all(): b.append("kl: not a permutation")
        if ((d["wc"][r] == 0x7F) | (d["wc"][r] == 0xFF)).any(): b.append("wc: a code that is no number")
        s = mx_ref.live(d["ws"][r])
        if ((s != none) & ((s < least) | (s > most))).any(): b.append("ws: a scale out of range")
    return b
def reference(x, u, v, kl, wc, ws):
    qu = [mx_ref.quantize(u[r]) for r in range(N)]
    lay = [pk(wc[r], ws[r]) for r in range(N)]
    now = [x[r] for r in range(N)]
    k = [gentries(kl[r]).astype(np.int64) for r in range(N)]
    for m in MASK:
        e, made = [], []
        for r in range(N):
            s = mx_ref.matmul(qu[r], mx_ref.quantize(now[r]))[::16]
            bits = (np.take_along_axis(s, k[r][:, :HALF], axis=1) > 0).astype(np.int64)
            e.append(np.take_along_axis(k[r], joined(register(bits)), axis=1))
            z = (gcols(now[r], k[r]).astype(np.float32) + gcols(now[r], e[r]).astype(np.float32)) * np.float32(0.5)
            q = mx_ref.quantize(z.astype(BF))
            made.append(tile([mx_ref.matmul(pick(lay[r], np.arange(128 * b, 128 * b + 128)), q) * np.float32(0.03125) for b in range(4)]))
        k = [np.take_along_axis(k[r ^ m], e[r], axis=1) for r in range(N)]
        for r in range(N):
            far = decode(mx_ref.quantize(np.ascontiguousarray(made[r ^ m][:, :4 * E]))).astype(BF)
            both = np.concatenate([far, made[r][:, 4 * E:]], axis=1)
            now[r] = (now[r].astype(np.float32) + gcols(both, k[r]).astype(np.float32)).astype(BF)
    y, kp = np.zeros((N, 128, C), np.float32), np.zeros((N, 8, C), np.float32)
    oc, osc = np.zeros((N, 128, 4 * C), np.uint8), np.zeros((N, 16, C), np.uint8)
    for r in range(N):
        q = mx_ref.quantize(now[r])
        y[r] = mx_ref.matmul(mx_ref.quantize(v[r]), q)
        kp[r] = k[r]
        oc[r], osc[r] = emit(q)
    return {"y": y, "kp": kp, "oc": oc, "osc": osc}

@@ -1,0 +1,490 @@
+from concourse.bass import DstId, RemoteDMATransfer
+from concourse.mybir import dt, AluOpType, ActivationFunctionType
+
+ROUNDS = 3
+LIFT = 512.0
+SINGLE = False
+SHARE = 32
+A = AluOpType
+CP = ActivationFunctionType.Copy
+
+SCRATCH = {
+    "ps": ("psum", [128, 4096], "float32"),
+    "kli": ("sbuf", [128, 16], "int32"),
+    "ut": ("sbuf", [128, 512], "bfloat16"),
+    "vt": ("sbuf", [128, 512], "bfloat16"),
+    "uq": ("sbuf", [128, 128], "float8_e4m3fn_x4"), "us": ("sbuf", [128, 128], "uint8"),
+    "up": ("sbuf", [128, 128], "float8_e4m3fn_x4"), "ups": ("sbuf", [128, 128], "uint8"),
+    "vq": ("sbuf", [128, 128], "float8_e4m3fn_x4"), "vqs": ("sbuf", [128, 128], "uint8"),
+    "wq": ("sbuf", [128, 512], "float8_e4m3fn_x4"), "wqs": ("sbuf", [128, 512], "uint8"),
+    "ones": ("sbuf", [128, 512], "bfloat16"),
+    "et": ("sbuf", [128, 2048], "bfloat16"),
+    "eq": ("sbuf", [128, 512], "float8_e4m3fn_x4"), "es": ("sbuf", [128, 512], "uint8"),
+    "pi": ("sbuf", [128, 8], "int32"),
+    "cs": ("sbuf", [128, 24], "float32"),
+    "i16": ("sbuf", [128, 16], "float32"), "ms": ("sbuf", [128, 64], "bfloat16"), "mw": ("sbuf", [128, 32], "bfloat16"),
+    "oq": ("sbuf", [128, 16], "uint16"), "ot": ("sbuf", [128, 16], "uint16"),
+    "mt": ("sbuf", [128, 512], "bfloat16"),
+    "d0": ("sbuf", [128, 160], "float32"), "d1": ("sbuf", [128, 160], "float32"),
+    "one": ("sbuf", [128, 256], "bfloat16"),
+    "c21": ("sbuf", [128, 128], "bfloat16"), "c43": ("sbuf", [128, 128], "float32"),
+    "ci": ("sbuf", [128, 40], "float32"), "cc": ("sbuf", [128, 120], "float32"),
+    "cmp": ("sbuf", [128, 80], "float32"), "c127": ("sbuf", [128, 24], "float32"), "mk": ("sbuf", [128, 448], "bfloat16"),
+    "uo": ("sbuf", [128, 8], "uint16"),
+    "kyf": ("sbuf", [128, 256], "float32"),
+    "yo": ("sbuf", [128, 256], "float32"),
+    "x0": ("sbuf", [128, 1024], "bfloat16"),
+}
+for _r in range(ROUNDS + 1):
+    if _r:
+        SCRATCH["x%d" % _r] = ("sbuf", [128, 1024], "bfloat16")
+    SCRATCH["xq%d" % _r] = ("sbuf", [128, 256], "float8_e4m3fn_x4")
+    SCRATCH["xs%d" % _r] = ("sbuf", [128, 256], "uint8")
+for _r in range(ROUNDS):
+    for _n, _w, _d in (("xk", 1024, "bfloat16"), ("xj", 1024, "bfloat16"), ("lc", 8 * 256, "bfloat16"), ("z", 1024, "bfloat16"), ("h", 768, "bfloat16"), ("b", 1024, "bfloat16"),
+                       ("bit", 272, "bfloat16"), ("w", 8 * 256, "bfloat16"), ("low", 8 * 256, "bfloat16"),
+                       ("sc", 14 * 256, "bfloat16"), ("fr", 4 * 256, "bfloat16"), ("sm", 48, "float32"), ("so", 160, "float32"),
+                       ("to", 8 * 16, "uint16"), ("tt", 80, "uint16"),
+                       ("kf", 24, "float32"), ("k16_", 16, "uint16"), ("kb", 8, "uint16"), ("k4_", 64, "uint16"),
+                       ("kin", 16, "uint16")):
+        SCRATCH["%s%d" % (_n, _r)] = ("sbuf", [128, _w], _d)
+    for _n, _w in (("qz", 384), ("qh", 256), ("cin", 192)):
+        SCRATCH["%s_%d" % (_n, _r)] = ("sbuf", [128, _w], "float8_e4m3fn_x4")
+        SCRATCH["%ss_%d" % (_n, _r)] = ("sbuf", [128, _w], "uint8")
+SCRATCH["k4_3"] = ("sbuf", [128, 64], "uint16")
+
+SEMAPHORES = ["sv", "sa", "st", "sg", "dx", "du", "dk", "dwc", "dws", "dv", "dxk", "dout", "loc"]
+SEMAPHORES += ["%s%d" % (n, r) for r in range(ROUNDS) for n in ("rk", "ra", "rb")]
+
+
+def rank_program(g, core, T, topo):
+    rank = T.rank_of(core)
+    if rank is None:
+        return
+    queues = {"v": g.vector, "a": g.scalar, "t": g.tensor, "g": g, "y": g.sync}
+    own = {"v": "sv", "a": "sa", "t": "st", "g": "sg"}
+    done = {"sv": 0, "sa": 0, "st": 0, "sg": 0}
+    seen = {q: {} for q in queues}
+
+    def wait(q, *toks):
+        need = {}
+        for t in toks:
+            if t is not None:
+                need[t[0]] = max(need.get(t[0], 0), t[1])
+        for s, n in need.items():
+            if seen[q].get(s, 0) < n:
+                queues[q].wait_ge(T.sem[s], n)
+                seen[q][s] = n
+
+    def fin(q, ins):
+        s = own[q]
+        ins.then_inc(T.sem[s], 1)
+        done[s] += 1
+        return (s, done[s])
+
+    def dma(q, sem, total, out, in_):
+        queues[q].dma_start(out, in_).then_inc(T.sem[sem], 16)
+        return (sem, total)
+
+    def ts(out, in0, s1, s2, op0, op1, *toks):
+        wait("v", *toks)
+        if op1 is None:
+            return fin("v", g.vector.tensor_scalar(out, in0, s1, None, op0))
+        return fin("v", g.vector.tensor_scalar(out, in0, s1, s2, op0, op1))
+
+    def tt(out, in0, in1, op, *toks):
+        wait("v", *toks)
+        return fin("v", g.vector.tensor_tensor(out, in0, in1, op))
+
+    def vcopy(out, in_, *toks):
+        wait("v", *toks)
+        return fin("v", g.vector.tensor_copy(out, in_))
+
+    def scan(out, mask, data, *toks):
+        wait("v", *toks)
+        return fin("v", g.vector.tensor_tensor_scan(out, mask, data, 0.0, A.mult, A.max))
+
+    def chain(out, mul, add, *toks):
+        wait("v", *toks)
+        return fin("v", g.vector.tensor_tensor_scan(out, mul, add, 0.0, A.mult, A.add))
+
+    def quant(codes, plane, tile, *toks):
+        wait("v", *toks)
+        return fin("v", g.vector.quantize_mx(codes, plane, tile))
+
+    def act(out, in_, scale, *toks):
+        wait("a", *toks)
+        if scale is None:
+            return fin("a", g.scalar.activation(out, in_, CP))
+        return fin("a", g.scalar.activation(out, in_, CP, scale=scale))
+
+    def mm(bank, n, lq, ls, rq, rs, *toks):
+        wait("t", *toks)
+        return fin("t", g.tensor.matmul_mx(T.ps[:, 512 * bank:512 * bank + n], lq, ls, rq, rs, True, True))
+
+    def psv(bank, a, b):
+        return T.ps[:, 512 * bank + a:512 * bank + b]
+
+    def remote(r, out, in_, sem):
+        dst = T.cores[rank ^ (1 << r)]
+        rid, pid, _ = topo.addr(dst)
+        ne = len(topo.engines(core, dst))
+        g.remote_dma(out, in_, T.sem[sem], T.sem.loc, pid, rid, topo.mask(core, dst))
+        loc[0] += ne
+        return ne
+
+    loc = [0]
+    cs, d0, d1 = T.cs, T.d0, T.d1
+
+    t_kl = dma("y", "dk", 16, T.kli[:], T.kl[:])
+    t_x = dma("y", "dx", 16, T.x0[:], T.x[:])
+    t_u = dma("a", "du", 16, T.ut[:], T.u[:])
+    t_wc = dma("y", "dwc", 16, T.wq[:, 0:512].bitcast(dt.uint8), T.wc[:])
+    t_ws = dma("y", "dws", 16, T.wqs[:], T.ws[:])
+    t_v = dma("y", "dv", 16, T.vt[:], T.v[:])
+
+    def iota(out, pat, base, ch, small=True):
+        if small:
+            return fin("g", g.iota(out, pat, base, ch, allow_small_or_imprecise_dtypes=True))
+        return fin("g", g.iota(out, pat, base, ch))
+    g_pi = iota(T.pi[:, 0:1], [[0, 1]], 0, 1, False)
+    g_is = iota(T.i16[:], [[1, 16]], 0, 0)
+    g_ci = iota(T.ci[:, 32:40], [[16, 8]], 0, 0)
+    g_ci4 = iota(T.ci[:, 0:32], [[4, 32]], 0, 0)
+    g_one = iota(T.one[:], [[1, 256]], 1, 0)
+    g_c21 = iota(T.c21[:], [[2, 128]], 1, 0)
+    g_c43 = iota(T.c43[:], [[4, 128]], 3, 0)
+    g_i2 = iota(T.mk[:, 0:64], [[0, 32], [1, 2]], 0, 0)
+    g_i8 = iota(T.mk[:, 64:128], [[0, 8], [1, 8]], 0, 0)
+    a_pre = [None] * ROUNDS
+
+    def prefill(r):
+        act(T["low%d" % r][:, 0:128], T.one[:, 0:128], None, g_one)
+        a_pre[r] = act(T["lc%d" % r][:, 0:128], T.one[:, 0:128], None)
+
+    v_bit = fin("v", g.vector.memset(T.bit0[:, 256:272], 1.0))
+    ts(T.pi[:, 1:2], T.pi[:, 0:1], 15, None, A.bitwise_and, None, g_pi)
+    ts(T.pi[:, 2:3], T.pi[:, 0:1], 2, 3, A.logical_shift_right, A.bitwise_and)
+    ts(T.pi[:, 4:5], T.pi[:, 0:1], 1, 7, A.logical_shift_right, A.bitwise_and)
+    t = ts(T.pi[:, 3:4], T.pi[:, 0:1], 3, None, A.bitwise_and, None)
+    v_uo = vcopy(T.uo[:], T.ci[:, 32:40], g_ci)
+    vcopy(cs[:, 15:16], T.pi[:, 4:5], t)
+    t = vcopy(cs[:, 0:3], T.pi[:, 1:4])
+    q_, r_ = cs[:, 0:1], cs[:, 1:2]
+
+    def fun(f, out, in_, scale, bias, *toks):
+        wait("a", *toks)
+        return fin("a", g.scalar.activation(out, in_, f, bias=bias, scale=scale))
+    ID, SG = ActivationFunctionType.Identity, ActivationFunctionType.Sign
+    fun(SG, cs[:, 8:9], q_, 1.0, -14.5, t)
+    a_cs = fun(SG, cs[:, 20:21], r_, 1.0, -2.5)
+    h = LIFT / 2
+    fun(ID, cs[:, 4:5], cs[:, 8:9], 0.5 - 0.5 / LIFT, 0.5 + 0.5 / LIFT, a_cs)
+    fun(ID, cs[:, 5:6], cs[:, 20:21], 2.0 - 2.0 / LIFT, 2.0 + 2.0 / LIFT)
+    fun(ID, cs[:, 6:7], cs[:, 8:9], 0.5 - h, 0.5 + h)
+    a_cs = fun(ID, cs[:, 7:8], cs[:, 20:21], 0.5 - h, 0.5 + h)
+    prefill(0)
+    ms, mw = T.ms, T.mw
+    ts(ms[:, 16:32], T.i16[:], q_, 1.0, A.subtract, A.is_equal, g_is, t)
+    ta = ts(ms[:, 36:40], T.i16[:, 0:4], r_, 1.0, A.subtract, A.is_equal)
+    ts(ms[:, 0:16], T.i16[:], q_, 0.0, A.subtract, A.is_gt)
+    ts(ms[:, 32:36], T.i16[:, 0:4], r_, 0.0, A.subtract, A.is_gt)
+    ts(ms[:, 40:56], ms[:, 16:32], LIFT, None, A.mult, None, ta)
+    tb = ts(ms[:, 56:60], ms[:, 36:40], LIFT, None, A.mult, None)
+    ts(T.oq[:], T.i16[:], 0.0, q_, A.mult, A.add)
+    ts(T.ot[:], T.i16[:], 0.0, cs[:, 2:3], A.mult, A.add)
+    tt(mw[:, 0:16], ms[:, 0:16], ms[:, 40:56], A.max, tb)
+    t = tt(mw[:, 16:20], ms[:, 32:36], ms[:, 56:60], A.max)
+    m16, m4 = T.mt[:, 0:256], T.mt[:, 256:512]
+    act(m16, mw[:, 0:16].indirect(T.oq[:]), None, t)
+    a_m = act(m4, mw[:, 16:20].indirect(T.ot[:]), None)
+
+    v_t4 = ts(cs[:, 3:4], cs[:, 2:3], 4.0, None, A.subtract, None)
+    v_cs = a_cs
+    un16, un4, tau4 = cs[:, 4:5], cs[:, 5:6], cs[:, 3:4]
+
+    cc = T.cc
+    v_cc = ts(cc[:, 32:40], T.ci[:, 32:40], q_, None, A.add, None)
+    t = ts(T.c127[:, 8:16], cc[:, 32:40], 4.0, 3.0, A.mult, A.add, v_cc)
+    v_c127 = ts(T.c127[:, 0:8], cc[:, 32:40], 127.0, 256.0, A.is_equal, A.mult)
+    v_hic = ts(T.c127[:, 16:24], T.c127[:, 8:16], cs[:, 6:7], None, A.mult, None, t, a_cs)
+
+    def tables(k):
+        h = LIFT / 2
+        if k == 1:
+            tab[1] = fun(ID, cs[:, 12:13], tau4, 2.0, 12.0, v_t4)
+            fin("v", g.vector.memset(d0[:], -1.0))
+            tab["bit"] = [None] + [fin("v", g.vector.memset(T["bit%d" % i][:, 256:272], 1.0)) for i in (1, 2)]
+        if k == 2:
+            fun(ID, cs[:, 13:14], cs[:, 18:19], 0.5 - h, 0.5 + h, tab[1])
+            fun(ID, cs[:, 14:15], cs[:, 19:20], 0.5 - h, 0.5 + h)
+            tab["sg"] = fun(SG, cc[:, 40:80], cc[:, 0:40], 1.0, -0.5, v_c127)
+            ts(d0[:, 0:160:4], d0[:, 0:160:4], 0.0, None, A.mult, None)
+            fun(ID, cs[:, 11:12], cs[:, 18:19], -h, h)
+            fun(SG, mk[:, 256:320], mk[:, 64:128], 1.0, cs[:, 16:17], g_i8)
+            tab[2] = fun(ActivationFunctionType.Abs, mk[:, 320:384], mk[:, 64:128], 1.0, cs[:, 17:18])
+        if k == 3:
+            fun(ID, d1[:, 3:128:4], cc[:, 0:32], 16.0, cs[:, 12:13], tab[2])
+            fun(ID, d1[:, 131:160:4], cc[:, 32:40], 4.0, 1.0)
+            fun(ActivationFunctionType.Relu, mk[:, 384:448], mk[:, 320:384], -LIFT, LIFT)
+            tab[3] = fun(ID, mk[:, 128:192], mk[:, 0:64], cs[:, 11:12], 0.0, g_i2)
+            tab["cy"] = tt(cc[:, 80:120], cc[:, 0:40], cc[:, 40:80], A.add, tab["sg"])
+        if k == 5:
+            fun(ID, cmp_[:, 0:32], cc[:, 80:112], cs[:, 7:8], 0.0, tab["cy"])
+            fun(ID, cmp_[:, 32:40], cc[:, 112:120], cs[:, 6:7], 0.0)
+            fun(ID, cmp_[:, 40:72], cc[:, 80:112], cs[:, 13:14], 0.0)
+            tab[5] = fun(ID, cmp_[:, 72:80], cc[:, 112:120], cs[:, 14:15], 0.0)
+            tab["m8"] = tt(mk[:, 192:256], mk[:, 256:320], mk[:, 384:448], A.max, tab[3])
+    tab = {}
+
+    cmp_, mk, hic = T.cmp, T.mk, T.c127[:, 16:24]
+    m2, m8 = mk[:, 128:192], mk[:, 192:256]
+
+    v_k16 = vcopy(T.k16_0[:], T.kli[:], t_kl)
+    v_kf = vcopy(T.kf0[:, 0:16], T.kli[:])
+
+    v_uq = quant(T.uq[:, 0:128], T.us[:, 0:128], T.ut[:, 0:512], t_u)
+    tk = tt(T.kf0[:, 16:24], T.kf0[:, 0:8], T.c127[:, 0:8], A.max, v_kf, v_c127)
+    v_up = vcopy(T.up[:, 0:128].bitcast(dt.uint32), T.uq[:, 0:128].bitcast(dt.uint32).indirect(T.uo[:, 0:8]), v_uq, v_uo)
+    v_kb = vcopy(T.kb0[:], T.kf0[:, 16:24], tk)
+    v_q1 = quant(T.xq0[:, 0:128], T.xs0[:, 0:128], T.x0[:, 0:512], t_x)
+    a_up = act(T.ups[:, 0:128], T.us[:, 0:128].indirect(T.uo[:, 0:8]), None, v_uq, v_uo)
+    a_kfr = act(T.fr0[:, 0:256], T.one[:].indirect(T.k16_0[:, 0:16]), None, v_k16, g_one)
+    fun(SG, cs[:, 18:19], r_, 1.0, -1.5)
+    fun(SG, cs[:, 19:20], q_, 1.0, -13.5)
+    fun(ID, cc[:, 0:32], T.ci[:, 0:32], 1.0, r_, g_ci4)
+    fun(ID, cs[:, 16:17], cs[:, 15:16], -1.0, 0.0)
+    fun(ID, cs[:, 17:18], cs[:, 15:16], -1.0, -1.0)
+    v_q2 = quant(T.xq0[:, 128:256], T.xs0[:, 128:256], T.x0[:, 512:1024])
+    t = scan(T.sc0[:, 13 * 256:14 * 256], m4, T.fr0[:, 0:256], a_kfr, a_m)
+    v_k4 = ts(T.k4_0[:], T.sc0[:, 13 * 256 + 3:14 * 256:4], un4, tau4, A.mult, A.add, t, v_cs)
+
+    wait("g", v_k16)
+    rk = [remote(0, T.kin0[:], T.k16_0[:], "rk0"), 0, 0]
+    g_e = []
+    wait("g", iota(T.ones[:], [[0, 512]], 1, 0))
+    for b in range(4):
+        g_e.append(fin("g", g.affine_select(T.et[:, 512 * b:512 * b + 512], T.ones[:], [[-1, 512]], A.is_equal, 0.0, b, 4)))
+
+    bankuse = [[] for _ in range(8)]
+    x_done = (t_x,)
+    for r in range(ROUNDS):
+        X, xk, Z, H, B = T["x%d" % r], T["xk%d" % r], T["z%d" % r], T["h%d" % r], T["b%d" % r]
+        xq, xs, bit, W, low, SC = T["xq%d" % r], T["xs%d" % r], T["bit%d" % r], T["w%d" % r], T["low%d" % r], T["sc%d" % r]
+        fr, sm, to, tw = T["fr%d" % r], T["sm%d" % r], T["to%d" % r], T["tt%d" % r]
+        last = r == ROUNDS - 1
+
+        def sc(i):
+            return SC[:, 256 * i:256 * i + 256]
+
+        a_xk = act(xk[:], X[:].indirect(T["k4_%d" % r][:, 0:64]), 0.5, v_k4, *x_done)
+        xk2 = T["xj%d" % r]
+        wait("y", a_xk)
+        d_xk = dma("y", "dxk", 16 * (r + 1), xk2[:], xk[:])
+
+        sb = (4, 5)
+        p1 = mm(sb[0], 128, T.up[:, 0:128], T.ups[:, 0:128], xq[:, 0:128], xs[:, 0:128], v_q1, v_up, a_up, *bankuse[sb[0]])
+        p2 = mm(sb[1], 128, T.up[:, 0:128], T.ups[:, 0:128], xq[:, 128:256], xs[:, 128:256], v_q2, *bankuse[sb[1]])
+        ts(bit[:, 0:128], psv(sb[0], 0, 128), 0.0, None, A.is_gt, None, p1)
+        t = ts(bit[:, 128:256], psv(sb[1], 0, 128), 0.0, None, A.is_gt, None, p2)
+        bankuse[sb[0]], bankuse[sb[1]] = [t], [t]
+        tl = tt(W[:, 0:128], bit[:, 0:272].indirect(T["kb%d" % r][:, 0:8]), T.c21[:], A.add, t, v_kb, tab["bit"][r] if r else v_bit, g_c21)
+        t = scan(SC[:, 0:128], m16[:, 0:128], W[:, 0:128], tl)
+        th = tt(W[:, 128:256], T.c43[:], W[:, 0:128], A.subtract, g_c43)
+        t = tt(sm[:, 40:48], hic, SC[:, 15:128:16], A.subtract, t, v_hic)
+        v_tl = ts(to[:, 0:8], SC[:, 15:128:16], un16, 1.0, A.mult, A.subtract)
+        v_to = ts(to[:, 8:16], sm[:, 40:48], un16, 1.0, A.mult, A.subtract, t)
+
+        lc = T["lc%d" % r]
+        v_low = vcopy(low[:, 128:256], W[:, 128:256], th)
+        v_lc = vcopy(lc[:, 128:256], W[:, 128:256])
+        a_w = act(W[:, 256:384], W[:, 0:256].indirect(to[:, 0:8]), None, v_tl)
+        v_w = vcopy(W[:, 384:512], W[:, 0:256].indirect(to[:, 8:16]), v_to)
+        scan(SC[:, 256:384], m16[:, 0:128], W[:, 256:384], a_w)
+        t = scan(SC[:, 384:512], m16[:, 0:128], W[:, 384:512], v_w)
+        t4 = scan(SC[:, 9 * 256:9 * 256 + 128], m4[:, 0:128], W[:, 0:128])
+        v_to = ts(to[:, 16:32], SC[:, 256 + 15:512:16], un16, 1.0, A.mult, A.subtract, t)
+        v_lc = (v_lc, a_pre[r])
+        for k in range(1, 7):
+            o, i, off = W[:, 256 * k + 256:256 * k + 512], W[:, 256 * k:256 * k + 256], to[:, 16 * k:16 * k + 16]
+            nl, pl = low[:, 256 * k:256 * k + 256], low[:, 256 * k - 256:256 * k]
+            if k < 6:
+                e = 256 - SHARE
+                a_w = act(o[:, 0:e], i.indirect(to[:, 16 * k:16 * k + e // 16]), None, v_to, a_w)
+                v_w = vcopy(o[:, e:256], i.indirect(to[:, 16 * k + e // 16:16 * k + 16]), v_to) if SHARE else None
+            else:
+                a_w = act(o[:, 128:256], i.indirect(to[:, 16 * k + 8:16 * k + 16]), None, v_to, a_w)
+            v_low = tt(nl, pl.indirect(off), lc[:, 256 * k - 256:256 * k], A.min, v_to, v_low, *v_lc)
+            if k < 6:
+                v_lc = (act(lc[:, 256 * k:256 * k + 256], nl, None, v_low),)
+                t = scan(sc(k + 1), m16, o, a_w, v_w)
+            else:
+                v_lc = (act(lc[:, 256 * k + 128:256 * k + 256], nl[:, 128:256], None, v_low),)
+                t = scan(SC[:, 256 * k + 384:256 * k + 512], m16[:, 0:128], o[:, 128:256], a_w)
+            if r == 0:
+                tables(k)
+            if k == 1:
+                ts(d1[:, 2:128:4], SC[:, 9 * 256 + 3:9 * 256 + 128:4], un4, tau4, A.mult, A.add, t4)
+            if k == 2:
+                td = ts(d1[:, 130:160:4], SC[:, 15:128:16], un16, 1.0, A.mult, A.subtract)
+            if k == 3:
+                td = ts(sm[:, 0:40], d1[:, 2:160:4], -2.0, None, A.mult, None, td)
+            if k == 4:
+                v_d = tt(d0[:, 2:160:4], sm[:, 0:40], d1[:, 3:160:4], A.add, td, tab[3])
+            h = 0 if k < 6 else 8
+            v_to = ts(to[:, 16 * k + 16 + h:16 * k + 32], SC[:, 256 * (k + 1) + 15 + 16 * h:256 * (k + 2):16], un16, 1.0, A.mult, A.subtract, t)
+        l8 = low[:, 7 * 256 + 128:8 * 256]
+        v_low = tt(l8, low[:, 6 * 256:7 * 256].indirect(to[:, 120:128]), lc[:, 6 * 256 + 128:7 * 256], A.min, v_to, v_low, *v_lc)
+        so = T["so%d" % r]
+        scan(SC[:, 2560:2624], m2, l8[:, 0:64], v_low, tab[5])
+        t4 = scan(SC[:, 2624:2752], m4[:, 0:128], l8)
+        scan(SC[:, 2816:2880], m8, l8[:, 0:64])
+        t16 = scan(SC[:, 2880:3008], m16[:, 0:128], l8)
+        tt(d1[:, 1:128:4], SC[:, 2561:2624:2], cmp_[:, 40:72], A.is_equal, t4)
+        e4 = tt(d1[:, 0:128:4], SC[:, 2627:2752:4], cmp_[:, 0:32], A.is_equal)
+        tt(d1[:, 129:160:4], SC[:, 2823:2880:8], cmp_[:, 72:80], A.is_equal, t16)
+        e16 = tt(d1[:, 128:160:4], SC[:, 2895:3008:16], cmp_[:, 32:40], A.is_equal)
+        s4 = chain(so[:, 0:128], d0[:, 0:128], d1[:, 0:128], e4, v_d)
+        s16 = chain(so[:, 128:160], d0[:, 128:160], d1[:, 128:160], e16)
+        clo = vcopy(tw[:, 0:32], so[:, 2:128:4], s4)
+        chi = vcopy(tw[:, 40:72], so[:, 3:128:4])
+        c16 = vcopy(tw[:, 32:40], so[:, 130:160:4], s16)
+
+        ne = rk[r]
+        f1 = act(fr[:, 256:512], T.one[:].indirect(T["kin%d" % r][:, 0:16]), None, ("rk%d" % r, ne), g_one)
+        f2 = act(fr[:, 512:768], fr[:, 256:512].indirect(T["k16_%d" % r][:, 0:16]), None, f1, v_k16)
+        act(fr[:, 768:896], fr[:, 512:768].indirect(tw[:, 32:40]), None, f2, c16)
+
+        def layer(qz, qzs, banks, tok):
+            out = []
+            for b in range(4):
+                out.append(mm(banks[b], 128, T.wq[:, 128 * b:128 * b + 128], T.wqs[:, 128 * b:128 * b + 128], qz, qzs,
+                              tok, t_wc, t_ws, *bankuse[banks[b]]))
+            return out
+
+        def nm(s):
+            return T["%s_%d" % (s, r)]
+        z1 = tt(Z[:, 0:512], xk[:].indirect(tw[:, 0:32]), xk2[:, 0:512], A.add, clo, a_xk, d_xk)
+        chi16 = vcopy(tw[:, 72:80], so[:, 131:160:4])
+        a_n = act(fr[:, 896:1024], fr[:, 512:768].indirect(tw[:, 72:80]), None, chi16)
+        tq = quant(nm("qz")[:, 0:128], nm("qzs")[:, 0:128], Z[:, 0:512], z1)
+        p = layer(nm("qz")[:, 0:128], nm("qzs")[:, 0:128], (0, 1, 2, 3), tq)
+        h1 = []
+        for b in range(4):
+            h1.append(act(H[:, b:512:4], psv(b, 0, 128), 0.03125, p[b]))
+            bankuse[b] = [h1[b]]
+        z2 = tt(Z[:, 512:768], xk[:].indirect(tw[:, 40:56]), xk2[:, 512:768], A.add, chi)
+        tq = quant(nm("qz")[:, 128:256], nm("qzs")[:, 128:256], Z[:, 256:768], z2)
+        p = layer(nm("qz")[:, 128:256], nm("qzs")[:, 128:256], (4, 5, 6, 7), tq)
+        if not SINGLE:
+            tq1 = quant(nm("qh")[:, 0:128], nm("qhs")[:, 0:128], H[:, 0:512], h1[3])
+        h2 = [None] * 4
+        for b in (0, 2):
+            h2[b] = ts(H[:, 512 + b:768:4], psv(4 + b, 64, 128), 0.03125, None, A.mult, None, p[b])
+            bankuse[4 + b] = [h2[b]]
+        for b in (1, 3):
+            h2[b] = act(H[:, 512 + b:768:4], psv(4 + b, 64, 128), 0.03125, p[b])
+            bankuse[4 + b] = [h2[b]]
+        if SINGLE:
+            tq2 = quant(nm("qh")[:, 0:192], nm("qhs")[:, 0:192], H[:, 0:768], h1[3], h2[2], h2[3])
+            wait("g", tq2)
+            na = remote(r, nm("cin")[:, 0:192].bitcast(dt.uint8), nm("qh")[:, 0:192].bitcast(dt.uint8), "ra%d" % r)
+            na += remote(r, nm("cins")[:, 0:192], nm("qhs")[:, 0:192], "ra%d" % r)
+        else:
+            tq2 = quant(nm("qh")[:, 128:256], nm("qhs")[:, 128:256], H[:, 256:768], h2[2], h2[3])
+
+            wait("g", tq1)
+            na = remote(r, nm("cin")[:, 0:128].bitcast(dt.uint8), nm("qh")[:, 0:128].bitcast(dt.uint8), "ra%d" % r)
+            na += remote(r, nm("cins")[:, 0:128], nm("qhs")[:, 0:128], "ra%d" % r)
+            wait("g", tq2)
+            nb = remote(r, nm("cin")[:, 128:192].bitcast(dt.uint8), nm("qh")[:, 192:256].bitcast(dt.uint8), "rb%d" % r)
+            nb += remote(r, nm("cins")[:, 128:192], nm("qhs")[:, 192:256], "rb%d" % r)
+
+        z3 = tt(Z[:, 768:1024], xk[:].indirect(tw[:, 56:72]), xk2[:, 768:1024], A.add)
+        s16 = None
+        if not last:
+            s16 = scan(sc(12), m16, fr[:, 768:1024], a_n)
+        s4 = scan(sc(13) if r else sc(9), m4, fr[:, 768:1024], a_n)
+        tq = quant(nm("qz")[:, 256:384], nm("qzs")[:, 256:384], Z[:, 512:1024], z3)
+        p = layer(nm("qz")[:, 256:384], nm("qzs")[:, 256:384], (0, 1, 2, 3), tq)
+        for b in range(4):
+            t = act(B[:, 768 + b:1024:4], psv(b, 64, 128), 0.03125, p[b])
+            bankuse[b] = [t]
+        a_b = t
+        if not last:
+            prefill(r + 1)
+        s4o = 256 * (13 if r else 9)
+        if not last:
+            kf = T["kf%d" % (r + 1)]
+            v_k16 = ts(T["k16_%d" % (r + 1)][:], SC[:, 12 * 256 + 15:13 * 256:16], un16, 1.0, A.mult, A.subtract, s16)
+            v_kf = ts(kf[:, 0:16], SC[:, 12 * 256 + 15:13 * 256:16], un16, 1.0, A.mult, A.subtract)
+            v_k4 = ts(T["k4_%d" % (r + 1)][:], SC[:, s4o + 3:s4o + 256:4], un4, tau4, A.mult, A.add, s4)
+            t = tt(kf[:, 16:24], kf[:, 0:8], T.c127[:, 0:8], A.max, v_kf)
+            v_kb = vcopy(T["kb%d" % (r + 1)][:], kf[:, 16:24], t)
+            wait("g", v_k16)
+            rk[r + 1] = remote(r + 1, T["kin%d" % (r + 1)][:], T["k16_%d" % (r + 1)][:], "rk%d" % (r + 1))
+        else:
+            v_k4 = ts(T["k4_%d" % (r + 1)][:], SC[:, s4o + 3:s4o + 256:4], un4, tau4, A.mult, A.add, s4)
+            v_ky = ts(T.kyf[:], fr[:, 768:1024], 1.0, None, A.subtract, None)
+        if r == 0:
+            for b in range(4):
+                v_e = quant(T.eq[:, 128 * b:128 * b + 128], T.es[:, 128 * b:128 * b + 128], T.et[:, 512 * b:512 * b + 512], g_e[b])
+            v_v = quant(T.vq[:, 0:128], T.vqs[:, 0:128], T.vt[:], t_v)
+
+        cin, cins = nm("cin"), nm("cins")
+        p, bt = [], []
+        if SINGLE:
+            for b in range(4):
+                p.append(mm(4 + b, 192, T.eq[:, 128 * b:128 * b + 128], T.es[:, 128 * b:128 * b + 128], cin[:, 0:192], cins[:, 0:192],
+                            ("ra%d" % r, na), v_e, *bankuse[4 + b]))
+            for b in range(4):
+                o, i = B[:, b:768:4], psv(4 + b, 0, 192)
+                t = vcopy(o, i, p[b]) if b % 2 == 0 else act(o, i, None, p[b])
+                bankuse[4 + b] = [t]
+                bt.append(t)
+        else:
+            for b in range(4):
+                p.append(mm(4 + b, 128, T.eq[:, 128 * b:128 * b + 128], T.es[:, 128 * b:128 * b + 128], cin[:, 0:128], cins[:, 0:128],
+                            ("ra%d" % r, na), v_e, *bankuse[4 + b]))
+            for b in range(4):
+                t = act(B[:, b:512:4], psv(4 + b, 0, 128), None, p[b])
+                bankuse[4 + b] = [t]
+            p = []
+            for b in range(4):
+                p.append(mm(b, 128, T.eq[:, 128 * b:128 * b + 128], T.es[:, 128 * b:128 * b + 128], cin[:, 64:192], cins[:, 64:192],
+                            ("rb%d" % r, nb), *bankuse[b]))
+            for b in range(4):
+                o, i = B[:, 512 + b:768:4], psv(b, 64, 128)
+                t = vcopy(o, i, p[b]) if b % 2 == 0 else act(o, i, None, p[b])
+                bankuse[b] = [t]
+                bt.append(t)
+
+        nx, n4 = T["x%d" % (r + 1)], T["k4_%d" % (r + 1)]
+        nq, ns = T["xq%d" % (r + 1)], T["xs%d" % (r + 1)]
+        g1 = tt(nx[:, 0:512], B[:].indirect(n4[:, 0:32]), X[:, 0:512], A.add, v_k4, a_b, *bt)
+        g2 = tt(nx[:, 512:1024], B[:].indirect(n4[:, 32:64]), X[:, 512:1024], A.add)
+        v_q1 = quant(nq[:, 0:128], ns[:, 0:128], nx[:, 0:512], g1)
+        v_q2 = quant(nq[:, 128:256], ns[:, 128:256], nx[:, 512:1024], g2)
+        x_done = (g1, g2)
+
+    nd = [0]
+
+    def out(q, o, i, *toks):
+        wait(q, *toks)
+        queues[q].dma_start(o, i).then_inc(T.sem.dout, 16)
+        nd[0] += 16
+    xq, xs = T["xq%d" % ROUNDS], T["xs%d" % ROUNDS]
+    p1 = mm(4, 128, T.vq[:, 0:128], T.vqs[:, 0:128], xq[:, 0:128], xs[:, 0:128], v_q1, v_v, *bankuse[4])
+    p2 = mm(5, 128, T.vq[:, 0:128], T.vqs[:, 0:128], xq[:, 128:256], xs[:, 128:256], v_q2, *bankuse[5])
+    y1 = vcopy(T.yo[:, 0:128], psv(4, 0, 128), p1)
+    y2 = vcopy(T.yo[:, 128:256], psv(5, 0, 128), p2)
+    out("y", T.kp[:], T.kyf[0:128:16, :], v_ky)
+    out("y", T.oc[:], xq[:, 0:256].bitcast(dt.uint8), v_q2)
+    out("a", T.osc[0:4, :], xs[0:4, :], v_q2)
+    out("y", T.osc[4:8, :], xs[32:36, :])
+    out("a", T.osc[8:12, :], xs[64:68, :])
+    out("y", T.osc[12:16, :], xs[96:100, :])
+    out("y", T.y[:, 0:128], T.yo[:, 0:128], y1)
+    out("a", T.y[:, 128:256], T.yo[:, 128:256], y2)
+
+    wait("g", ("dout", nd[0]), ("loc", loc[0]), *[(s, n) for s, n in done.items()])

@@ -3,10 +3,24 @@ from concourse.mybir import dt, AluOpType, ActivationFunctionType
 
 ROUNDS = 3
 LIFT = 512.0
-SINGLE = False
-SHARE = 32
+TINY = 2.0 ** -100
 A = AluOpType
-CP = ActivationFunctionType.Copy
+CP, ID, SG = ActivationFunctionType.Copy, ActivationFunctionType.Identity, ActivationFunctionType.Sign
+
+
+def lay(*parts):
+    at, out = 0, {}
+    for n, w in parts:
+        out[n] = (at, at + w)
+        at += (w + 15) // 16 * 16
+    return out, at
+
+
+FREE, NFREE = lay(("sg", 256), ("tmp", 128), ("tg", 240), ("ts", 240), ("tm", 16), ("t1", 64), ("r0", 128), ("c0", 64), ("s0", 128),
+                  *[("r%d" % i, 64) for i in range(1, 7)], *[("m%d" % i, 64) for i in range(1, 10)], ("c1", 64), ("c2", 64),
+                  ("s1", 64), ("s2", 64), ("f", 128), ("sf", 128), ("f1", 32), ("hi", 32), ("so", 256),
+                  ("nn", 512), ("kp", 256), ("kk", 512), ("n4", 256), ("n16", 256), ("kt", 240), ("st", 240))
+WRAP, NWRAP = lay(("bl", 12), ("l0", 8), ("l1", 4), ("l2", 4), ("lo", 32), ("hi", 32), ("tn", 32), ("k4", 64), ("tl", 15))
 
 SCRATCH = {
     "ps": ("psum", [128, 4096], "float32"),
@@ -20,38 +34,35 @@ SCRATCH = {
     "ones": ("sbuf", [128, 512], "bfloat16"),
     "et": ("sbuf", [128, 2048], "bfloat16"),
     "eq": ("sbuf", [128, 512], "float8_e4m3fn_x4"), "es": ("sbuf", [128, 512], "uint8"),
-    "pi": ("sbuf", [128, 8], "int32"),
-    "cs": ("sbuf", [128, 24], "float32"),
-    "i16": ("sbuf", [128, 16], "float32"), "ms": ("sbuf", [128, 64], "bfloat16"), "mw": ("sbuf", [128, 32], "bfloat16"),
+    "pi": ("sbuf", [128, 32], "int32"),
+    "cs": ("sbuf", [128, 32], "float32"),
+    "im": ("sbuf", [128, 24], "float32"), "ms": ("sbuf", [128, 64], "bfloat16"), "mw": ("sbuf", [128, 48], "bfloat16"),
     "oq": ("sbuf", [128, 16], "uint16"), "ot": ("sbuf", [128, 16], "uint16"),
     "mt": ("sbuf", [128, 512], "bfloat16"),
-    "d0": ("sbuf", [128, 160], "float32"), "d1": ("sbuf", [128, 160], "float32"),
-    "one": ("sbuf", [128, 256], "bfloat16"),
-    "c21": ("sbuf", [128, 128], "bfloat16"), "c43": ("sbuf", [128, 128], "float32"),
-    "ci": ("sbuf", [128, 40], "float32"), "cc": ("sbuf", [128, 120], "float32"),
-    "cmp": ("sbuf", [128, 80], "float32"), "c127": ("sbuf", [128, 24], "float32"), "mk": ("sbuf", [128, 448], "bfloat16"),
+    "one": ("sbuf", [128, 256], "bfloat16"), "cd": ("sbuf", [128, 128], "bfloat16"),
+    "ci": ("sbuf", [128, 48], "float32"), "cc": ("sbuf", [128, 64], "float32"),
+    "mark": ("sbuf", [128, 48], "bfloat16"), "yw": ("sbuf", [128, 32], "float32"), "yl": ("sbuf", [128, 24], "uint16"),
+    "fi": ("sbuf", [128, 16], "uint16"), "yc": ("sbuf", [128, 288], "bfloat16"), "wa": ("sbuf", [128, 352], "bfloat16"),
+    "wt": ("sbuf", [128, 240], "bfloat16"), "tk": ("sbuf", [128, 240], "bfloat16"), "tr": ("sbuf", [128, 240], "bfloat16"),
+    "kf": ("sbuf", [128, 128], "bfloat16"), "ke": ("sbuf", [128, 64], "bfloat16"),
+    "d0": ("sbuf", [128, 256], "bfloat16"), "d1": ("sbuf", [128, 256], "bfloat16"),
     "uo": ("sbuf", [128, 8], "uint16"),
     "kyf": ("sbuf", [128, 256], "float32"),
     "yo": ("sbuf", [128, 256], "float32"),
-    "x0": ("sbuf", [128, 1024], "bfloat16"),
 }
 for _r in range(ROUNDS + 1):
-    if _r:
-        SCRATCH["x%d" % _r] = ("sbuf", [128, 1024], "bfloat16")
+    SCRATCH["x%d" % _r] = ("sbuf", [128, 1024], "bfloat16")
     SCRATCH["xq%d" % _r] = ("sbuf", [128, 256], "float8_e4m3fn_x4")
     SCRATCH["xs%d" % _r] = ("sbuf", [128, 256], "uint8")
+    SCRATCH["fr%d" % _r] = ("sbuf", [128, NFREE], "bfloat16")
+    SCRATCH["wr%d" % _r] = ("sbuf", [128, NWRAP], "uint16")
 for _r in range(ROUNDS):
-    for _n, _w, _d in (("xk", 1024, "bfloat16"), ("xj", 1024, "bfloat16"), ("lc", 8 * 256, "bfloat16"), ("z", 1024, "bfloat16"), ("h", 768, "bfloat16"), ("b", 1024, "bfloat16"),
-                       ("bit", 272, "bfloat16"), ("w", 8 * 256, "bfloat16"), ("low", 8 * 256, "bfloat16"),
-                       ("sc", 14 * 256, "bfloat16"), ("fr", 4 * 256, "bfloat16"), ("sm", 48, "float32"), ("so", 160, "float32"),
-                       ("to", 8 * 16, "uint16"), ("tt", 80, "uint16"),
-                       ("kf", 24, "float32"), ("k16_", 16, "uint16"), ("kb", 8, "uint16"), ("k4_", 64, "uint16"),
-                       ("kin", 16, "uint16")):
+    for _n, _w, _d in (("xk", 1024, "bfloat16"), ("xj", 1024, "bfloat16"), ("z", 1024, "bfloat16"), ("h", 768, "bfloat16"), ("b", 1024, "bfloat16"),
+                       ("k16_", 16, "uint16"), ("kin", 16, "uint16")):
         SCRATCH["%s%d" % (_n, _r)] = ("sbuf", [128, _w], _d)
     for _n, _w in (("qz", 384), ("qh", 256), ("cin", 192)):
         SCRATCH["%s_%d" % (_n, _r)] = ("sbuf", [128, _w], "float8_e4m3fn_x4")
         SCRATCH["%ss_%d" % (_n, _r)] = ("sbuf", [128, _w], "uint8")
-SCRATCH["k4_3"] = ("sbuf", [128, 64], "uint16")
 
 SEMAPHORES = ["sv", "sa", "st", "sg", "dx", "du", "dk", "dwc", "dws", "dv", "dxk", "dout", "loc"]
 SEMAPHORES += ["%s%d" % (n, r) for r in range(ROUNDS) for n in ("rk", "ra", "rb")]
@@ -100,6 +111,10 @@ def rank_program(g, core, T, topo):
         wait("v", *toks)
         return fin("v", g.vector.tensor_copy(out, in_))
 
+    def fill(out, c, *toks):
+        wait("v", *toks)
+        return fin("v", g.vector.memset(out, c))
+
     def scan(out, mask, data, *toks):
         wait("v", *toks)
         return fin("v", g.vector.tensor_tensor_scan(out, mask, data, 0.0, A.mult, A.max))
@@ -118,6 +133,10 @@ def rank_program(g, core, T, topo):
             return fin("a", g.scalar.activation(out, in_, CP))
         return fin("a", g.scalar.activation(out, in_, CP, scale=scale))
 
+    def fun(f, out, in_, scale, bias, *toks):
+        wait("a", *toks)
+        return fin("a", g.scalar.activation(out, in_, f, bias=bias, scale=scale))
+
     def mm(bank, n, lq, ls, rq, rs, *toks):
         wait("t", *toks)
         return fin("t", g.tensor.matmul_mx(T.ps[:, 512 * bank:512 * bank + n], lq, ls, rq, rs, True, True))
@@ -133,8 +152,24 @@ def rank_program(g, core, T, topo):
         loc[0] += ne
         return ne
 
+    def iota(out, pat, base, ch, small=True):
+        if small:
+            return fin("g", g.iota(out, pat, base, ch, allow_small_or_imprecise_dtypes=True))
+        return fin("g", g.iota(out, pat, base, ch))
+
+    def fr(r, name, a=0, b=None, step=1):
+        lo, hi = FREE[name]
+        return T["fr%d" % r][:, lo + a:(hi if b is None else lo + b):step]
+
+    def wr(r, name, a=0, b=None):
+        lo, hi = WRAP[name]
+        return T["wr%d" % r][:, lo + a:(hi if b is None else lo + b)]
+
     loc = [0]
-    cs, d0, d1 = T.cs, T.d0, T.d1
+    cs, d0, d1, pi, im, mark, yw, wa, wt, yc = T.cs, T.d0, T.d1, T.pi, T.im, T.mark, T.yw, T.wa, T.wt, T.yc
+
+    def col(i):
+        return cs[:, i:i + 1]
 
     t_kl = dma("y", "dk", 16, T.kli[:], T.kl[:])
     t_x = dma("y", "dx", 16, T.x0[:], T.x[:])
@@ -143,217 +178,226 @@ def rank_program(g, core, T, topo):
     t_ws = dma("y", "dws", 16, T.wqs[:], T.ws[:])
     t_v = dma("y", "dv", 16, T.vt[:], T.v[:])
 
-    def iota(out, pat, base, ch, small=True):
-        if small:
-            return fin("g", g.iota(out, pat, base, ch, allow_small_or_imprecise_dtypes=True))
-        return fin("g", g.iota(out, pat, base, ch))
-    g_pi = iota(T.pi[:, 0:1], [[0, 1]], 0, 1, False)
-    g_is = iota(T.i16[:], [[1, 16]], 0, 0)
+    g_pi = iota(pi[:, 0:1], [[0, 1]], 0, 1, False)
+    g_pj = iota(pi[:, 1:2], [[0, 1]], 127, -1, False)
+    g_im = iota(im[:, 0:17], [[1, 17]], -1, 0)
+    g_tm = iota(T.ci[:, 40:48], [[-1, 8]], 6, 0)
     g_ci = iota(T.ci[:, 32:40], [[16, 8]], 0, 0)
-    g_ci4 = iota(T.ci[:, 0:32], [[4, 32]], 0, 0)
     g_one = iota(T.one[:], [[1, 256]], 1, 0)
-    g_c21 = iota(T.c21[:], [[2, 128]], 1, 0)
-    g_c43 = iota(T.c43[:], [[4, 128]], 3, 0)
-    g_i2 = iota(T.mk[:, 0:64], [[0, 32], [1, 2]], 0, 0)
-    g_i8 = iota(T.mk[:, 64:128], [[0, 8], [1, 8]], 0, 0)
-    a_pre = [None] * ROUNDS
+    g_nn = iota(fr(0, "nn"), [[0, 512]], 1, 0)
+    iota(T.tr[:, 0:192], [[0, 12], [1, 16]], 0, 0)
+    g_tr = iota(T.tr[:, 192:240], [[0, 12], [1, 4]], 0, 0)
+    g_cd = iota(T.cd[:], [[4, 64], [1, 2]], 1, 0)
+    i0 = im[:, 1:17]
 
-    def prefill(r):
-        act(T["low%d" % r][:, 0:128], T.one[:, 0:128], None, g_one)
-        a_pre[r] = act(T["lc%d" % r][:, 0:128], T.one[:, 0:128], None)
-
-    v_bit = fin("v", g.vector.memset(T.bit0[:, 256:272], 1.0))
-    ts(T.pi[:, 1:2], T.pi[:, 0:1], 15, None, A.bitwise_and, None, g_pi)
-    ts(T.pi[:, 2:3], T.pi[:, 0:1], 2, 3, A.logical_shift_right, A.bitwise_and)
-    ts(T.pi[:, 4:5], T.pi[:, 0:1], 1, 7, A.logical_shift_right, A.bitwise_and)
-    t = ts(T.pi[:, 3:4], T.pi[:, 0:1], 3, None, A.bitwise_and, None)
+    fill(yw[:, 24:26], 7.0)
+    fill(yw[:, 26:27], 3.0)
+    fill(mark[:, 0:2], 0.0)
+    ts(pi[:, 2:3], pi[:, 0:1], 15, None, A.bitwise_and, None, g_pi)
+    ts(pi[:, 3:4], pi[:, 0:1], 2, 3, A.logical_shift_right, A.bitwise_and)
+    ts(pi[:, 4:5], pi[:, 0:1], 3, None, A.bitwise_and, None)
+    ts(pi[:, 5:6], pi[:, 0:1], 1, None, A.bitwise_and, None)
+    for d in range(4):
+        t = ts(pi[:, 6 + d:7 + d], pi[:, 1:2], 15, 3 - d, A.bitwise_and, A.logical_shift_right, g_pj)
+    v_c = vcopy(cs[:, 0:8], pi[:, 2:10], t)
+    q_, r_, tau = col(0), col(1), col(2)
     v_uo = vcopy(T.uo[:], T.ci[:, 32:40], g_ci)
-    vcopy(cs[:, 15:16], T.pi[:, 4:5], t)
-    t = vcopy(cs[:, 0:3], T.pi[:, 1:4])
-    q_, r_ = cs[:, 0:1], cs[:, 1:2]
 
-    def fun(f, out, in_, scale, bias, *toks):
-        wait("a", *toks)
-        return fin("a", g.scalar.activation(out, in_, f, bias=bias, scale=scale))
-    ID, SG = ActivationFunctionType.Identity, ActivationFunctionType.Sign
-    fun(SG, cs[:, 8:9], q_, 1.0, -14.5, t)
-    a_cs = fun(SG, cs[:, 20:21], r_, 1.0, -2.5)
-    h = LIFT / 2
-    fun(ID, cs[:, 4:5], cs[:, 8:9], 0.5 - 0.5 / LIFT, 0.5 + 0.5 / LIFT, a_cs)
-    fun(ID, cs[:, 5:6], cs[:, 20:21], 2.0 - 2.0 / LIFT, 2.0 + 2.0 / LIFT)
-    fun(ID, cs[:, 6:7], cs[:, 8:9], 0.5 - h, 0.5 + h)
-    a_cs = fun(ID, cs[:, 7:8], cs[:, 20:21], 0.5 - h, 0.5 + h)
-    prefill(0)
+    fun(SG, col(8), q_, 1.0, -14.5, v_c)
+    t = fun(SG, col(9), r_, 1.0, -2.5)
+    a_tau = fun(ActivationFunctionType.Square, col(10), tau, 0.25, 0.125)
+    fun(ID, col(11), col(8), 0.5 - 0.5 / LIFT, 0.5 + 0.5 / LIFT, t)
+    fun(ID, col(12), col(9), 2.0 - 2.0 / LIFT, 2.0 + 2.0 / LIFT)
+    fun(ID, col(13), tau, 1.0, -4.0)
+    fun(ID, col(14), col(10), 1.0, 0.109375, a_tau)
+    a_my = fun(ID, col(15), col(10), 2.0, 0.21875)
+    un16, un4x4, tau4 = col(11), col(12), col(13)
+
     ms, mw = T.ms, T.mw
-    ts(ms[:, 16:32], T.i16[:], q_, 1.0, A.subtract, A.is_equal, g_is, t)
-    ta = ts(ms[:, 36:40], T.i16[:, 0:4], r_, 1.0, A.subtract, A.is_equal)
-    ts(ms[:, 0:16], T.i16[:], q_, 0.0, A.subtract, A.is_gt)
-    ts(ms[:, 32:36], T.i16[:, 0:4], r_, 0.0, A.subtract, A.is_gt)
-    ts(ms[:, 40:56], ms[:, 16:32], LIFT, None, A.mult, None, ta)
-    tb = ts(ms[:, 56:60], ms[:, 36:40], LIFT, None, A.mult, None)
-    ts(T.oq[:], T.i16[:], 0.0, q_, A.mult, A.add)
-    ts(T.ot[:], T.i16[:], 0.0, cs[:, 2:3], A.mult, A.add)
-    tt(mw[:, 0:16], ms[:, 0:16], ms[:, 40:56], A.max, tb)
-    t = tt(mw[:, 16:20], ms[:, 32:36], ms[:, 56:60], A.max)
-    m16, m4 = T.mt[:, 0:256], T.mt[:, 256:512]
-    act(m16, mw[:, 0:16].indirect(T.oq[:]), None, t)
-    a_m = act(m4, mw[:, 16:20].indirect(T.ot[:]), None)
-
-    v_t4 = ts(cs[:, 3:4], cs[:, 2:3], 4.0, None, A.subtract, None)
-    v_cs = a_cs
-    un16, un4, tau4 = cs[:, 4:5], cs[:, 5:6], cs[:, 3:4]
-
-    cc = T.cc
-    v_cc = ts(cc[:, 32:40], T.ci[:, 32:40], q_, None, A.add, None)
-    t = ts(T.c127[:, 8:16], cc[:, 32:40], 4.0, 3.0, A.mult, A.add, v_cc)
-    v_c127 = ts(T.c127[:, 0:8], cc[:, 32:40], 127.0, 256.0, A.is_equal, A.mult)
-    v_hic = ts(T.c127[:, 16:24], T.c127[:, 8:16], cs[:, 6:7], None, A.mult, None, t, a_cs)
-
-    def tables(k):
-        h = LIFT / 2
-        if k == 1:
-            tab[1] = fun(ID, cs[:, 12:13], tau4, 2.0, 12.0, v_t4)
-            fin("v", g.vector.memset(d0[:], -1.0))
-            tab["bit"] = [None] + [fin("v", g.vector.memset(T["bit%d" % i][:, 256:272], 1.0)) for i in (1, 2)]
-        if k == 2:
-            fun(ID, cs[:, 13:14], cs[:, 18:19], 0.5 - h, 0.5 + h, tab[1])
-            fun(ID, cs[:, 14:15], cs[:, 19:20], 0.5 - h, 0.5 + h)
-            tab["sg"] = fun(SG, cc[:, 40:80], cc[:, 0:40], 1.0, -0.5, v_c127)
-            ts(d0[:, 0:160:4], d0[:, 0:160:4], 0.0, None, A.mult, None)
-            fun(ID, cs[:, 11:12], cs[:, 18:19], -h, h)
-            fun(SG, mk[:, 256:320], mk[:, 64:128], 1.0, cs[:, 16:17], g_i8)
-            tab[2] = fun(ActivationFunctionType.Abs, mk[:, 320:384], mk[:, 64:128], 1.0, cs[:, 17:18])
-        if k == 3:
-            fun(ID, d1[:, 3:128:4], cc[:, 0:32], 16.0, cs[:, 12:13], tab[2])
-            fun(ID, d1[:, 131:160:4], cc[:, 32:40], 4.0, 1.0)
-            fun(ActivationFunctionType.Relu, mk[:, 384:448], mk[:, 320:384], -LIFT, LIFT)
-            tab[3] = fun(ID, mk[:, 128:192], mk[:, 0:64], cs[:, 11:12], 0.0, g_i2)
-            tab["cy"] = tt(cc[:, 80:120], cc[:, 0:40], cc[:, 40:80], A.add, tab["sg"])
-        if k == 5:
-            fun(ID, cmp_[:, 0:32], cc[:, 80:112], cs[:, 7:8], 0.0, tab["cy"])
-            fun(ID, cmp_[:, 32:40], cc[:, 112:120], cs[:, 6:7], 0.0)
-            fun(ID, cmp_[:, 40:72], cc[:, 80:112], cs[:, 13:14], 0.0)
-            tab[5] = fun(ID, cmp_[:, 72:80], cc[:, 112:120], cs[:, 14:15], 0.0)
-            tab["m8"] = tt(mk[:, 192:256], mk[:, 256:320], mk[:, 384:448], A.max, tab[3])
-    tab = {}
-
-    cmp_, mk, hic = T.cmp, T.mk, T.c127[:, 16:24]
-    m2, m8 = mk[:, 128:192], mk[:, 192:256]
-
+    ts(col(16), q_, 2.0, 1.0, A.is_ge, A.add, v_c)
+    ts(col(17), q_, 4.0, 2.0, A.is_ge, A.mult)
+    t = ts(col(18), q_, 8.0, 4.0, A.is_ge, A.mult)
+    t3 = ts(yw[:, 28:31], yw[:, 24:27], r_, None, A.subtract, None)
+    ts(ms[:, 0:16], im[:, 0:16], q_, LIFT, A.is_equal, A.mult, g_im)
+    tb = ts(ms[:, 32:48], im[:, 0:16], q_, None, A.is_ge, None)
+    t = ts(col(19), col(16), col(17), col(18), A.add, A.add, t)
+    ts(T.oq[:], i0, 0.0, q_, A.mult, A.add)
+    tb = tt(mw[:, 0:16], ms[:, 0:16], ms[:, 32:48], A.max, tb)
+    m16, m4 = T.mt[:, 0:240], T.mt[:, 256:384]
+    a_m16 = act(m16, mw[:, 0:16].indirect(T.oq[:, 0:15]), None, tb)
+    ts(yw[:, 12:15], yw[:, 28:31], col(14), -0.4375, A.mult, A.add, t3, a_my)
+    ts(yw[:, 15:18], yw[:, 28:31], col(15), -0.4375, A.mult, A.add)
+    ts(yw[:, 0:4], T.ci[:, 40:44], col(19), q_, A.mult, A.add, t, g_tm)
+    t = ts(yw[:, 4:12], T.ci[:, 40:48], col(19), q_, A.mult, A.add)
+    ts(mark[:, 2:4], im[:, 1:3], col(4), 2.0, A.is_equal, A.mult)
+    t = vcopy(pi[:, 12:30], yw[:, 0:18], t)
+    ts(mark[:, 4:8], im[:, 1:5], col(5), 2.0, A.is_equal, A.mult)
+    v_yl = vcopy(T.yl[:, 0:18], pi[:, 12:30], t)
+    a_yc = fun(ID, yc[:], T.one[:].indirect(T.yl[:, 0:18]), 1.0, -1.0, v_yl, g_one)
     v_k16 = vcopy(T.k16_0[:], T.kli[:], t_kl)
-    v_kf = vcopy(T.kf0[:, 0:16], T.kli[:])
-
+    a_n = act(fr(0, "nn", 0, 512, 4), T.one[:].indirect(T.k16_0[:, 0:8]), None, v_k16, g_nn)
     v_uq = quant(T.uq[:, 0:128], T.us[:, 0:128], T.ut[:, 0:512], t_u)
-    tk = tt(T.kf0[:, 16:24], T.kf0[:, 0:8], T.c127[:, 0:8], A.max, v_kf, v_c127)
-    v_up = vcopy(T.up[:, 0:128].bitcast(dt.uint32), T.uq[:, 0:128].bitcast(dt.uint32).indirect(T.uo[:, 0:8]), v_uq, v_uo)
-    v_kb = vcopy(T.kb0[:], T.kf0[:, 16:24], tk)
-    v_q1 = quant(T.xq0[:, 0:128], T.xs0[:, 0:128], T.x0[:, 0:512], t_x)
+    ts(T.fi[:, 0:4], T.yl[:, 0:4], 4.0, None, A.mult, None, v_yl)
+    ts(T.fi[:, 4:12], T.yl[:, 4:12], -4.0, 508.0, A.mult, A.add)
+    ts(T.fi[:, 12:13], T.yl[:, 12:13], 4.0, None, A.mult, None)
+    v_fi = ts(T.fi[:, 13:15], T.yl[:, 13:15], -4.0, 508.0, A.mult, A.add)
+    a_kt = act(fr(0, "kt"), fr(0, "nn").indirect(T.fi[:, 0:15]), None, a_n, v_fi)
     a_up = act(T.ups[:, 0:128], T.us[:, 0:128].indirect(T.uo[:, 0:8]), None, v_uq, v_uo)
-    a_kfr = act(T.fr0[:, 0:256], T.one[:].indirect(T.k16_0[:, 0:16]), None, v_k16, g_one)
-    fun(SG, cs[:, 18:19], r_, 1.0, -1.5)
-    fun(SG, cs[:, 19:20], q_, 1.0, -13.5)
-    fun(ID, cc[:, 0:32], T.ci[:, 0:32], 1.0, r_, g_ci4)
-    fun(ID, cs[:, 16:17], cs[:, 15:16], -1.0, 0.0)
-    fun(ID, cs[:, 17:18], cs[:, 15:16], -1.0, -1.0)
+    fun(ID, wa[:, 192:240], yc[:, 192:240], -8.0, -2.0, a_yc)
+    a_wa = fun(ID, wa[:, 240:288], yc[:, 240:288], 4.0, 0.0)
+    v_tk = fun(SG, T.tk[:], T.tr[:], 1.0, 0.0, g_tr)
+    ts(mark[:, 8:16], im[:, 1:9], col(6), 2.0, A.is_equal, A.mult)
+    t = ts(mark[:, 16:32], im[:, 1:17], col(7), 2.0, A.is_equal, A.mult)
+    v_up = vcopy(T.up[:, 0:128].bitcast(dt.uint32), T.uq[:, 0:128].bitcast(dt.uint32).indirect(T.uo[:, 0:8]), v_uq, v_uo)
+    v_sg = tt(mark[:, 32:48], mark[:, 1:32:2], mark[:, 0:32:2], A.subtract, t)
+    sgn = mark[:, 32:48]
+    ts(ms[:, 16:20], im[:, 0:4], r_, LIFT, A.is_equal, A.mult)
+    tb = ts(ms[:, 48:52], im[:, 0:4], r_, None, A.is_ge, None)
+
+    tw = tt(wt[:, 0:192], sgn.indirect(T.oq[:, 0:12]), yc[:, 0:192], A.mult, v_sg, a_yc)
+    tp = ts(wa[:, 64:128], sgn.indirect(T.oq[:, 0:4]), 0.0, None, A.max, None)
+    t2 = ts(wa[:, 0:64], wt[:, 0:64], 2.0, None, A.mult, None, tw)
+    v_q1 = quant(T.xq0[:, 0:128], T.xs0[:, 0:128], T.x0[:, 0:512], t_x)
     v_q2 = quant(T.xq0[:, 128:256], T.xs0[:, 128:256], T.x0[:, 512:1024])
-    t = scan(T.sc0[:, 13 * 256:14 * 256], m4, T.fr0[:, 0:256], a_kfr, a_m)
-    v_k4 = ts(T.k4_0[:], T.sc0[:, 13 * 256 + 3:14 * 256:4], un4, tau4, A.mult, A.add, t, v_cs)
+    tt(mw[:, 16:20], ms[:, 16:20], ms[:, 48:52], A.max, tb)
+    v_ot = ts(T.ot[:], i0, 0.0, tau, A.mult, A.add)
+    a_n = act(fr(0, "nn", 1, 512, 4), T.one[:].indirect(T.k16_0[:, 8:16]), None, a_kt)
+    a_m4 = act(m4, mw[:, 16:20].indirect(T.ot[:, 0:8]), None, v_ot)
+    t = scan(fr(0, "st"), m16[:, 0:240], fr(0, "kt"), a_kt, a_m16)
+    ta = tt(wa[:, 288:336], wa[:, 192:240], wa[:, 240:288], A.add, a_wa)
+    tt(wt[:, 0:64], wa[:, 0:64], wa[:, 64:128], A.add, t2, tp)
+    v_tl = ts(wr(0, "tl"), fr(0, "st", 15, 240, 16), un16, 1.0, A.mult, A.subtract, t)
+    tt(wt[:, 192:208], wa[:, 288:304], yc[:, 240:256], A.mult, ta)
+    t = tt(wt[:, 208:240], wa[:, 304:336], yc[:, 208:240], A.mult)
+    v_wt = fill(wt[:, 195:240:4], 0.0, t)
+
+    def four(r, *toks):
+        scan(fr(r, "n4", 0, 128), m4[:, 0:128], fr(r, "nn", 0, 512, 4), *toks)
+        return scan(fr(r, "n4", 128, 256), m4[:, 0:128], fr(r, "nn", 1, 512, 4))
+
+    def four_end(r, t):
+        return ts(wr(r, "k4"), fr(r, "n4", 3, 256, 4), un4x4, tau4, A.mult, A.add, t)
 
     wait("g", v_k16)
     rk = [remote(0, T.kin0[:], T.k16_0[:], "rk0"), 0, 0]
+    g_c8 = iota(T.ci[:, 0:32], [[8, 32]], 0, 0)
     g_e = []
     wait("g", iota(T.ones[:], [[0, 512]], 1, 0))
     for b in range(4):
         g_e.append(fin("g", g.affine_select(T.et[:, 512 * b:512 * b + 512], T.ones[:], [[-1, 512]], A.is_equal, 0.0, b, 4)))
 
+    def partner_list(r, *toks):
+        f1 = act(fr(r, "kp"), T.one[:].indirect(T["kin%d" % r][:, 0:16]), None, ("rk%d" % r, rk[r]))
+        f2 = act(fr(r, "kk", 0, 256), fr(r, "kp").indirect(T["k16_%d" % r][:, 0:16]), None, f1, *toks)
+        act(fr(r, "kk", 256, 512, 2), fr(r, "kk", 1, 256, 2), None, f2)
+        return act(fr(r, "kk", 257, 512, 2), fr(r, "kk", 0, 256, 2), None)
+
+    def signs(r, half, p):
+        if half == 0 and r:
+            t = fun(SG, fr(r, "tmp"), psv(4, 0, 128), -1.0, TINY, p)
+            bankuse[4] = [t]
+            return act(fr(r, "sg", 0, 128), fr(r, "tmp"), 0.5, t)
+        t = ts(fr(r, "sg", 128 * half, 128 * half + 128), psv(4 + half, 0, 128), 0.0, 0.5, A.is_le, A.subtract, p)
+        bankuse[4 + half] = [t]
+        return t
+
+    def scores(lq, ls, r, half, *toks):
+        a, b = 128 * half, 128 * half + 128
+        return mm(4 + half, 128, lq[:, 0:128], ls[:, 0:128], T["xq%d" % r][:, a:b], T["xs%d" % r][:, a:b], *toks, *bankuse[4 + half])
+
     bankuse = [[] for _ in range(8)]
     x_done = (t_x,)
+    p1 = scores(T.up, T.ups, 0, 0, v_q1, v_up, a_up)
+    s1 = signs(0, 0, p1)
+    tab = {}
     for r in range(ROUNDS):
         X, xk, Z, H, B = T["x%d" % r], T["xk%d" % r], T["z%d" % r], T["h%d" % r], T["b%d" % r]
-        xq, xs, bit, W, low, SC = T["xq%d" % r], T["xs%d" % r], T["bit%d" % r], T["w%d" % r], T["low%d" % r], T["sc%d" % r]
-        fr, sm, to, tw = T["fr%d" % r], T["sm%d" % r], T["to%d" % r], T["tt%d" % r]
         last = r == ROUNDS - 1
+        k16 = T["k16_%d" % r]
 
-        def sc(i):
-            return SC[:, 256 * i:256 * i + 256]
-
-        a_xk = act(xk[:], X[:].indirect(T["k4_%d" % r][:, 0:64]), 0.5, v_k4, *x_done)
+        p2 = scores(T.up, T.ups, r, 1, v_q2)
+        s2 = signs(r, 1, p2)
+        t = tt(fr(r, "tg"), fr(r, "sg").indirect(wr(r, "tl")), wt[:], A.mult, s1, s2, v_tl, v_wt)
+        if r == 0:
+            t4 = four(0, a_n, a_m4)
+        t = scan(fr(r, "ts"), T.tk[:], fr(r, "tg"), t, v_tk)
+        if r == 0:
+            v_k4 = four_end(0, t4)
+        a_xk = act(xk[:], X[:].indirect(wr(r, "k4")), 0.5, v_k4, *x_done)
         xk2 = T["xj%d" % r]
         wait("y", a_xk)
         d_xk = dma("y", "dxk", 16 * (r + 1), xk2[:], xk[:])
+        a_f = fun(ID, fr(r, "f"), fr(r, "sg").indirect(k16[:, 0:8]), -1.0, 1.5, s1, s2, v_k16)
+        a_f = fun(ID, fr(r, "f", 127, 128), q_, 0.0, 2.0, a_f)
 
-        sb = (4, 5)
-        p1 = mm(sb[0], 128, T.up[:, 0:128], T.ups[:, 0:128], xq[:, 0:128], xs[:, 0:128], v_q1, v_up, a_up, *bankuse[sb[0]])
-        p2 = mm(sb[1], 128, T.up[:, 0:128], T.ups[:, 0:128], xq[:, 128:256], xs[:, 128:256], v_q2, *bankuse[sb[1]])
-        ts(bit[:, 0:128], psv(sb[0], 0, 128), 0.0, None, A.is_gt, None, p1)
-        t = ts(bit[:, 128:256], psv(sb[1], 0, 128), 0.0, None, A.is_gt, None, p2)
-        bankuse[sb[0]], bankuse[sb[1]] = [t], [t]
-        tl = tt(W[:, 0:128], bit[:, 0:272].indirect(T["kb%d" % r][:, 0:8]), T.c21[:], A.add, t, v_kb, tab["bit"][r] if r else v_bit, g_c21)
-        t = scan(SC[:, 0:128], m16[:, 0:128], W[:, 0:128], tl)
-        th = tt(W[:, 128:256], T.c43[:], W[:, 0:128], A.subtract, g_c43)
-        t = tt(sm[:, 40:48], hic, SC[:, 15:128:16], A.subtract, t, v_hic)
-        v_tl = ts(to[:, 0:8], SC[:, 15:128:16], un16, 1.0, A.mult, A.subtract)
-        v_to = ts(to[:, 8:16], sm[:, 40:48], un16, 1.0, A.mult, A.subtract, t)
+        t = tt(fr(r, "tm", 0, 12), fr(r, "ts", 15, 192, 16), fr(r, "ts", 195, 240, 4), A.max, t)
+        if r == 0:
+            a = fun(ID, col(20), col(8), 0.125 - 0.125 / LIFT, 0.125 + 0.125 / LIFT)
+            fun(ID, col(21), col(9), 0.5 - 0.5 / LIFT, 0.5 + 0.5 / LIFT)
+            fun(ID, col(22), col(9), 1.0 - 1.0 / LIFT, 1.0 + 1.0 / LIFT)
+            fun(ID, col(23), col(3), 256.0, 0.0)
+            fun(ID, col(24), r_, 2.0, -1.0)
+            tab["col"] = fun(ID, col(25), r_, 4.0, 1.0)
+            tab["un"] = ts(col(26), un16, 0.25, None, A.mult, None)
+        t = vcopy(wr(r, "bl"), fr(r, "tm", 0, 12), t)
+        if r == 0:
+            tab["eq"] = ts(mw[:, 32:36], im[:, 1:5], r_, None, A.is_equal, None)
+        t = vcopy(fr(r, "t1"), T.cd[:].indirect(wr(r, "bl", 0, 4)), t, g_cd)
+        if r == 0:
+            tab["d0"] = fill(d0[:], -1.0)
+        t = vcopy(fr(r, "r0"), fr(r, "t1").indirect(wr(r, "bl", 4, 12)), t)
+        if r == 0:
+            fill(d0[:, 0:256:8], 0.0, tab["d0"])
+        v_r = t
+        t = scan(fr(r, "s0"), m16[:, 0:128], fr(r, "r0"), t)
+        v_cp = vcopy(fr(r, "c0"), fr(r, "r0", 0, 64))
+        v_l = ts(wr(r, "l0"), fr(r, "s0", 15, 128, 16), col(26), 0.2, A.mult, A.subtract, t, tab["un"])
 
-        lc = T["lc%d" % r]
-        v_low = vcopy(low[:, 128:256], W[:, 128:256], th)
-        v_lc = vcopy(lc[:, 128:256], W[:, 128:256])
-        a_w = act(W[:, 256:384], W[:, 0:256].indirect(to[:, 0:8]), None, v_tl)
-        v_w = vcopy(W[:, 384:512], W[:, 0:256].indirect(to[:, 8:16]), v_to)
-        scan(SC[:, 256:384], m16[:, 0:128], W[:, 256:384], a_w)
-        t = scan(SC[:, 384:512], m16[:, 0:128], W[:, 384:512], v_w)
-        t4 = scan(SC[:, 9 * 256:9 * 256 + 128], m4[:, 0:128], W[:, 0:128])
-        v_to = ts(to[:, 16:32], SC[:, 256 + 15:512:16], un16, 1.0, A.mult, A.subtract, t)
-        v_lc = (v_lc, a_pre[r])
-        for k in range(1, 7):
-            o, i, off = W[:, 256 * k + 256:256 * k + 512], W[:, 256 * k:256 * k + 256], to[:, 16 * k:16 * k + 16]
-            nl, pl = low[:, 256 * k:256 * k + 256], low[:, 256 * k - 256:256 * k]
-            if k < 6:
-                e = 256 - SHARE
-                a_w = act(o[:, 0:e], i.indirect(to[:, 16 * k:16 * k + e // 16]), None, v_to, a_w)
-                v_w = vcopy(o[:, e:256], i.indirect(to[:, 16 * k + e // 16:16 * k + 16]), v_to) if SHARE else None
-            else:
-                a_w = act(o[:, 128:256], i.indirect(to[:, 16 * k + 8:16 * k + 16]), None, v_to, a_w)
-            v_low = tt(nl, pl.indirect(off), lc[:, 256 * k - 256:256 * k], A.min, v_to, v_low, *v_lc)
-            if k < 6:
-                v_lc = (act(lc[:, 256 * k:256 * k + 256], nl, None, v_low),)
-                t = scan(sc(k + 1), m16, o, a_w, v_w)
-            else:
-                v_lc = (act(lc[:, 256 * k + 128:256 * k + 256], nl[:, 128:256], None, v_low),)
-                t = scan(SC[:, 256 * k + 384:256 * k + 512], m16[:, 0:128], o[:, 128:256], a_w)
-            if r == 0:
-                tables(k)
-            if k == 1:
-                ts(d1[:, 2:128:4], SC[:, 9 * 256 + 3:9 * 256 + 128:4], un4, tau4, A.mult, A.add, t4)
-            if k == 2:
-                td = ts(d1[:, 130:160:4], SC[:, 15:128:16], un16, 1.0, A.mult, A.subtract)
-            if k == 3:
-                td = ts(sm[:, 0:40], d1[:, 2:160:4], -2.0, None, A.mult, None, td)
-            if k == 4:
-                v_d = tt(d0[:, 2:160:4], sm[:, 0:40], d1[:, 3:160:4], A.add, td, tab[3])
-            h = 0 if k < 6 else 8
-            v_to = ts(to[:, 16 * k + 16 + h:16 * k + 32], SC[:, 256 * (k + 1) + 15 + 16 * h:256 * (k + 2):16], un16, 1.0, A.mult, A.subtract, t)
-        l8 = low[:, 7 * 256 + 128:8 * 256]
-        v_low = tt(l8, low[:, 6 * 256:7 * 256].indirect(to[:, 120:128]), lc[:, 6 * 256 + 128:7 * 256], A.min, v_to, v_low, *v_lc)
-        so = T["so%d" % r]
-        scan(SC[:, 2560:2624], m2, l8[:, 0:64], v_low, tab[5])
-        t4 = scan(SC[:, 2624:2752], m4[:, 0:128], l8)
-        scan(SC[:, 2816:2880], m8, l8[:, 0:64])
-        t16 = scan(SC[:, 2880:3008], m16[:, 0:128], l8)
-        tt(d1[:, 1:128:4], SC[:, 2561:2624:2], cmp_[:, 40:72], A.is_equal, t4)
-        e4 = tt(d1[:, 0:128:4], SC[:, 2627:2752:4], cmp_[:, 0:32], A.is_equal)
-        tt(d1[:, 129:160:4], SC[:, 2823:2880:8], cmp_[:, 72:80], A.is_equal, t16)
-        e16 = tt(d1[:, 128:160:4], SC[:, 2895:3008:16], cmp_[:, 32:40], A.is_equal)
-        s4 = chain(so[:, 0:128], d0[:, 0:128], d1[:, 0:128], e4, v_d)
-        s16 = chain(so[:, 128:160], d0[:, 128:160], d1[:, 128:160], e16)
-        clo = vcopy(tw[:, 0:32], so[:, 2:128:4], s4)
-        chi = vcopy(tw[:, 40:72], so[:, 3:128:4])
-        c16 = vcopy(tw[:, 32:40], so[:, 130:160:4], s16)
-
-        ne = rk[r]
-        f1 = act(fr[:, 256:512], T.one[:].indirect(T["kin%d" % r][:, 0:16]), None, ("rk%d" % r, ne), g_one)
-        f2 = act(fr[:, 512:768], fr[:, 256:512].indirect(T["k16_%d" % r][:, 0:16]), None, f1, v_k16)
-        act(fr[:, 768:896], fr[:, 512:768].indirect(tw[:, 32:40]), None, f2, c16)
+        side = []
+        if r == 0:
+            side += [lambda: fill(d1[:, 3:256:8], 0.0),
+                     lambda: tab.update(kf=tt(T.kf[:], mw[:, 32:36].indirect(T.ot[:, 0:8]), T.cd[:], A.mult, tab["eq"]))]
+        side += [lambda: tab.update(sf=scan(fr(r, "sf"), m4[:, 0:128], fr(r, "f"), a_f))]
+        if r == 0:
+            side += [lambda: tab.update(kf=fill(T.kf[:, 0:1], 0.0, tab["kf"])),
+                     lambda: tab.update(ke=tt(T.ke[:], T.kf[:, 0:128:2], T.kf[:, 1:128:2], A.add, tab["kf"]))]
+        a_r, v_m = v_r, v_r
+        rw, mn = fr(r, "r0", 0, 64), fr(r, "r0", 0, 64)
+        for lv in range(3):
+            off = wr(r, "l%d" % lv, 0, 4)
+            base = mn
+            for k in range(3):
+                i = 3 * lv + k + 1
+                if lv < 2:
+                    a_r = act(fr(r, "r%d" % i), rw.indirect(off), None, v_l, a_r)
+                    rw = fr(r, "r%d" % i)
+                v_m = tt(fr(r, "m%d" % i), mn.indirect(off), base if k else fr(r, "c%d" % lv), A.min, v_l, v_m, v_cp)
+                mn = fr(r, "m%d" % i)
+                if side and lv < 2:
+                    side.pop(0)()
+            if lv < 2:
+                t = scan(fr(r, "s%d" % (lv + 1)), m16[:, 0:64], rw, a_r)
+                v_cp = act(fr(r, "c%d" % (lv + 1)), mn, None, v_m)
+                if lv == 0:
+                    if r == 0:
+                        fun(ID, T.cc[:, 0:32], T.ci[:, 0:32], 1.0, col(24), g_c8, tab["col"])
+                        tab["cc"] = fun(ID, T.cc[:, 32:64], T.ci[:, 0:32], 2.0, col(25))
+                else:
+                    a_f1 = act(fr(r, "f1"), fr(r, "sf", 3, 128, 4), col(21), tab["sf"])
+                    a_dd = fun(ID, d0[:, 7:256:8], fr(r, "sf", 3, 128, 4), col(22), -3.0)
+                    if r == 0:
+                        a_kk = partner_list(0)
+                v_l = ts(wr(r, "l%d" % (lv + 1)), fr(r, "s%d" % (lv + 1), 15, 64, 16), col(26), 0.2, A.mult, A.subtract, t)
+            if lv == 1:
+                side = []
+        v_b = tt(d1[:, 7:256:8], fr(r, "f1"), T.cc[:, 0:32], A.add, a_f1, tab["cc"])
+        tt(d1[:, 0:256:2], mn.indirect(wr(r, "l0")), T.kf[:], A.is_equal, v_m, tab["ke"])
+        t = tt(d1[:, 1:256:4], mn, T.ke[:], A.is_equal)
+        t = chain(fr(r, "so"), d0[:], d1[:], t, a_dd)
+        tc = fr(r, "so", 7, 256, 8)
+        clo = ts(wr(r, "lo"), tc, 4.0, tau, A.mult, A.add, t)
+        ctn = ts(wr(r, "tn"), tc, col(23), None, A.add, None)
+        a_n = act(fr(r + 1, "nn"), fr(r, "kk").indirect(wr(r, "tn")), None, ctn, a_kk)
 
         def layer(qz, qzs, banks, tok):
             out = []
@@ -364,20 +408,19 @@ def rank_program(g, core, T, topo):
 
         def nm(s):
             return T["%s_%d" % (s, r)]
-        z1 = tt(Z[:, 0:512], xk[:].indirect(tw[:, 0:32]), xk2[:, 0:512], A.add, clo, a_xk, d_xk)
-        chi16 = vcopy(tw[:, 72:80], so[:, 131:160:4])
-        a_n = act(fr[:, 896:1024], fr[:, 512:768].indirect(tw[:, 72:80]), None, chi16)
+        z1 = tt(Z[:, 0:512], xk[:].indirect(wr(r, "lo")), xk2[:, 0:512], A.add, clo, a_xk, d_xk)
+        th = tt(fr(r, "hi"), T.cc[:, 32:64], tc, A.subtract)
         tq = quant(nm("qz")[:, 0:128], nm("qzs")[:, 0:128], Z[:, 0:512], z1)
+        chi = ts(wr(r, "hi"), fr(r, "hi"), 4.0, tau, A.mult, A.add, th)
         p = layer(nm("qz")[:, 0:128], nm("qzs")[:, 0:128], (0, 1, 2, 3), tq)
         h1 = []
         for b in range(4):
             h1.append(act(H[:, b:512:4], psv(b, 0, 128), 0.03125, p[b]))
             bankuse[b] = [h1[b]]
-        z2 = tt(Z[:, 512:768], xk[:].indirect(tw[:, 40:56]), xk2[:, 512:768], A.add, chi)
+        z2 = tt(Z[:, 512:768], xk[:].indirect(wr(r, "hi", 0, 16)), xk2[:, 512:768], A.add, chi)
         tq = quant(nm("qz")[:, 128:256], nm("qzs")[:, 128:256], Z[:, 256:768], z2)
         p = layer(nm("qz")[:, 128:256], nm("qzs")[:, 128:256], (4, 5, 6, 7), tq)
-        if not SINGLE:
-            tq1 = quant(nm("qh")[:, 0:128], nm("qhs")[:, 0:128], H[:, 0:512], h1[3])
+        tq1 = quant(nm("qh")[:, 0:128], nm("qhs")[:, 0:128], H[:, 0:512], h1[3])
         h2 = [None] * 4
         for b in (0, 2):
             h2[b] = ts(H[:, 512 + b:768:4], psv(4 + b, 64, 128), 0.03125, None, A.mult, None, p[b])
@@ -385,26 +428,20 @@ def rank_program(g, core, T, topo):
         for b in (1, 3):
             h2[b] = act(H[:, 512 + b:768:4], psv(4 + b, 64, 128), 0.03125, p[b])
             bankuse[4 + b] = [h2[b]]
-        if SINGLE:
-            tq2 = quant(nm("qh")[:, 0:192], nm("qhs")[:, 0:192], H[:, 0:768], h1[3], h2[2], h2[3])
-            wait("g", tq2)
-            na = remote(r, nm("cin")[:, 0:192].bitcast(dt.uint8), nm("qh")[:, 0:192].bitcast(dt.uint8), "ra%d" % r)
-            na += remote(r, nm("cins")[:, 0:192], nm("qhs")[:, 0:192], "ra%d" % r)
-        else:
-            tq2 = quant(nm("qh")[:, 128:256], nm("qhs")[:, 128:256], H[:, 256:768], h2[2], h2[3])
+        tq2 = quant(nm("qh")[:, 128:256], nm("qhs")[:, 128:256], H[:, 256:768], h2[2], h2[3])
 
-            wait("g", tq1)
-            na = remote(r, nm("cin")[:, 0:128].bitcast(dt.uint8), nm("qh")[:, 0:128].bitcast(dt.uint8), "ra%d" % r)
-            na += remote(r, nm("cins")[:, 0:128], nm("qhs")[:, 0:128], "ra%d" % r)
-            wait("g", tq2)
-            nb = remote(r, nm("cin")[:, 128:192].bitcast(dt.uint8), nm("qh")[:, 192:256].bitcast(dt.uint8), "rb%d" % r)
-            nb += remote(r, nm("cins")[:, 128:192], nm("qhs")[:, 192:256], "rb%d" % r)
+        wait("g", tq1)
+        na = remote(r, nm("cin")[:, 0:128].bitcast(dt.uint8), nm("qh")[:, 0:128].bitcast(dt.uint8), "ra%d" % r)
+        na += remote(r, nm("cins")[:, 0:128], nm("qhs")[:, 0:128], "ra%d" % r)
+        wait("g", tq2)
+        nb = remote(r, nm("cin")[:, 128:192].bitcast(dt.uint8), nm("qh")[:, 192:256].bitcast(dt.uint8), "rb%d" % r)
+        nb += remote(r, nm("cins")[:, 128:192], nm("qhs")[:, 192:256], "rb%d" % r)
 
-        z3 = tt(Z[:, 768:1024], xk[:].indirect(tw[:, 56:72]), xk2[:, 768:1024], A.add)
-        s16 = None
+        z3 = tt(Z[:, 768:1024], xk[:].indirect(wr(r, "hi", 16, 32)), xk2[:, 768:1024], A.add)
         if not last:
-            s16 = scan(sc(12), m16, fr[:, 768:1024], a_n)
-        s4 = scan(sc(13) if r else sc(9), m4, fr[:, 768:1024], a_n)
+            a_kt = act(fr(r + 1, "kt"), fr(r + 1, "nn").indirect(T.fi[:, 0:15]), None, a_n)
+            scan(fr(r + 1, "n16", 0, 128), m16[:, 0:128], fr(r + 1, "nn", 0, 512, 4), a_n)
+            s16 = scan(fr(r + 1, "n16", 128, 256), m16[:, 0:128], fr(r + 1, "nn", 1, 512, 4))
         tq = quant(nm("qz")[:, 256:384], nm("qzs")[:, 256:384], Z[:, 512:1024], z3)
         p = layer(nm("qz")[:, 256:384], nm("qzs")[:, 256:384], (0, 1, 2, 3), tq)
         for b in range(4):
@@ -412,20 +449,18 @@ def rank_program(g, core, T, topo):
             bankuse[b] = [t]
         a_b = t
         if not last:
-            prefill(r + 1)
-        s4o = 256 * (13 if r else 9)
-        if not last:
-            kf = T["kf%d" % (r + 1)]
-            v_k16 = ts(T["k16_%d" % (r + 1)][:], SC[:, 12 * 256 + 15:13 * 256:16], un16, 1.0, A.mult, A.subtract, s16)
-            v_kf = ts(kf[:, 0:16], SC[:, 12 * 256 + 15:13 * 256:16], un16, 1.0, A.mult, A.subtract)
-            v_k4 = ts(T["k4_%d" % (r + 1)][:], SC[:, s4o + 3:s4o + 256:4], un4, tau4, A.mult, A.add, s4)
-            t = tt(kf[:, 16:24], kf[:, 0:8], T.c127[:, 0:8], A.max, v_kf)
-            v_kb = vcopy(T["kb%d" % (r + 1)][:], kf[:, 16:24], t)
+            v_k16 = ts(T["k16_%d" % (r + 1)][:], fr(r + 1, "n16", 15, 256, 16), un16, 1.0, A.mult, A.subtract, s16)
             wait("g", v_k16)
             rk[r + 1] = remote(r + 1, T["kin%d" % (r + 1)][:], T["k16_%d" % (r + 1)][:], "rk%d" % (r + 1))
+        t4 = four(r + 1, a_n)
+        if not last:
+            t = scan(fr(r + 1, "st"), m16[:, 0:240], fr(r + 1, "kt"), a_kt)
+        v_k4 = four_end(r + 1, t4)
+        if not last:
+            v_tl = ts(wr(r + 1, "tl"), fr(r + 1, "st", 15, 240, 16), un16, 1.0, A.mult, A.subtract, t)
         else:
-            v_k4 = ts(T["k4_%d" % (r + 1)][:], SC[:, s4o + 3:s4o + 256:4], un4, tau4, A.mult, A.add, s4)
-            v_ky = ts(T.kyf[:], fr[:, 768:1024], 1.0, None, A.subtract, None)
+            ts(T.kyf[:, 0:128], fr(r + 1, "nn", 0, 512, 4), 1.0, None, A.subtract, None)
+            v_ky = ts(T.kyf[:, 128:256], fr(r + 1, "nn", 1, 512, 4), 1.0, None, A.subtract, None)
         if r == 0:
             for b in range(4):
                 v_e = quant(T.eq[:, 128 * b:128 * b + 128], T.es[:, 128 * b:128 * b + 128], T.et[:, 512 * b:512 * b + 512], g_e[b])
@@ -433,37 +468,31 @@ def rank_program(g, core, T, topo):
 
         cin, cins = nm("cin"), nm("cins")
         p, bt = [], []
-        if SINGLE:
-            for b in range(4):
-                p.append(mm(4 + b, 192, T.eq[:, 128 * b:128 * b + 128], T.es[:, 128 * b:128 * b + 128], cin[:, 0:192], cins[:, 0:192],
-                            ("ra%d" % r, na), v_e, *bankuse[4 + b]))
-            for b in range(4):
-                o, i = B[:, b:768:4], psv(4 + b, 0, 192)
-                t = vcopy(o, i, p[b]) if b % 2 == 0 else act(o, i, None, p[b])
-                bankuse[4 + b] = [t]
-                bt.append(t)
-        else:
-            for b in range(4):
-                p.append(mm(4 + b, 128, T.eq[:, 128 * b:128 * b + 128], T.es[:, 128 * b:128 * b + 128], cin[:, 0:128], cins[:, 0:128],
-                            ("ra%d" % r, na), v_e, *bankuse[4 + b]))
-            for b in range(4):
-                t = act(B[:, b:512:4], psv(4 + b, 0, 128), None, p[b])
-                bankuse[4 + b] = [t]
-            p = []
-            for b in range(4):
-                p.append(mm(b, 128, T.eq[:, 128 * b:128 * b + 128], T.es[:, 128 * b:128 * b + 128], cin[:, 64:192], cins[:, 64:192],
-                            ("rb%d" % r, nb), *bankuse[b]))
-            for b in range(4):
-                o, i = B[:, 512 + b:768:4], psv(b, 64, 128)
-                t = vcopy(o, i, p[b]) if b % 2 == 0 else act(o, i, None, p[b])
-                bankuse[b] = [t]
-                bt.append(t)
+        for b in range(4):
+            p.append(mm(4 + b, 128, T.eq[:, 128 * b:128 * b + 128], T.es[:, 128 * b:128 * b + 128], cin[:, 0:128], cins[:, 0:128],
+                        ("ra%d" % r, na), v_e, *bankuse[4 + b]))
+        for b in range(4):
+            t = act(B[:, b:512:4], psv(4 + b, 0, 128), None, p[b])
+            bankuse[4 + b] = [t]
+        p = []
+        for b in range(4):
+            p.append(mm(b, 128, T.eq[:, 128 * b:128 * b + 128], T.es[:, 128 * b:128 * b + 128], cin[:, 64:192], cins[:, 64:192],
+                        ("rb%d" % r, nb), *bankuse[b]))
+        for b in range(4):
+            o, i = B[:, 512 + b:768:4], psv(b, 64, 128)
+            t = vcopy(o, i, p[b]) if b % 2 == 0 else act(o, i, None, p[b])
+            bankuse[b] = [t]
+            bt.append(t)
 
-        nx, n4 = T["x%d" % (r + 1)], T["k4_%d" % (r + 1)]
+        nx = T["x%d" % (r + 1)]
         nq, ns = T["xq%d" % (r + 1)], T["xs%d" % (r + 1)]
-        g1 = tt(nx[:, 0:512], B[:].indirect(n4[:, 0:32]), X[:, 0:512], A.add, v_k4, a_b, *bt)
-        g2 = tt(nx[:, 512:1024], B[:].indirect(n4[:, 32:64]), X[:, 512:1024], A.add)
+        g1 = tt(nx[:, 0:512], B[:].indirect(wr(r + 1, "k4", 0, 32)), X[:, 0:512], A.add, v_k4, a_b, *bt)
         v_q1 = quant(nq[:, 0:128], ns[:, 0:128], nx[:, 0:512], g1)
+        g2 = tt(nx[:, 512:1024], B[:].indirect(wr(r + 1, "k4", 32, 64)), X[:, 512:1024], A.add)
+        if not last:
+            a_kk = partner_list(r + 1, v_k16)
+            p1 = scores(T.up, T.ups, r + 1, 0, v_q1)
+            s1 = signs(r + 1, 0, p1)
         v_q2 = quant(nq[:, 128:256], ns[:, 128:256], nx[:, 512:1024], g2)
         x_done = (g1, g2)
 
@@ -474,17 +503,18 @@ def rank_program(g, core, T, topo):
         queues[q].dma_start(o, i).then_inc(T.sem.dout, 16)
         nd[0] += 16
     xq, xs = T["xq%d" % ROUNDS], T["xs%d" % ROUNDS]
-    p1 = mm(4, 128, T.vq[:, 0:128], T.vqs[:, 0:128], xq[:, 0:128], xs[:, 0:128], v_q1, v_v, *bankuse[4])
-    p2 = mm(5, 128, T.vq[:, 0:128], T.vqs[:, 0:128], xq[:, 128:256], xs[:, 128:256], v_q2, *bankuse[5])
-    y1 = vcopy(T.yo[:, 0:128], psv(4, 0, 128), p1)
+    p1 = scores(T.vq, T.vqs, ROUNDS, 0, v_q1, v_v)
+    p2 = scores(T.vq, T.vqs, ROUNDS, 1, v_q2)
+    y1 = act(T.yo[:, 0:128], psv(4, 0, 128), None, p1)
     y2 = vcopy(T.yo[:, 128:256], psv(5, 0, 128), p2)
     out("y", T.kp[:], T.kyf[0:128:16, :], v_ky)
-    out("y", T.oc[:], xq[:, 0:256].bitcast(dt.uint8), v_q2)
+    out("y", T.oc[:, 0:512], xq[:, 0:128].bitcast(dt.uint8), v_q1)
+    out("a", T.y[:, 0:128], T.yo[:, 0:128], y1)
+    out("y", T.oc[:, 512:1024], xq[:, 128:256].bitcast(dt.uint8), v_q2)
     out("a", T.osc[0:4, :], xs[0:4, :], v_q2)
     out("y", T.osc[4:8, :], xs[32:36, :])
     out("a", T.osc[8:12, :], xs[64:68, :])
     out("y", T.osc[12:16, :], xs[96:100, :])
-    out("y", T.y[:, 0:128], T.yo[:, 0:128], y1)
-    out("a", T.y[:, 128:256], T.yo[:, 128:256], y2)
+    out("y", T.y[:, 128:256], T.yo[:, 128:256], y2)
 
     wait("g", ("dout", nd[0]), ("loc", loc[0]), *[(s, n) for s, n in done.items()])

@@ -3,9 +3,9 @@ from concourse.mybir import dt, AluOpType, ActivationFunctionType
 
 ROUNDS = 3
 LIFT = 512.0
-TINY = 2.0 ** -100
 A = AluOpType
-CP, ID, SG = ActivationFunctionType.Copy, ActivationFunctionType.Identity, ActivationFunctionType.Sign
+F = ActivationFunctionType
+CP, ID, SG = F.Copy, F.Identity, F.Sign
 
 
 def lay(*parts):
@@ -16,11 +16,11 @@ def lay(*parts):
     return out, at
 
 
-FREE, NFREE = lay(("sg", 256), ("tmp", 128), ("tg", 240), ("ts", 240), ("tm", 16), ("t1", 64), ("r0", 128), ("c0", 64), ("s0", 128),
+FREE, NFREE = lay(("sg", 256), ("tg", 288), ("ts", 288), ("tm", 16), ("t1", 64), ("r0", 128), ("c0", 64), ("s0", 128),
                   *[("r%d" % i, 64) for i in range(1, 7)], *[("m%d" % i, 64) for i in range(1, 10)], ("c1", 64), ("c2", 64),
                   ("s1", 64), ("s2", 64), ("f", 128), ("sf", 128), ("f1", 32), ("hi", 32), ("so", 256),
-                  ("nn", 512), ("kp", 256), ("kk", 512), ("n4", 256), ("n16", 256), ("kt", 240), ("st", 240))
-WRAP, NWRAP = lay(("bl", 12), ("l0", 8), ("l1", 4), ("l2", 4), ("lo", 32), ("hi", 32), ("tn", 32), ("k4", 64), ("tl", 15))
+                  ("nn", 512), ("kp", 256), ("kk", 512), ("n4", 256), ("n16", 256), ("kt", 288), ("st", 288))
+WRAP, NWRAP = lay(("bl", 12), ("l0", 8), ("l1", 4), ("l2", 4), ("lo", 32), ("hi", 32), ("tn", 32), ("k4", 64), ("tl", 18))
 
 SCRATCH = {
     "ps": ("psum", [128, 4096], "float32"),
@@ -34,16 +34,16 @@ SCRATCH = {
     "ones": ("sbuf", [128, 512], "bfloat16"),
     "et": ("sbuf", [128, 2048], "bfloat16"),
     "eq": ("sbuf", [128, 512], "float8_e4m3fn_x4"), "es": ("sbuf", [128, 512], "uint8"),
-    "pi": ("sbuf", [128, 32], "int32"),
+    "pi": ("sbuf", [128, 16], "int32"),
     "cs": ("sbuf", [128, 32], "float32"),
-    "im": ("sbuf", [128, 24], "float32"), "ms": ("sbuf", [128, 64], "bfloat16"), "mw": ("sbuf", [128, 48], "bfloat16"),
+    "im": ("sbuf", [128, 40], "float32"), "ms": ("sbuf", [128, 64], "bfloat16"), "mw": ("sbuf", [128, 48], "bfloat16"),
     "oq": ("sbuf", [128, 16], "uint16"), "ot": ("sbuf", [128, 16], "uint16"),
-    "mt": ("sbuf", [128, 512], "bfloat16"),
+    "mt": ("sbuf", [128, 320], "bfloat16"),
     "one": ("sbuf", [128, 256], "bfloat16"), "cd": ("sbuf", [128, 128], "bfloat16"),
-    "ci": ("sbuf", [128, 48], "float32"), "cc": ("sbuf", [128, 64], "float32"),
-    "mark": ("sbuf", [128, 48], "bfloat16"), "yw": ("sbuf", [128, 32], "float32"), "yl": ("sbuf", [128, 24], "uint16"),
-    "fi": ("sbuf", [128, 16], "uint16"), "yc": ("sbuf", [128, 288], "bfloat16"), "wa": ("sbuf", [128, 352], "bfloat16"),
-    "wt": ("sbuf", [128, 240], "bfloat16"), "tk": ("sbuf", [128, 240], "bfloat16"), "tr": ("sbuf", [128, 240], "bfloat16"),
+    "ci": ("sbuf", [128, 64], "float32"), "cc": ("sbuf", [128, 64], "float32"),
+    "mark": ("sbuf", [128, 48], "bfloat16"), "yw": ("sbuf", [128, 32], "float32"), "yl": ("sbuf", [128, 32], "uint16"),
+    "fi": ("sbuf", [128, 48], "uint16"), "yc": ("sbuf", [128, 192], "bfloat16"), "wa": ("sbuf", [128, 128], "bfloat16"),
+    "wt": ("sbuf", [128, 288], "bfloat16"), "tk": ("sbuf", [128, 80], "bfloat16"), "tr": ("sbuf", [128, 80], "bfloat16"),
     "kf": ("sbuf", [128, 128], "bfloat16"), "ke": ("sbuf", [128, 64], "bfloat16"),
     "d0": ("sbuf", [128, 256], "bfloat16"), "d1": ("sbuf", [128, 256], "bfloat16"),
     "uo": ("sbuf", [128, 8], "uint16"),
@@ -165,8 +165,19 @@ def rank_program(g, core, T, topo):
         lo, hi = WRAP[name]
         return T["wr%d" % r][:, lo + a:(hi if b is None else lo + b)]
 
+    def half(r, h):
+        return fr(r, "nn", h, 512, 4) if r else fr(0, "nn", 128 * h, 128 * h + 128)
+
     loc = [0]
-    cs, d0, d1, pi, im, mark, yw, wa, wt, yc = T.cs, T.d0, T.d1, T.pi, T.im, T.mark, T.yw, T.wa, T.wt, T.yc
+    tab = {}
+    side = {}
+
+    def gap(name):
+        for f in side.pop(name, []):
+            f()
+
+    cs, d0, d1, pi, im, mark, yw, yl, wa, wt, yc, ci = T.cs, T.d0, T.d1, T.pi, T.im, T.mark, T.yw, T.yl, T.wa, T.wt, T.yc, T.ci
+    ms, mw, m16, m4, fi = T.ms, T.mw, T.mt[:, 0:192], T.mt[:, 192:320], T.fi
 
     def col(i):
         return cs[:, i:i + 1]
@@ -179,108 +190,111 @@ def rank_program(g, core, T, topo):
     t_v = dma("y", "dv", 16, T.vt[:], T.v[:])
 
     g_pi = iota(pi[:, 0:1], [[0, 1]], 0, 1, False)
-    g_pj = iota(pi[:, 1:2], [[0, 1]], 127, -1, False)
     g_im = iota(im[:, 0:17], [[1, 17]], -1, 0)
-    g_tm = iota(T.ci[:, 40:48], [[-1, 8]], 6, 0)
-    g_ci = iota(T.ci[:, 32:40], [[16, 8]], 0, 0)
+    iota(ci[:, 40:52], [[0, 2], [-1, 6]], 6, 0)
+    g_tm = iota(ci[:, 52:58], [[-1, 6]], 2, 0)
+    g_ci = iota(ci[:, 32:40], [[16, 8]], 0, 0)
     g_one = iota(T.one[:], [[1, 256]], 1, 0)
-    g_nn = iota(fr(0, "nn"), [[0, 512]], 1, 0)
-    iota(T.tr[:, 0:192], [[0, 12], [1, 16]], 0, 0)
-    g_tr = iota(T.tr[:, 192:240], [[0, 12], [1, 4]], 0, 0)
-    g_cd = iota(T.cd[:], [[4, 64], [1, 2]], 1, 0)
+    g_dn = iota(im[:, 24:40], [[-1, 16]], 15, 0)
+    iota(T.tr[:, 0:64], [[0, 4], [1, 16]], 0, 0)
+    g_tr = iota(T.tr[:, 64:80], [[0, 4], [1, 4]], 0, 0)
     i0 = im[:, 1:17]
 
-    fill(yw[:, 24:26], 7.0)
-    fill(yw[:, 26:27], 3.0)
     fill(mark[:, 0:2], 0.0)
-    ts(pi[:, 2:3], pi[:, 0:1], 15, None, A.bitwise_and, None, g_pi)
-    ts(pi[:, 3:4], pi[:, 0:1], 2, 3, A.logical_shift_right, A.bitwise_and)
-    ts(pi[:, 4:5], pi[:, 0:1], 3, None, A.bitwise_and, None)
-    ts(pi[:, 5:6], pi[:, 0:1], 1, None, A.bitwise_and, None)
+    v_w0 = fill(wt[:], 0.0)
     for d in range(4):
-        t = ts(pi[:, 6 + d:7 + d], pi[:, 1:2], 15, 3 - d, A.bitwise_and, A.logical_shift_right, g_pj)
-    v_c = vcopy(cs[:, 0:8], pi[:, 2:10], t)
-    q_, r_, tau = col(0), col(1), col(2)
-    v_uo = vcopy(T.uo[:], T.ci[:, 32:40], g_ci)
+        ts(pi[:, 2 + d:3 + d], pi[:, 0:1], 3 - d, (2 << d) - 1, A.logical_shift_right, A.bitwise_and, g_pi)
+    t = ts(pi[:, 6:7], pi[:, 0:1], 3, None, A.bitwise_and, None)
+    v_c = vcopy(cs[:, 0:5], pi[:, 2:7], t)
+    q_, r_, tau = col(3), col(1), col(4)
 
-    fun(SG, col(8), q_, 1.0, -14.5, v_c)
-    t = fun(SG, col(9), r_, 1.0, -2.5)
-    a_tau = fun(ActivationFunctionType.Square, col(10), tau, 0.25, 0.125)
-    fun(ID, col(11), col(8), 0.5 - 0.5 / LIFT, 0.5 + 0.5 / LIFT, t)
-    fun(ID, col(12), col(9), 2.0 - 2.0 / LIFT, 2.0 + 2.0 / LIFT)
+    def on_top(a):
+        for e in range(3):
+            w = []
+            for lead in range(7 - 4 * (a // 2), 3 - 4 * (a // 2), -1):
+                child = lead >> (2 - e)
+                w.append((4 * (child & 1) - 2) * (child if a == 0 else child >> 1))
+            at = 96 * a + 64 + e
+            if w[0] - w[1] == w[2] - w[3] and any(w):
+                t = iota(wt[:, at:at + 16:4], [[w[2] - w[0], 2], [w[1] - w[0], 2]], w[0], 0)
+            elif any(w):
+                iota(wt[:, at:at + 16:8], [[w[2] - w[0], 2]], w[0], 0)
+                t = iota(wt[:, at + 4:at + 16:8], [[w[3] - w[1], 2]], w[1], 0)
+        return t
+    wait("g", v_w0)
+    on_top(0)
+    g_wt = on_top(1)
+    g_c8 = iota(ci[:, 0:32], [[8, 32]], 0, 0)
+    g_cd = iota(T.cd[:], [[4, 64], [1, 2]], 1, 0)
+
+    a_tau = fun(F.Square, col(10), tau, 0.25, 0.125, v_c)
+    fun(SG, col(16), col(2), 1.0, 0.0)
+    t = fun(SG, col(17), r_, 1.0, 0.0)
+    a_my = fun(ID, col(14), col(10), 1.0, 0.109375, a_tau)
+    td = fun(ID, col(18), col(0), 4.0, 1.0)
+    fun(SG, col(8), q_, 1.0, -14.5)
+    td = fun(ID, col(15), col(17), 2.0, col(18), td)
+    a_sg = fun(SG, col(9), r_, 1.0, -2.5)
     fun(ID, col(13), tau, 1.0, -4.0)
-    fun(ID, col(14), col(10), 1.0, 0.109375, a_tau)
-    a_my = fun(ID, col(15), col(10), 2.0, 0.21875)
+    td = fun(ID, col(19), col(16), 1.0, col(15), td)
+    fun(ID, col(11), col(8), 0.5 - 0.5 / LIFT, 0.5 + 0.5 / LIFT, a_sg)
+    a_un = fun(ID, col(12), col(9), 2.0 - 2.0 / LIFT, 2.0 + 2.0 / LIFT)
     un16, un4x4, tau4 = col(11), col(12), col(13)
 
-    ms, mw = T.ms, T.mw
-    ts(col(16), q_, 2.0, 1.0, A.is_ge, A.add, v_c)
-    ts(col(17), q_, 4.0, 2.0, A.is_ge, A.mult)
-    t = ts(col(18), q_, 8.0, 4.0, A.is_ge, A.mult)
-    t3 = ts(yw[:, 28:31], yw[:, 24:27], r_, None, A.subtract, None)
-    ts(ms[:, 0:16], im[:, 0:16], q_, LIFT, A.is_equal, A.mult, g_im)
+    ts(ms[:, 0:16], im[:, 0:16], q_, LIFT, A.is_equal, A.mult, v_c, g_im)
     tb = ts(ms[:, 32:48], im[:, 0:16], q_, None, A.is_ge, None)
-    t = ts(col(19), col(16), col(17), col(18), A.add, A.add, t)
+    t3 = ts(yw[:, 0:3], ci[:, 40:58:6], r_, 1.0, A.subtract, A.add, g_tm)
     ts(T.oq[:], i0, 0.0, q_, A.mult, A.add)
     tb = tt(mw[:, 0:16], ms[:, 0:16], ms[:, 32:48], A.max, tb)
-    m16, m4 = T.mt[:, 0:240], T.mt[:, 256:384]
-    a_m16 = act(m16, mw[:, 0:16].indirect(T.oq[:, 0:15]), None, tb)
-    ts(yw[:, 12:15], yw[:, 28:31], col(14), -0.4375, A.mult, A.add, t3, a_my)
-    ts(yw[:, 15:18], yw[:, 28:31], col(15), -0.4375, A.mult, A.add)
-    ts(yw[:, 0:4], T.ci[:, 40:44], col(19), q_, A.mult, A.add, t, g_tm)
-    t = ts(yw[:, 4:12], T.ci[:, 40:48], col(19), q_, A.mult, A.add)
-    ts(mark[:, 2:4], im[:, 1:3], col(4), 2.0, A.is_equal, A.mult)
-    t = vcopy(pi[:, 12:30], yw[:, 0:18], t)
-    ts(mark[:, 4:8], im[:, 1:5], col(5), 2.0, A.is_equal, A.mult)
-    v_yl = vcopy(T.yl[:, 0:18], pi[:, 12:30], t)
-    a_yc = fun(ID, yc[:], T.one[:].indirect(T.yl[:, 0:18]), 1.0, -1.0, v_yl, g_one)
-    v_k16 = vcopy(T.k16_0[:], T.kli[:], t_kl)
-    a_n = act(fr(0, "nn", 0, 512, 4), T.one[:].indirect(T.k16_0[:, 0:8]), None, v_k16, g_nn)
-    v_uq = quant(T.uq[:, 0:128], T.us[:, 0:128], T.ut[:, 0:512], t_u)
-    ts(T.fi[:, 0:4], T.yl[:, 0:4], 4.0, None, A.mult, None, v_yl)
-    ts(T.fi[:, 4:12], T.yl[:, 4:12], -4.0, 508.0, A.mult, A.add)
-    ts(T.fi[:, 12:13], T.yl[:, 12:13], 4.0, None, A.mult, None)
-    v_fi = ts(T.fi[:, 13:15], T.yl[:, 13:15], -4.0, 508.0, A.mult, A.add)
-    a_kt = act(fr(0, "kt"), fr(0, "nn").indirect(T.fi[:, 0:15]), None, a_n, v_fi)
-    a_up = act(T.ups[:, 0:128], T.us[:, 0:128].indirect(T.uo[:, 0:8]), None, v_uq, v_uo)
-    fun(ID, wa[:, 192:240], yc[:, 192:240], -8.0, -2.0, a_yc)
-    a_wa = fun(ID, wa[:, 240:288], yc[:, 240:288], 4.0, 0.0)
-    v_tk = fun(SG, T.tk[:], T.tr[:], 1.0, 0.0, g_tr)
-    ts(mark[:, 8:16], im[:, 1:9], col(6), 2.0, A.is_equal, A.mult)
-    t = ts(mark[:, 16:32], im[:, 1:17], col(7), 2.0, A.is_equal, A.mult)
-    v_up = vcopy(T.up[:, 0:128].bitcast(dt.uint32), T.uq[:, 0:128].bitcast(dt.uint32).indirect(T.uo[:, 0:8]), v_uq, v_uo)
-    v_sg = tt(mark[:, 32:48], mark[:, 1:32:2], mark[:, 0:32:2], A.subtract, t)
-    sgn = mark[:, 32:48]
+    a_m16 = act(m16, mw[:, 0:16].indirect(T.oq[:, 0:12]), None, tb)
+    t3 = ts(yw[:, 4:7], yw[:, 0:3], col(14), -0.4375, A.mult, A.add, t3, a_my)
+    v_uo = vcopy(T.uo[:], ci[:, 32:40], g_ci)
     ts(ms[:, 16:20], im[:, 0:4], r_, LIFT, A.is_equal, A.mult)
+    t3 = vcopy(pi[:, 10:13], yw[:, 4:7], t3)
     tb = ts(ms[:, 48:52], im[:, 0:4], r_, None, A.is_ge, None)
-
-    tw = tt(wt[:, 0:192], sgn.indirect(T.oq[:, 0:12]), yc[:, 0:192], A.mult, v_sg, a_yc)
-    tp = ts(wa[:, 64:128], sgn.indirect(T.oq[:, 0:4]), 0.0, None, A.max, None)
-    t2 = ts(wa[:, 0:64], wt[:, 0:64], 2.0, None, A.mult, None, tw)
+    ts(T.ot[:], i0, 0.0, tau, A.mult, A.add)
+    for d in range(2):
+        ts(mark[:, 2 << d:4 << d], im[:, 40 - (2 << d):40], col(d), 2.0, A.is_equal, A.mult, g_dn)
+    t = ts(yl[:, 0:18], ci[:, 40:58], col(19), q_, A.mult, A.add, td)
+    v_ot = tt(mw[:, 16:20], ms[:, 16:20], ms[:, 48:52], A.max, tb)
+    a_m4 = act(m4, mw[:, 16:20].indirect(T.ot[:, 0:8]), None, v_ot)
+    for d in range(2, 4):
+        tb = ts(mark[:, 2 << d:4 << d], im[:, 40 - (2 << d):40], col(d), 2.0, A.is_equal, A.mult)
+    v_yl = vcopy(yl[:, 4:18:6], pi[:, 10:13], t3, t)
+    v_uq = quant(T.uq[:, 0:128], T.us[:, 0:128], T.ut[:, 0:512], t_u)
+    v_k16 = vcopy(T.k16_0[:], T.kli[:], t_kl)
+    v_sg = tt(mark[:, 32:48], mark[:, 1:32:2], mark[:, 0:32:2], A.subtract, tb)
+    sgn = mark[:, 32:48]
+    v_fi = ts(fi[:, 6:18], yl[:, 6:18], -1.0, 127.0, A.mult, A.add, v_yl)
+    a_y2 = fun(ID, yc[:, 0:64], T.one[:].indirect(yl[:, 0:4]), 2.0, -2.0, v_yl, g_one)
+    a_n = act(half(0, 0), T.one[:].indirect(T.k16_0[:, 0:8]), None, v_k16)
+    a_yc = fun(ID, yc[:, 64:128], T.one[:].indirect(yl[:, 0:4]), 1.0, -1.0)
+    act(fr(0, "kt", 0, 96), half(0, 0).indirect(yl[:, 0:6]), None, a_n)
+    a_kt = act(fr(0, "kt", 96, 192), half(0, 0).indirect(fi[:, 6:12]), None, v_fi)
+    a_wa = fun(F.Relu, wa[:, 64:128], sgn.indirect(T.oq[:, 0:4]), 1.0, 0.0, v_sg)
+    a_n = act(half(0, 1), T.one[:].indirect(T.k16_0[:, 8:16]), None)
+    v_tk = fun(SG, T.tk[:], T.tr[:], 1.0, 0.0, g_tr)
+    tab["un"] = fun(ID, col(20), col(8), 0.125 - 0.125 / LIFT, 0.125 + 0.125 / LIFT)
+    vcopy(T.up[:, 0:128].bitcast(dt.uint32), T.uq[:, 0:128].bitcast(dt.uint32).indirect(T.uo[:, 0:8]), v_uq, v_uo)
+    v_up = vcopy(T.ups[:, 0:128], T.us[:, 0:128].indirect(T.uo[:, 0:8]))
+    tw = tt(wa[:, 0:64], sgn.indirect(T.oq[:, 0:4]), yc[:, 0:64], A.mult, a_y2, v_sg)
+    tt(wt[:, 96:160], sgn.indirect(T.oq[:, 0:4]), yc[:, 64:128], A.mult, v_w0, a_yc)
     v_q1 = quant(T.xq0[:, 0:128], T.xs0[:, 0:128], T.x0[:, 0:512], t_x)
     v_q2 = quant(T.xq0[:, 128:256], T.xs0[:, 128:256], T.x0[:, 512:1024])
-    tt(mw[:, 16:20], ms[:, 16:20], ms[:, 48:52], A.max, tb)
-    v_ot = ts(T.ot[:], i0, 0.0, tau, A.mult, A.add)
-    a_n = act(fr(0, "nn", 1, 512, 4), T.one[:].indirect(T.k16_0[:, 8:16]), None, a_kt)
-    a_m4 = act(m4, mw[:, 16:20].indirect(T.ot[:, 0:8]), None, v_ot)
-    t = scan(fr(0, "st"), m16[:, 0:240], fr(0, "kt"), a_kt, a_m16)
-    ta = tt(wa[:, 288:336], wa[:, 192:240], wa[:, 240:288], A.add, a_wa)
-    tt(wt[:, 0:64], wa[:, 0:64], wa[:, 64:128], A.add, t2, tp)
-    v_tl = ts(wr(0, "tl"), fr(0, "st", 15, 240, 16), un16, 1.0, A.mult, A.subtract, t)
-    tt(wt[:, 192:208], wa[:, 288:304], yc[:, 240:256], A.mult, ta)
-    t = tt(wt[:, 208:240], wa[:, 304:336], yc[:, 208:240], A.mult)
-    v_wt = fill(wt[:, 195:240:4], 0.0, t)
+    t = scan(fr(0, "st", 0, 192), m16, fr(0, "kt", 0, 192), a_kt, a_m16)
+    v_wt = tt(wt[:, 0:64], wa[:, 0:64], wa[:, 64:128], A.add, tw, a_wa)
+    v_tl = ts(wr(0, "tl", 0, 12), fr(0, "st", 15, 192, 16), un16, 1.0, A.mult, A.subtract, t, a_un)
 
-    def four(r, *toks):
-        scan(fr(r, "n4", 0, 128), m4[:, 0:128], fr(r, "nn", 0, 512, 4), *toks)
-        return scan(fr(r, "n4", 128, 256), m4[:, 0:128], fr(r, "nn", 1, 512, 4))
+    def four(r, h, *toks):
+        return scan(fr(r, "n4", 128 * h, 128 * h + 128), m4, half(r, h), *toks)
 
     def four_end(r, t):
         return ts(wr(r, "k4"), fr(r, "n4", 3, 256, 4), un4x4, tau4, A.mult, A.add, t)
 
     wait("g", v_k16)
     rk = [remote(0, T.kin0[:], T.k16_0[:], "rk0"), 0, 0]
-    g_c8 = iota(T.ci[:, 0:32], [[8, 32]], 0, 0)
+    g_w2 = on_top(2)
+    tab["x"] = None
     g_e = []
     wait("g", iota(T.ones[:], [[0, 512]], 1, 0))
     for b in range(4):
@@ -292,75 +306,125 @@ def rank_program(g, core, T, topo):
         act(fr(r, "kk", 256, 512, 2), fr(r, "kk", 1, 256, 2), None, f2)
         return act(fr(r, "kk", 257, 512, 2), fr(r, "kk", 0, 256, 2), None)
 
-    def signs(r, half, p):
-        if half == 0 and r:
-            t = fun(SG, fr(r, "tmp"), psv(4, 0, 128), -1.0, TINY, p)
-            bankuse[4] = [t]
-            return act(fr(r, "sg", 0, 128), fr(r, "tmp"), 0.5, t)
-        t = ts(fr(r, "sg", 128 * half, 128 * half + 128), psv(4 + half, 0, 128), 0.0, 0.5, A.is_le, A.subtract, p)
-        bankuse[4 + half] = [t]
-        return t
+    def scores(lq, ls, r, h, *toks):
+        a, b = 128 * h, 128 * h + 128
+        return mm(4 + h, 128, lq[:, 0:128], ls[:, 0:128], T["xq%d" % r][:, a:b], T["xs%d" % r][:, a:b], *toks, *bankuse[4 + h])
 
-    def scores(lq, ls, r, half, *toks):
-        a, b = 128 * half, 128 * half + 128
-        return mm(4 + half, 128, lq[:, 0:128], ls[:, 0:128], T["xq%d" % r][:, a:b], T["xs%d" % r][:, a:b], *toks, *bankuse[4 + half])
+    def put(name, key, f, *a):
+        side.setdefault(name, []).append(lambda: tab.update({key: f(*[tab[x] if isinstance(x, str) else x for x in a])}))
 
     bankuse = [[] for _ in range(8)]
     x_done = (t_x,)
-    p1 = scores(T.up, T.ups, 0, 0, v_q1, v_up, a_up)
-    s1 = signs(0, 0, p1)
-    tab = {}
     for r in range(ROUNDS):
         X, xk, Z, H, B = T["x%d" % r], T["xk%d" % r], T["z%d" % r], T["h%d" % r], T["b%d" % r]
         last = r == ROUNDS - 1
         k16 = T["k16_%d" % r]
+        tg, tsc, sg = fr(r, "tg"), fr(r, "ts"), fr(r, "sg")
 
-        p2 = scores(T.up, T.ups, r, 1, v_q2)
-        s2 = signs(r, 1, p2)
-        t = tt(fr(r, "tg"), fr(r, "sg").indirect(wr(r, "tl")), wt[:], A.mult, s1, s2, v_tl, v_wt)
+        def tree(a, *toks):
+            return tt(tg[:, 96 * a:96 * a + 80], sg.indirect(wr(r, "tl", 6 * a, 6 * a + 5)), wt[:, 96 * a:96 * a + 80], A.mult, *toks)
+
+        def climb(a, *toks):
+            return scan(tsc[:, 96 * a:96 * a + 80], T.tk[:, 0:80], tg[:, 96 * a:96 * a + 80], *toks)
+
+        def top(a, *toks):
+            return tt(fr(r, "tm", 4 * a, 4 * a + 4), tsc[:, 96 * a + 15:96 * a + 64:16], tsc[:, 96 * a + 67:96 * a + 80:4], A.max, *toks)
+
+        def step(a, *toks):
+            return vcopy(wr(r, "bl", 4 * a, 4 * a + 4), fr(r, "tm", 4 * a, 4 * a + 4), *toks)
+
+        def wrap(out, src, *toks):
+            return ts(out, src, col(20), 0.2, A.mult, A.subtract, *toks)
+
+        for h in range(2):
+            p = scores(T.up, T.ups, r, h, (v_q1, v_q2)[h], v_up)
+            s = ts(sg[:, 128 * h:128 * h + 128], psv(4 + h, 0, 128), 0.0, 0.5, A.is_le, A.subtract, p)
+            bankuse[4 + h] = [s]
         if r == 0:
-            t4 = four(0, a_n, a_m4)
-        t = scan(fr(r, "ts"), T.tk[:], fr(r, "tg"), t, v_tk)
+            four(0, 0, a_m4)
+            t4 = four(0, 1, a_n)
+        tb_ = tree(0, s, v_tl, v_wt, g_wt)
+        tg_ = tree(1)
         if r == 0:
             v_k4 = four_end(0, t4)
+        tb_ = climb(0, tb_, v_tk)
+        tg_ = climb(1, tg_)
+        tb_ = top(0, tb_)
+        tg_ = top(1, tg_)
+        tb_ = step(0, tb_)
+        if r == 0:
+            a_kt = act(fr(0, "kt", 192, 288), half(0, 0).indirect(fi[:, 12:18]), None)
+            ta = fun(F.Abs, col(5), tau, 1.0, -2.0)
+            fun(ID, col(21), col(9), 0.5 - 0.5 / LIFT, 0.5 + 0.5 / LIFT)
+            fun(ID, col(22), col(9), 1.0 - 1.0 / LIFT, 1.0 + 1.0 / LIFT)
+            fun(ID, col(24), r_, 2.0, -1.0)
+            tb = fun(ID, col(25), r_, 4.0, 1.0)
+            ta = fun(F.Abs, col(6), col(5), 256.0, -256.0, ta)
+            fun(ID, T.cc[:, 0:32], ci[:, 0:32], 1.0, col(24), g_c8, tb)
+            fun(ID, T.cc[:, 32:64], ci[:, 0:32], 2.0, col(25))
+            tab["cc"] = fun(ID, col(23), col(6), -1.0, 256.0, ta)
         a_xk = act(xk[:], X[:].indirect(wr(r, "k4")), 0.5, v_k4, *x_done)
         xk2 = T["xj%d" % r]
         wait("y", a_xk)
         d_xk = dma("y", "dxk", 16 * (r + 1), xk2[:], xk[:])
-        a_f = fun(ID, fr(r, "f"), fr(r, "sg").indirect(k16[:, 0:8]), -1.0, 1.5, s1, s2, v_k16)
-        a_f = fun(ID, fr(r, "f", 127, 128), q_, 0.0, 2.0, a_f)
 
-        t = tt(fr(r, "tm", 0, 12), fr(r, "ts", 15, 192, 16), fr(r, "ts", 195, 240, 4), A.max, t)
+        def bits():
+            t = fun(ID, fr(r, "f"), sg.indirect(k16[:, 0:8]), -1.0, 1.5, s, v_k16)
+            tab["f"] = fun(ID, fr(r, "f", 127, 128), q_, 0.0, 2.0, t)
+
+        def back():
+            tab["x"] = act(fr(r, "r0", 64, 128), fr(r, "t1").indirect(wr(r, "bl", 8, 12)), None, tab["x"])
+
+        def place():
+            tab["f1"] = act(fr(r, "f1"), fr(r, "sf", 3, 128, 4), col(21), tab["sf"])
+            tab["dd"] = fun(ID, d0[:, 7:256:8], fr(r, "sf", 3, 128, 4), col(22), -3.0, tab["d0"])
+        third = (("x", tree, 2, "x"), ("x", climb, 2, "x"), ("x", top, 2, "x"), ("x", step, 2, "x"))
+        wrap3 = (("x", scan, fr(r, "s0", 64, 128), m16[:, 0:64], fr(r, "r0", 64, 128), "x"),
+                 ("x", wrap, wr(r, "l0", 4, 8), fr(r, "s0", 64 + 15, 128, 16), "x"))
+        bit4 = ("sf", scan, fr(r, "sf"), m4, fr(r, "f"), "f")
+        base4 = ("b", tt, d1[:, 7:256:8], fr(r, "f1"), T.cc[:, 0:32], A.add, "f1", "cc")
         if r == 0:
-            a = fun(ID, col(20), col(8), 0.125 - 0.125 / LIFT, 0.125 + 0.125 / LIFT)
-            fun(ID, col(21), col(9), 0.5 - 0.5 / LIFT, 0.5 + 0.5 / LIFT)
-            fun(ID, col(22), col(9), 1.0 - 1.0 / LIFT, 1.0 + 1.0 / LIFT)
-            fun(ID, col(23), col(3), 256.0, 0.0)
-            fun(ID, col(24), r_, 2.0, -1.0)
-            tab["col"] = fun(ID, col(25), r_, 4.0, 1.0)
-            tab["un"] = ts(col(26), un16, 0.25, None, A.mult, None)
-        t = vcopy(wr(r, "bl"), fr(r, "tm", 0, 12), t)
-        if r == 0:
-            tab["eq"] = ts(mw[:, 32:36], im[:, 1:5], r_, None, A.is_equal, None)
-        t = vcopy(fr(r, "t1"), T.cd[:].indirect(wr(r, "bl", 0, 4)), t, g_cd)
-        if r == 0:
-            tab["d0"] = fill(d0[:], -1.0)
-        t = vcopy(fr(r, "r0"), fr(r, "t1").indirect(wr(r, "bl", 4, 12)), t)
-        if r == 0:
-            fill(d0[:, 0:256:8], 0.0, tab["d0"])
-        v_r = t
-        t = scan(fr(r, "s0"), m16[:, 0:128], fr(r, "r0"), t)
+            put("t1", "z", ts, yc[:, 128:192], T.one[:].indirect(yl[:, 12:16]), 1.0, None, A.subtract, None)
+            put("r0", "z", tt, wt[:, 192:256], sgn.indirect(T.oq[:, 0:4]), yc[:, 128:192], A.mult, "z", g_w2)
+            put("s0", "x", scan, fr(0, "st", 192, 288), m16[:, 0:96], fr(0, "kt", 192, 288), a_kt)
+            put("l0", "eq", ts, mw[:, 32:36], im[:, 1:5], r_, None, A.is_equal, None)
+            put("l0", "x", ts, wr(0, "tl", 12, 18), fr(0, "st", 192 + 15, 288, 16), un16, 1.0, A.mult, A.subtract, "x")
+            for name, call in zip(("m1", "m2", "m3", "s1"), third):
+                put(name, *call)
+            put("m2", "d1", fill, d1[:, 3:256:8], 0.0)
+            put("m3", "d0", fill, d0[:], -1.0)
+            put("s1", "d0", fill, d0[:, 0:256:8], 0.0, "d0")
+            put("m4", "kf", tt, T.kf[:], mw[:, 32:36].indirect(T.ot[:, 0:8]), T.cd[:], A.mult, "eq")
+            put("m5", "kf", fill, T.kf[:, 0:1], 0.0, "kf")
+            put("m6", "ke", tt, T.ke[:], T.kf[:, 0:128:2], T.kf[:, 1:128:2], A.add, "kf")
+            side["c2"] = [back, bits]
+            put("m7", *wrap3[0])
+            put("m8", *wrap3[1])
+            put("m8", *bit4)
+            side["m8"] += [place, lambda: tab.update(kk=partner_list(0))]
+            put("e", *base4)
+            for b, name in enumerate(("m9", "z2", "h1", "h2")):
+                put(name, "e", quant, T.eq[:, 128 * b:128 * b + 128], T.es[:, 128 * b:128 * b + 128], T.et[:, 512 * b:512 * b + 512], g_e[b])
+        else:
+            bits()
+            for name, call in zip(("t1", "r0", "s0", "l0"), third):
+                put(name, *call)
+            put("m1", *bit4)
+            side["c1"], side["c2"] = [back], [place]
+            put("m4", *wrap3[0])
+            put("m5", *wrap3[1])
+            put("m7", *base4)
+        tg_ = step(1, tg_)
+        t = vcopy(fr(r, "t1"), T.cd[:].indirect(wr(r, "bl", 0, 4)), tb_, g_cd)
+        gap("t1")
+        v_r = vcopy(fr(r, "r0", 0, 64), fr(r, "t1").indirect(wr(r, "bl", 4, 8)), t, tg_)
+        gap("r0")
+        t = scan(fr(r, "s0", 0, 64), m16[:, 0:64], fr(r, "r0", 0, 64), v_r)
         v_cp = vcopy(fr(r, "c0"), fr(r, "r0", 0, 64))
-        v_l = ts(wr(r, "l0"), fr(r, "s0", 15, 128, 16), col(26), 0.2, A.mult, A.subtract, t, tab["un"])
+        gap("s0")
+        v_l = wrap(wr(r, "l0", 0, 4), fr(r, "s0", 15, 64, 16), t, tab["un"])
+        gap("l0")
 
-        side = []
-        if r == 0:
-            side += [lambda: fill(d1[:, 3:256:8], 0.0),
-                     lambda: tab.update(kf=tt(T.kf[:], mw[:, 32:36].indirect(T.ot[:, 0:8]), T.cd[:], A.mult, tab["eq"]))]
-        side += [lambda: tab.update(sf=scan(fr(r, "sf"), m4[:, 0:128], fr(r, "f"), a_f))]
-        if r == 0:
-            side += [lambda: tab.update(kf=fill(T.kf[:, 0:1], 0.0, tab["kf"])),
-                     lambda: tab.update(ke=tt(T.ke[:], T.kf[:, 0:128:2], T.kf[:, 1:128:2], A.add, tab["kf"]))]
         a_r, v_m = v_r, v_r
         rw, mn = fr(r, "r0", 0, 64), fr(r, "r0", 0, 64)
         for lv in range(3):
@@ -373,31 +437,24 @@ def rank_program(g, core, T, topo):
                     rw = fr(r, "r%d" % i)
                 v_m = tt(fr(r, "m%d" % i), mn.indirect(off), base if k else fr(r, "c%d" % lv), A.min, v_l, v_m, v_cp)
                 mn = fr(r, "m%d" % i)
-                if side and lv < 2:
-                    side.pop(0)()
-            if lv < 2:
-                t = scan(fr(r, "s%d" % (lv + 1)), m16[:, 0:64], rw, a_r)
-                v_cp = act(fr(r, "c%d" % (lv + 1)), mn, None, v_m)
-                if lv == 0:
-                    if r == 0:
-                        fun(ID, T.cc[:, 0:32], T.ci[:, 0:32], 1.0, col(24), g_c8, tab["col"])
-                        tab["cc"] = fun(ID, T.cc[:, 32:64], T.ci[:, 0:32], 2.0, col(25))
-                else:
-                    a_f1 = act(fr(r, "f1"), fr(r, "sf", 3, 128, 4), col(21), tab["sf"])
-                    a_dd = fun(ID, d0[:, 7:256:8], fr(r, "sf", 3, 128, 4), col(22), -3.0)
-                    if r == 0:
-                        a_kk = partner_list(0)
-                v_l = ts(wr(r, "l%d" % (lv + 1)), fr(r, "s%d" % (lv + 1), 15, 64, 16), col(26), 0.2, A.mult, A.subtract, t)
-            if lv == 1:
-                side = []
-        v_b = tt(d1[:, 7:256:8], fr(r, "f1"), T.cc[:, 0:32], A.add, a_f1, tab["cc"])
-        tt(d1[:, 0:256:2], mn.indirect(wr(r, "l0")), T.kf[:], A.is_equal, v_m, tab["ke"])
+                gap("m%d" % i)
+            if lv == 2:
+                break
+            t = scan(fr(r, "s%d" % (lv + 1)), m16[:, 0:64], rw, a_r)
+            v_cp = act(fr(r, "c%d" % (lv + 1)), mn, None, v_m)
+            gap("s%d" % (lv + 1))
+            gap("c%d" % (lv + 1))
+            v_l = wrap(wr(r, "l%d" % (lv + 1)), fr(r, "s%d" % (lv + 1), 15, 64, 16), t)
+        tt(d1[:, 0:256:2], mn.indirect(wr(r, "l0")), T.kf[:], A.is_equal, v_m, tab["ke"], tab["x"])
         t = tt(d1[:, 1:256:4], mn, T.ke[:], A.is_equal)
-        t = chain(fr(r, "so"), d0[:], d1[:], t, a_dd)
+        gap("e")
+        t = chain(fr(r, "so"), d0[:], d1[:], t, tab["dd"], tab["b"])
         tc = fr(r, "so", 7, 256, 8)
         clo = ts(wr(r, "lo"), tc, 4.0, tau, A.mult, A.add, t)
         ctn = ts(wr(r, "tn"), tc, col(23), None, A.add, None)
-        a_n = act(fr(r + 1, "nn"), fr(r, "kk").indirect(wr(r, "tn")), None, ctn, a_kk)
+        th = tt(fr(r, "hi"), T.cc[:, 32:64], tc, A.subtract)
+        if r:
+            a_n = act(fr(r + 1, "nn"), fr(r, "kk").indirect(wr(r, "tn")), None, ctn, tab["kk"])
 
         def layer(qz, qzs, banks, tok):
             out = []
@@ -406,29 +463,30 @@ def rank_program(g, core, T, topo):
                               tok, t_wc, t_ws, *bankuse[banks[b]]))
             return out
 
+        def scaled(on, out, bank, a, p):
+            t = ts(out, psv(bank, a, 128), 0.03125, None, A.mult, None, p) if on == "v" else act(out, psv(bank, a, 128), 0.03125, p)
+            bankuse[bank] = [t]
+            return t
+
         def nm(s):
             return T["%s_%d" % (s, r)]
         z1 = tt(Z[:, 0:512], xk[:].indirect(wr(r, "lo")), xk2[:, 0:512], A.add, clo, a_xk, d_xk)
-        th = tt(fr(r, "hi"), T.cc[:, 32:64], tc, A.subtract)
-        tq = quant(nm("qz")[:, 0:128], nm("qzs")[:, 0:128], Z[:, 0:512], z1)
         chi = ts(wr(r, "hi"), fr(r, "hi"), 4.0, tau, A.mult, A.add, th)
-        p = layer(nm("qz")[:, 0:128], nm("qzs")[:, 0:128], (0, 1, 2, 3), tq)
-        h1 = []
-        for b in range(4):
-            h1.append(act(H[:, b:512:4], psv(b, 0, 128), 0.03125, p[b]))
-            bankuse[b] = [h1[b]]
+        tq = quant(nm("qz")[:, 0:128], nm("qzs")[:, 0:128], Z[:, 0:512], z1)
+        p1 = layer(nm("qz")[:, 0:128], nm("qzs")[:, 0:128], (0, 1, 2, 3), tq)
+        h1 = [scaled("a", H[:, b:512:4], b, 0, p1[b]) for b in range(3)]
         z2 = tt(Z[:, 512:768], xk[:].indirect(wr(r, "hi", 0, 16)), xk2[:, 512:768], A.add, chi)
+        gap("z2")
         tq = quant(nm("qz")[:, 128:256], nm("qzs")[:, 128:256], Z[:, 256:768], z2)
-        p = layer(nm("qz")[:, 128:256], nm("qzs")[:, 128:256], (4, 5, 6, 7), tq)
-        tq1 = quant(nm("qh")[:, 0:128], nm("qhs")[:, 0:128], H[:, 0:512], h1[3])
-        h2 = [None] * 4
-        for b in (0, 2):
-            h2[b] = ts(H[:, 512 + b:768:4], psv(4 + b, 64, 128), 0.03125, None, A.mult, None, p[b])
-            bankuse[4 + b] = [h2[b]]
-        for b in (1, 3):
-            h2[b] = act(H[:, 512 + b:768:4], psv(4 + b, 64, 128), 0.03125, p[b])
-            bankuse[4 + b] = [h2[b]]
-        tq2 = quant(nm("qh")[:, 128:256], nm("qhs")[:, 128:256], H[:, 256:768], h2[2], h2[3])
+        p2 = layer(nm("qz")[:, 128:256], nm("qzs")[:, 128:256], (4, 5, 6, 7), tq)
+        h1.append(scaled("v", H[:, 3:512:4], 3, 0, p1[3]))
+        gap("h1")
+        tq1 = quant(nm("qh")[:, 0:128], nm("qhs")[:, 0:128], H[:, 0:512], *h1)
+        h2 = [scaled("aavv"[b], H[:, 512 + b:768:4], 4 + b, 64, p2[b]) for b in range(4)]
+        gap("h2")
+        tq2 = quant(nm("qh")[:, 128:256], nm("qhs")[:, 128:256], H[:, 256:768], *h2)
+        if r == 0:
+            a_n = act(fr(r + 1, "nn"), fr(r, "kk").indirect(wr(r, "tn")), None, ctn, tab["kk"])
 
         wait("g", tq1)
         na = remote(r, nm("cin")[:, 0:128].bitcast(dt.uint8), nm("qh")[:, 0:128].bitcast(dt.uint8), "ra%d" % r)
@@ -439,60 +497,63 @@ def rank_program(g, core, T, topo):
 
         z3 = tt(Z[:, 768:1024], xk[:].indirect(wr(r, "hi", 16, 32)), xk2[:, 768:1024], A.add)
         if not last:
-            a_kt = act(fr(r + 1, "kt"), fr(r + 1, "nn").indirect(T.fi[:, 0:15]), None, a_n)
-            scan(fr(r + 1, "n16", 0, 128), m16[:, 0:128], fr(r + 1, "nn", 0, 512, 4), a_n)
-            s16 = scan(fr(r + 1, "n16", 128, 256), m16[:, 0:128], fr(r + 1, "nn", 1, 512, 4))
+            if r == 0:
+                ts(fi[:, 24:30], yl[:, 0:6], 4.0, None, A.mult, None)
+                v_fi = ts(fi[:, 30:42], fi[:, 6:18], 4.0, None, A.mult, None)
+            else:
+                scan(fr(r + 1, "n16", 0, 128), m16[:, 0:128], half(r + 1, 0), a_n)
+                s16 = scan(fr(r + 1, "n16", 128, 256), m16[:, 0:128], half(r + 1, 1))
+            a_kt = act(fr(r + 1, "kt"), fr(r + 1, "nn").indirect(fi[:, 24:42]), None, a_n, v_fi)
         tq = quant(nm("qz")[:, 256:384], nm("qzs")[:, 256:384], Z[:, 512:1024], z3)
         p = layer(nm("qz")[:, 256:384], nm("qzs")[:, 256:384], (0, 1, 2, 3), tq)
-        for b in range(4):
-            t = act(B[:, 768 + b:1024:4], psv(b, 64, 128), 0.03125, p[b])
-            bankuse[b] = [t]
-        a_b = t
+        a_b = [scaled("a", B[:, 768 + b:1024:4], b, 64, p[b]) for b in range(4)][3]
+        if r == 0:
+            scan(fr(r + 1, "n16", 0, 128), m16[:, 0:128], half(r + 1, 0), a_n)
+            s16 = scan(fr(r + 1, "n16", 128, 256), m16[:, 0:128], half(r + 1, 1))
+        four(r + 1, 0, a_n)
+        t4 = four(r + 1, 1)
         if not last:
             v_k16 = ts(T["k16_%d" % (r + 1)][:], fr(r + 1, "n16", 15, 256, 16), un16, 1.0, A.mult, A.subtract, s16)
             wait("g", v_k16)
             rk[r + 1] = remote(r + 1, T["kin%d" % (r + 1)][:], T["k16_%d" % (r + 1)][:], "rk%d" % (r + 1))
-        t4 = four(r + 1, a_n)
-        if not last:
-            t = scan(fr(r + 1, "st"), m16[:, 0:240], fr(r + 1, "kt"), a_kt)
+            scan(fr(r + 1, "st", 0, 192), m16, fr(r + 1, "kt", 0, 192), a_kt)
+            t = scan(fr(r + 1, "st", 192, 288), m16[:, 0:96], fr(r + 1, "kt", 192, 288))
         v_k4 = four_end(r + 1, t4)
-        if not last:
-            v_tl = ts(wr(r + 1, "tl"), fr(r + 1, "st", 15, 240, 16), un16, 1.0, A.mult, A.subtract, t)
-        else:
-            ts(T.kyf[:, 0:128], fr(r + 1, "nn", 0, 512, 4), 1.0, None, A.subtract, None)
-            v_ky = ts(T.kyf[:, 128:256], fr(r + 1, "nn", 1, 512, 4), 1.0, None, A.subtract, None)
-        if r == 0:
-            for b in range(4):
-                v_e = quant(T.eq[:, 128 * b:128 * b + 128], T.es[:, 128 * b:128 * b + 128], T.et[:, 512 * b:512 * b + 512], g_e[b])
+        if r == 1:
             v_v = quant(T.vq[:, 0:128], T.vqs[:, 0:128], T.vt[:], t_v)
+        if not last:
+            v_tl = ts(wr(r + 1, "tl"), fr(r + 1, "st", 15, 288, 16), un16, 1.0, A.mult, A.subtract, t)
+        else:
+            ts(T.kyf[:, 0:128], half(r + 1, 0), 1.0, None, A.subtract, None)
+            v_ky = ts(T.kyf[:, 128:256], half(r + 1, 1), 1.0, None, A.subtract, None)
 
         cin, cins = nm("cin"), nm("cins")
         p, bt = [], []
         for b in range(4):
             p.append(mm(4 + b, 128, T.eq[:, 128 * b:128 * b + 128], T.es[:, 128 * b:128 * b + 128], cin[:, 0:128], cins[:, 0:128],
-                        ("ra%d" % r, na), v_e, *bankuse[4 + b]))
+                        ("ra%d" % r, na), tab["e"], *bankuse[4 + b]))
         for b in range(4):
-            t = act(B[:, b:512:4], psv(4 + b, 0, 128), None, p[b])
+            o, i = B[:, b:512:4], psv(4 + b, 0, 128)
+            t = act(o, i, None, p[b]) if b % 2 == 0 else vcopy(o, i, p[b])
             bankuse[4 + b] = [t]
+            bt.append(t)
         p = []
         for b in range(4):
             p.append(mm(b, 128, T.eq[:, 128 * b:128 * b + 128], T.es[:, 128 * b:128 * b + 128], cin[:, 64:192], cins[:, 64:192],
                         ("rb%d" % r, nb), *bankuse[b]))
         for b in range(4):
             o, i = B[:, 512 + b:768:4], psv(b, 64, 128)
-            t = vcopy(o, i, p[b]) if b % 2 == 0 else act(o, i, None, p[b])
+            t = act(o, i, None, p[b]) if b == 1 else vcopy(o, i, p[b])
             bankuse[b] = [t]
             bt.append(t)
 
         nx = T["x%d" % (r + 1)]
         nq, ns = T["xq%d" % (r + 1)], T["xs%d" % (r + 1)]
         g1 = tt(nx[:, 0:512], B[:].indirect(wr(r + 1, "k4", 0, 32)), X[:, 0:512], A.add, v_k4, a_b, *bt)
-        v_q1 = quant(nq[:, 0:128], ns[:, 0:128], nx[:, 0:512], g1)
         g2 = tt(nx[:, 512:1024], B[:].indirect(wr(r + 1, "k4", 32, 64)), X[:, 512:1024], A.add)
         if not last:
-            a_kk = partner_list(r + 1, v_k16)
-            p1 = scores(T.up, T.ups, r + 1, 0, v_q1)
-            s1 = signs(r + 1, 0, p1)
+            tab["kk"] = partner_list(r + 1, v_k16)
+        v_q1 = quant(nq[:, 0:128], ns[:, 0:128], nx[:, 0:512], g1)
         v_q2 = quant(nq[:, 128:256], ns[:, 128:256], nx[:, 512:1024], g2)
         x_done = (g1, g2)
 
@@ -505,16 +566,15 @@ def rank_program(g, core, T, topo):
     xq, xs = T["xq%d" % ROUNDS], T["xs%d" % ROUNDS]
     p1 = scores(T.vq, T.vqs, ROUNDS, 0, v_q1, v_v)
     p2 = scores(T.vq, T.vqs, ROUNDS, 1, v_q2)
-    y1 = act(T.yo[:, 0:128], psv(4, 0, 128), None, p1)
+    y1 = vcopy(T.yo[:, 0:128], psv(4, 0, 128), p1)
     y2 = vcopy(T.yo[:, 128:256], psv(5, 0, 128), p2)
     out("y", T.kp[:], T.kyf[0:128:16, :], v_ky)
-    out("y", T.oc[:, 0:512], xq[:, 0:128].bitcast(dt.uint8), v_q1)
-    out("a", T.y[:, 0:128], T.yo[:, 0:128], y1)
-    out("y", T.oc[:, 512:1024], xq[:, 128:256].bitcast(dt.uint8), v_q2)
+    out("y", T.oc[:], xq[:, 0:256].bitcast(dt.uint8), v_q2)
     out("a", T.osc[0:4, :], xs[0:4, :], v_q2)
     out("y", T.osc[4:8, :], xs[32:36, :])
     out("a", T.osc[8:12, :], xs[64:68, :])
     out("y", T.osc[12:16, :], xs[96:100, :])
+    out("a", T.y[:, 0:128], T.yo[:, 0:128], y1)
     out("y", T.y[:, 128:256], T.yo[:, 128:256], y2)
 
     wait("g", ("dout", nd[0]), ("loc", loc[0]), *[(s, n) for s, n in done.items()])

@@ -3,6 +3,7 @@ from concourse.mybir import dt, AluOpType, ActivationFunctionType
 
 ROUNDS = 3
 LIFT = 512.0
+AHEAD = 80
 A = AluOpType
 F = ActivationFunctionType
 CP, ID, SG = F.Copy, F.Identity, F.Sign
@@ -17,10 +18,10 @@ def lay(*parts):
 
 
 FREE, NFREE = lay(("sg", 256), ("tg", 288), ("ts", 288), ("tm", 16), ("t1", 64), ("r0", 128), ("c0", 64), ("s0", 128),
-                  *[("r%d" % i, 64) for i in range(1, 7)], *[("m%d" % i, 64) for i in range(1, 10)], ("c1", 64), ("c2", 64),
-                  ("s1", 64), ("s2", 64), ("f", 128), ("sf", 128), ("f1", 32), ("hi", 32), ("so", 256),
-                  ("nn", 512), ("kp", 256), ("kk", 512), ("n4", 256), ("n16", 256), ("kt", 288), ("st", 288))
-WRAP, NWRAP = lay(("bl", 12), ("l0", 8), ("l1", 4), ("l2", 4), ("lo", 32), ("hi", 32), ("tn", 32), ("k4", 64), ("tl", 18))
+                  *[("r%d" % i, 64) for i in range(1, 9)], *[("m%d" % i, 64) for i in range(1, 10)],
+                  *[("s%d" % i, 64) for i in range(1, 5)], ("f", 128), ("sf", 128), ("f1", 32), ("hi", 32), ("so", 192), ("sp", 64), ("ss", 64), ("u", 64), ("su", 64), ("g", 64),
+                  ("nn", 512), ("kp", 256), ("kk", 512), ("n4", 256), ("n16", 256), ("kt", 288), ("k2", 288), ("st", 288))
+WRAP, NWRAP = lay(("bl", 12), *[("l%d" % i, 4) for i in range(5)], ("sp", 4), ("u", 4), ("lo", 32), ("hi", 32), ("tn", 32), ("k4", 64), ("tl", 18))
 
 SCRATCH = {
     "ps": ("psum", [128, 4096], "float32"),
@@ -31,8 +32,8 @@ SCRATCH = {
     "up": ("sbuf", [128, 128], "float8_e4m3fn_x4"), "ups": ("sbuf", [128, 128], "uint8"),
     "vq": ("sbuf", [128, 128], "float8_e4m3fn_x4"), "vqs": ("sbuf", [128, 128], "uint8"),
     "wq": ("sbuf", [128, 512], "float8_e4m3fn_x4"), "wqs": ("sbuf", [128, 512], "uint8"),
-    "ones": ("sbuf", [128, 512], "bfloat16"),
-    "et": ("sbuf", [128, 2048], "bfloat16"),
+    "ones": ("sbuf", [128, 514], "bfloat16"),
+    "et": ("sbuf", [128, 1056], "bfloat16"),
     "eq": ("sbuf", [128, 512], "float8_e4m3fn_x4"), "es": ("sbuf", [128, 512], "uint8"),
     "pi": ("sbuf", [128, 16], "int32"),
     "cs": ("sbuf", [128, 32], "float32"),
@@ -43,26 +44,28 @@ SCRATCH = {
     "ci": ("sbuf", [128, 64], "float32"), "cc": ("sbuf", [128, 64], "float32"),
     "mark": ("sbuf", [128, 48], "bfloat16"), "yw": ("sbuf", [128, 32], "float32"), "yl": ("sbuf", [128, 32], "uint16"),
     "fi": ("sbuf", [128, 48], "uint16"), "yc": ("sbuf", [128, 192], "bfloat16"), "wa": ("sbuf", [128, 128], "bfloat16"),
-    "wt": ("sbuf", [128, 288], "bfloat16"), "tk": ("sbuf", [128, 80], "bfloat16"), "tr": ("sbuf", [128, 80], "bfloat16"),
+    "wt": ("sbuf", [128, 288], "bfloat16"), "tk": ("sbuf", [128, 160], "bfloat16"),
+    "w2": ("sbuf", [128, 288], "bfloat16"), "pf": ("sbuf", [128, 192], "bfloat16"), "pl": ("sbuf", [128, 8], "uint16"),
+    "tr": ("sbuf", [128, 80], "bfloat16"),
     "kf": ("sbuf", [128, 128], "bfloat16"), "ke": ("sbuf", [128, 64], "bfloat16"),
     "d0": ("sbuf", [128, 256], "bfloat16"), "d1": ("sbuf", [128, 256], "bfloat16"),
-    "uo": ("sbuf", [128, 8], "uint16"),
+    "uo": ("sbuf", [128, 8], "uint16"), "zl": ("sbuf", [128, 32], "uint16"),
     "kyf": ("sbuf", [128, 256], "float32"),
     "yo": ("sbuf", [128, 256], "float32"),
 }
 for _r in range(ROUNDS + 1):
     SCRATCH["x%d" % _r] = ("sbuf", [128, 1024], "bfloat16")
     SCRATCH["xq%d" % _r] = ("sbuf", [128, 256], "float8_e4m3fn_x4")
-    SCRATCH["xs%d" % _r] = ("sbuf", [128, 256], "uint8")
+    SCRATCH["xs%d" % _r] = ("sbuf", [128, 896 if _r < ROUNDS else 256], "uint8")
     SCRATCH["fr%d" % _r] = ("sbuf", [128, NFREE], "bfloat16")
     SCRATCH["wr%d" % _r] = ("sbuf", [128, NWRAP], "uint16")
 for _r in range(ROUNDS):
-    for _n, _w, _d in (("xk", 1024, "bfloat16"), ("xj", 1024, "bfloat16"), ("z", 1024, "bfloat16"), ("h", 768, "bfloat16"), ("b", 1024, "bfloat16"),
+    for _n, _w, _d in (("xk", 1024, "bfloat16"), ("xj", 1536, "bfloat16"), ("z", 1024, "bfloat16"), ("h", 768, "bfloat16"), ("b", 1024, "bfloat16"),
                        ("k16_", 16, "uint16"), ("kin", 16, "uint16")):
         SCRATCH["%s%d" % (_n, _r)] = ("sbuf", [128, _w], _d)
     for _n, _w in (("qz", 384), ("qh", 256), ("cin", 192)):
         SCRATCH["%s_%d" % (_n, _r)] = ("sbuf", [128, _w], "float8_e4m3fn_x4")
-        SCRATCH["%ss_%d" % (_n, _r)] = ("sbuf", [128, _w], "uint8")
+    SCRATCH["la_%d" % _r] = ("sbuf", [128, 192], "uint8")
 
 SEMAPHORES = ["sv", "sa", "st", "sg", "dx", "du", "dk", "dwc", "dws", "dv", "dxk", "dout", "loc"]
 SEMAPHORES += ["%s%d" % (n, r) for r in range(ROUNDS) for n in ("rk", "ra", "rb")]
@@ -185,6 +188,7 @@ def rank_program(g, core, T, topo):
     t_kl = dma("y", "dk", 16, T.kli[:], T.kl[:])
     t_x = dma("y", "dx", 16, T.x0[:], T.x[:])
     t_u = dma("a", "du", 16, T.ut[:], T.u[:])
+    wait("y", t_x)
     t_wc = dma("y", "dwc", 16, T.wq[:, 0:512].bitcast(dt.uint8), T.wc[:])
     t_ws = dma("y", "dws", 16, T.wqs[:], T.ws[:])
     t_v = dma("y", "dv", 16, T.vt[:], T.v[:])
@@ -206,6 +210,7 @@ def rank_program(g, core, T, topo):
         ts(pi[:, 2 + d:3 + d], pi[:, 0:1], 3 - d, (2 << d) - 1, A.logical_shift_right, A.bitwise_and, g_pi)
     t = ts(pi[:, 6:7], pi[:, 0:1], 3, None, A.bitwise_and, None)
     v_c = vcopy(cs[:, 0:5], pi[:, 2:7], t)
+    v_uo = vcopy(T.uo[:], ci[:, 32:40], g_ci)
     q_, r_, tau = col(3), col(1), col(4)
 
     def on_top(a):
@@ -228,15 +233,15 @@ def rank_program(g, core, T, topo):
     g_cd = iota(T.cd[:], [[4, 64], [1, 2]], 1, 0)
 
     a_tau = fun(F.Square, col(10), tau, 0.25, 0.125, v_c)
-    fun(SG, col(16), col(2), 1.0, 0.0)
-    t = fun(SG, col(17), r_, 1.0, 0.0)
-    a_my = fun(ID, col(14), col(10), 1.0, 0.109375, a_tau)
+    fun(SG, cs[:, 15:17], cs[:, 1:3], 1.0, 0.0)
+    fun(SG, col(17), r_, 1.0, 0.0)
     td = fun(ID, col(18), col(0), 4.0, 1.0)
+    a_my = fun(ID, col(14), col(10), 1.0, 0.109375, a_tau)
     fun(SG, col(8), q_, 1.0, -14.5)
-    td = fun(ID, col(15), col(17), 2.0, col(18), td)
     a_sg = fun(SG, col(9), r_, 1.0, -2.5)
+    wait("a", td)
+    td = fin("a", g.scalar.activation(cs[:, 28:32], cs[:, 15:19], ID, accum_out=col(19)))
     fun(ID, col(13), tau, 1.0, -4.0)
-    td = fun(ID, col(19), col(16), 1.0, col(15), td)
     fun(ID, col(11), col(8), 0.5 - 0.5 / LIFT, 0.5 + 0.5 / LIFT, a_sg)
     a_un = fun(ID, col(12), col(9), 2.0 - 2.0 / LIFT, 2.0 + 2.0 / LIFT)
     un16, un4x4, tau4 = col(11), col(12), col(13)
@@ -247,43 +252,39 @@ def rank_program(g, core, T, topo):
     ts(T.oq[:], i0, 0.0, q_, A.mult, A.add)
     tb = tt(mw[:, 0:16], ms[:, 0:16], ms[:, 32:48], A.max, tb)
     a_m16 = act(m16, mw[:, 0:16].indirect(T.oq[:, 0:12]), None, tb)
-    t3 = ts(yw[:, 4:7], yw[:, 0:3], col(14), -0.4375, A.mult, A.add, t3, a_my)
-    v_uo = vcopy(T.uo[:], ci[:, 32:40], g_ci)
     ts(ms[:, 16:20], im[:, 0:4], r_, LIFT, A.is_equal, A.mult)
-    t3 = vcopy(pi[:, 10:13], yw[:, 4:7], t3)
+    t3 = ts(yw[:, 4:7], yw[:, 0:3], col(14), -0.4375, A.mult, A.add, t3, a_my)
     tb = ts(ms[:, 48:52], im[:, 0:4], r_, None, A.is_ge, None)
-    ts(T.ot[:], i0, 0.0, tau, A.mult, A.add)
+    t = ts(yl[:, 0:18], ci[:, 40:58], col(19), q_, A.mult, A.add, td)
+    t3 = vcopy(pi[:, 10:13], yw[:, 4:7], t3)
     for d in range(2):
         ts(mark[:, 2 << d:4 << d], im[:, 40 - (2 << d):40], col(d), 2.0, A.is_equal, A.mult, g_dn)
-    t = ts(yl[:, 0:18], ci[:, 40:58], col(19), q_, A.mult, A.add, td)
-    v_ot = tt(mw[:, 16:20], ms[:, 16:20], ms[:, 48:52], A.max, tb)
-    a_m4 = act(m4, mw[:, 16:20].indirect(T.ot[:, 0:8]), None, v_ot)
-    for d in range(2, 4):
-        tb = ts(mark[:, 2 << d:4 << d], im[:, 40 - (2 << d):40], col(d), 2.0, A.is_equal, A.mult)
     v_yl = vcopy(yl[:, 4:18:6], pi[:, 10:13], t3, t)
-    v_uq = quant(T.uq[:, 0:128], T.us[:, 0:128], T.ut[:, 0:512], t_u)
+    for d in range(2, 4):
+        tm = ts(mark[:, 2 << d:4 << d], im[:, 40 - (2 << d):40], col(d), 2.0, A.is_equal, A.mult)
     v_k16 = vcopy(T.k16_0[:], T.kli[:], t_kl)
-    v_sg = tt(mark[:, 32:48], mark[:, 1:32:2], mark[:, 0:32:2], A.subtract, tb)
-    sgn = mark[:, 32:48]
+    v_uq = quant(T.uq[:, 0:128], T.us[:, 0:128], T.ut[:, 0:512], t_u)
     v_fi = ts(fi[:, 6:18], yl[:, 6:18], -1.0, 127.0, A.mult, A.add, v_yl)
-    a_y2 = fun(ID, yc[:, 0:64], T.one[:].indirect(yl[:, 0:4]), 2.0, -2.0, v_yl, g_one)
+    v_sg = tt(mark[:, 32:48], mark[:, 1:32:2], mark[:, 0:32:2], A.subtract, tm)
+    sgn = mark[:, 32:48]
+    v_tk = fun(SG, T.tk[:, 0:80], T.tr[:], 1.0, 0.0, g_tr)
+    a_yc = fun(ID, yc[:, 64:128], T.one[:].indirect(yl[:, 0:4]), 1.0, -1.0, v_yl, g_one)
     a_n = act(half(0, 0), T.one[:].indirect(T.k16_0[:, 0:8]), None, v_k16)
-    a_yc = fun(ID, yc[:, 64:128], T.one[:].indirect(yl[:, 0:4]), 1.0, -1.0)
+    a_up = act(T.ups[:, 0:128], T.us[:, 0:128].indirect(T.uo[:, 0:8]), None, v_uq, v_uo)
     act(fr(0, "kt", 0, 96), half(0, 0).indirect(yl[:, 0:6]), None, a_n)
     a_kt = act(fr(0, "kt", 96, 192), half(0, 0).indirect(fi[:, 6:12]), None, v_fi)
-    a_wa = fun(F.Relu, wa[:, 64:128], sgn.indirect(T.oq[:, 0:4]), 1.0, 0.0, v_sg)
+    fun(F.Relu, wa[:, 64:128], sgn.indirect(T.oq[:, 0:4]), 1.0, 0.0, v_sg)
+    v_up = vcopy(T.up[:, 0:128].bitcast(dt.uint32), T.uq[:, 0:128].bitcast(dt.uint32).indirect(T.uo[:, 0:8]), v_uq, v_uo)
+    tw = tt(wt[:, 96:160], sgn.indirect(T.oq[:, 0:4]), yc[:, 64:128], A.mult, v_w0, a_yc, v_sg)
+    ts(T.ot[:], i0, 0.0, tau, A.mult, A.add)
+    v_ot = tt(mw[:, 16:20], ms[:, 16:20], ms[:, 48:52], A.max, tb)
+    a_wa = act(wa[:, 0:64], wt[:, 96:160], 2.0, tw)
+    a_m4 = act(m4, mw[:, 16:20].indirect(T.ot[:, 0:8]), None, v_ot)
     a_n = act(half(0, 1), T.one[:].indirect(T.k16_0[:, 8:16]), None)
-    v_tk = fun(SG, T.tk[:], T.tr[:], 1.0, 0.0, g_tr)
     tab["un"] = fun(ID, col(20), col(8), 0.125 - 0.125 / LIFT, 0.125 + 0.125 / LIFT)
-    vcopy(T.up[:, 0:128].bitcast(dt.uint32), T.uq[:, 0:128].bitcast(dt.uint32).indirect(T.uo[:, 0:8]), v_uq, v_uo)
-    v_up = vcopy(T.ups[:, 0:128], T.us[:, 0:128].indirect(T.uo[:, 0:8]))
-    tw = tt(wa[:, 0:64], sgn.indirect(T.oq[:, 0:4]), yc[:, 0:64], A.mult, a_y2, v_sg)
-    tt(wt[:, 96:160], sgn.indirect(T.oq[:, 0:4]), yc[:, 64:128], A.mult, v_w0, a_yc)
     v_q1 = quant(T.xq0[:, 0:128], T.xs0[:, 0:128], T.x0[:, 0:512], t_x)
     v_q2 = quant(T.xq0[:, 128:256], T.xs0[:, 128:256], T.x0[:, 512:1024])
-    t = scan(fr(0, "st", 0, 192), m16, fr(0, "kt", 0, 192), a_kt, a_m16)
-    v_wt = tt(wt[:, 0:64], wa[:, 0:64], wa[:, 64:128], A.add, tw, a_wa)
-    v_tl = ts(wr(0, "tl", 0, 12), fr(0, "st", 15, 192, 16), un16, 1.0, A.mult, A.subtract, t, a_un)
+    tab["tl"] = scan(fr(0, "st", 0, 192), m16, fr(0, "kt", 0, 192), a_kt, a_m16)
 
     def four(r, h, *toks):
         return scan(fr(r, "n4", 128 * h, 128 * h + 128), m4, half(r, h), *toks)
@@ -291,18 +292,29 @@ def rank_program(g, core, T, topo):
     def four_end(r, t):
         return ts(wr(r, "k4"), fr(r, "n4", 3, 256, 4), un4x4, tau4, A.mult, A.add, t)
 
+    g_w2 = on_top(2)
     wait("g", v_k16)
     rk = [remote(0, T.kin0[:], T.k16_0[:], "rk0"), 0, 0]
-    g_w2 = on_top(2)
     tab["x"] = None
+    iota(d1[:, 2:192:6], [[0, 32]], 0, 0)
+    for at, c in ((0, 0), (2, -1), (3, 1)):
+        g_d = iota(d0[:, at:192:6], [[0, 32]], c, 0)
     g_e = []
-    wait("g", iota(T.ones[:], [[0, 512]], 1, 0))
+    wait("g", iota(T.ones[:], [[0, 514]], 1, 0))
+    for b in range(2):
+        g_e.append(fin("g", g.affine_select(T.et[:, 528 * b:528 * b + 514], T.ones[:], [[-1, 514]], A.is_equal, 0.0, b + 2, 4)))
+    iota(T.pf[:, 80:96], [[1, 16]], 81, 0)
     for b in range(4):
-        g_e.append(fin("g", g.affine_select(T.et[:, 512 * b:512 * b + 512], T.ones[:], [[-1, 512]], A.is_equal, 0.0, b, 4)))
+        iota(T.pf[:, 20 * b:20 * b + 4], [[1, 4]], 65 + 4 * b, 0)
+        g_pf = iota(T.pf[:, 20 * b + 4:20 * b + 20], [[1, 16]], 1 + 16 * b, 0)
 
     def partner_list(r, *toks):
-        f1 = act(fr(r, "kp"), T.one[:].indirect(T["kin%d" % r][:, 0:16]), None, ("rk%d" % r, rk[r]))
-        f2 = act(fr(r, "kk", 0, 256), fr(r, "kp").indirect(T["k16_%d" % r][:, 0:16]), None, f1, *toks)
+        return act(fr(r, "kp"), T.one[:].indirect(T["kin%d" % r][:, 0:16]), None, ("rk%d" % r, rk[r]))
+
+    def read_by_own(r, f1, *toks):
+        return act(fr(r, "kk", 0, 256), fr(r, "kp").indirect(T["k16_%d" % r][:, 0:16]), None, f1, *toks)
+
+    def exchanged(r, f2):
         act(fr(r, "kk", 256, 512, 2), fr(r, "kk", 1, 256, 2), None, f2)
         return act(fr(r, "kk", 257, 512, 2), fr(r, "kk", 0, 256, 2), None)
 
@@ -318,102 +330,151 @@ def rank_program(g, core, T, topo):
     for r in range(ROUNDS):
         X, xk, Z, H, B = T["x%d" % r], T["xk%d" % r], T["z%d" % r], T["h%d" % r], T["b%d" % r]
         last = r == ROUNDS - 1
+        two = r > 0
         k16 = T["k16_%d" % r]
         tg, tsc, sg = fr(r, "tg"), fr(r, "ts"), fr(r, "sg")
 
         def tree(a, *toks):
-            return tt(tg[:, 96 * a:96 * a + 80], sg.indirect(wr(r, "tl", 6 * a, 6 * a + 5)), wt[:, 96 * a:96 * a + 80], A.mult, *toks)
+            return tt(tg[:, 96 * a:96 * a + 80], sg.indirect(wr(r, "tl", 6 * a, 6 * a + 5)), (T.w2 if r else wt)[:, 96 * a:96 * a + 80], A.mult, *toks)
 
         def climb(a, *toks):
-            return scan(tsc[:, 96 * a:96 * a + 80], T.tk[:, 0:80], tg[:, 96 * a:96 * a + 80], *toks)
+            return scan(tsc[:, 96 * a:96 * a + 80], T.tk[:, 80:160] if r else T.tk[:, 0:80], tg[:, 96 * a:96 * a + 80], *toks)
 
-        def top(a, *toks):
-            return tt(fr(r, "tm", 4 * a, 4 * a + 4), tsc[:, 96 * a + 15:96 * a + 64:16], tsc[:, 96 * a + 67:96 * a + 80:4], A.max, *toks)
+        def top(a, t):
+            if r:
+                return t
+            return tt(fr(r, "tm", 4 * a, 4 * a + 4), tsc[:, 96 * a + 15:96 * a + 64:16], tsc[:, 96 * a + 67:96 * a + 80:4], A.max, t)
 
-        def step(a, *toks):
-            return vcopy(wr(r, "bl", 4 * a, 4 * a + 4), fr(r, "tm", 4 * a, 4 * a + 4), *toks)
+        def step(a, t):
+            return vcopy(wr(r, "bl", 4 * a, 4 * a + 4), tsc[:, 96 * a + 19:96 * a + 80:20] if r else fr(r, "tm", 4 * a, 4 * a + 4), t)
 
         def wrap(out, src, *toks):
             return ts(out, src, col(20), 0.2, A.mult, A.subtract, *toks)
 
         for h in range(2):
-            p = scores(T.up, T.ups, r, h, (v_q1, v_q2)[h], v_up)
+            p = scores(T.up, T.ups, r, h, (v_q1, v_q2)[h], v_up, a_up)
             s = ts(sg[:, 128 * h:128 * h + 128], psv(4 + h, 0, 128), 0.0, 0.5, A.is_le, A.subtract, p)
             bankuse[4 + h] = [s]
+            if h == 0:
+                v_tl = ts(wr(r, "tl", 0, 12), fr(r, "st", 15, 192, 16), un16, 1.0, A.mult, A.subtract, tab["tl"], a_un)
         if r == 0:
+            v_wt = tt(wt[:, 0:64], wa[:, 0:64], wa[:, 64:128], A.add, a_wa)
+        else:
+            v_k16 = ts(k16[:], fr(r, "n16", 15, 256, 16), un16, 1.0, A.mult, A.subtract, tab["n16"])
+            wait("g", v_k16)
+            rk[r] = remote(r, T["kin%d" % r][:], k16[:], "rk%d" % r)
+            t3 = scan(fr(r, "st", 192, 288), m16[:, 0:96], fr(r, "k2", 192, 288))
+        if r == 0:
+            tg_ = tree(1, s, v_tl, g_wt)
+            tb_ = tree(0, v_wt)
             four(0, 0, a_m4)
             t4 = four(0, 1, a_n)
-        tb_ = tree(0, s, v_tl, v_wt, g_wt)
-        tg_ = tree(1)
-        if r == 0:
+            tg_ = climb(1, tg_, v_tk)
+            tb_ = climb(0, tb_)
             v_k4 = four_end(0, t4)
-        tb_ = climb(0, tb_, v_tk)
-        tg_ = climb(1, tg_)
-        tb_ = top(0, tb_)
-        tg_ = top(1, tg_)
+            tg_ = top(1, tg_)
+            tb_ = top(0, tb_)
+        else:
+            tb_ = tree(0, s, v_tl, v_wt)
+            tg_ = tree(1)
+            tb_ = climb(0, tb_, v_tk)
+            tab["x"] = ts(wr(r, "tl", 12, 18), fr(r, "st", 192 + 15, 288, 16), un16, 1.0, A.mult, A.subtract, t3)
+            tg_ = climb(1, tg_)
         tb_ = step(0, tb_)
         if r == 0:
             a_kt = act(fr(0, "kt", 192, 288), half(0, 0).indirect(fi[:, 12:18]), None)
             ta = fun(F.Abs, col(5), tau, 1.0, -2.0)
-            fun(ID, col(21), col(9), 0.5 - 0.5 / LIFT, 0.5 + 0.5 / LIFT)
-            fun(ID, col(22), col(9), 1.0 - 1.0 / LIFT, 1.0 + 1.0 / LIFT)
             fun(ID, col(24), r_, 2.0, -1.0)
             tb = fun(ID, col(25), r_, 4.0, 1.0)
-            ta = fun(F.Abs, col(6), col(5), 256.0, -256.0, ta)
+            fun(ID, col(21), col(9), 0.5 - 0.5 / LIFT, 0.5 + 0.5 / LIFT)
+            tab["a"] = fun(F.Abs, col(6), col(5), 256.0, -256.0, ta)
+            fun(ID, col(22), col(9), 1.0 - 1.0 / LIFT, 1.0 + 1.0 / LIFT)
             fun(ID, T.cc[:, 0:32], ci[:, 0:32], 1.0, col(24), g_c8, tb)
             fun(ID, T.cc[:, 32:64], ci[:, 0:32], 2.0, col(25))
-            tab["cc"] = fun(ID, col(23), col(6), -1.0, 256.0, ta)
-        a_xk = act(xk[:], X[:].indirect(wr(r, "k4")), 0.5, v_k4, *x_done)
+            put("ra0", "c", fun, ID, col(27), col(0), 4.0, tau)
+            put("ra0", "cc", fun, ID, col(23), col(6), -1.0, 256.0, "a")
         xk2 = T["xj%d" % r]
-        wait("y", a_xk)
-        d_xk = dma("y", "dxk", 16 * (r + 1), xk2[:], xk[:])
+
+        def halves(a, b):
+            tab["xk"] = act(xk[:, a:b], X[:].indirect(wr(r, "k4", a // 16, b // 16)), 0.5, v_k4, *x_done)
+            if b == 1024:
+                wait("y", tab["xk"])
+                tab["xj"] = dma("y", "dxk", 16 * (r + 1), xk2[:, 0:1024], xk[:])
+        halves(0, 1024 if r else 896)
 
         def bits():
             t = fun(ID, fr(r, "f"), sg.indirect(k16[:, 0:8]), -1.0, 1.5, s, v_k16)
-            tab["f"] = fun(ID, fr(r, "f", 127, 128), q_, 0.0, 2.0, t)
+            if r:
+                tab["f"] = fun(ID, fr(r, "f", 127, 128), q_, 0.0, 2.0, t)
+            else:
+                put("ra1", "f", fun, ID, fr(r, "f", 127, 128), q_, 0.0, 2.0, t)
 
         def back():
             tab["x"] = act(fr(r, "r0", 64, 128), fr(r, "t1").indirect(wr(r, "bl", 8, 12)), None, tab["x"])
 
         def place():
             tab["f1"] = act(fr(r, "f1"), fr(r, "sf", 3, 128, 4), col(21), tab["sf"])
-            tab["dd"] = fun(ID, d0[:, 7:256:8], fr(r, "sf", 3, 128, 4), col(22), -3.0, tab["d0"])
+            tab["dd"] = fun(ID, d0[:, 5:192:6], fr(r, "sf", 3, 128, 4), col(22), -3.0)
+
+        def other():
+            tab["u"] = act(fr(r, "u"), fr(r, "r0").indirect(wr(r, "sp")), None, tab["x"], tab["sp"])
+
+        def none_lower():
+            tab["g"] = act(d0[:, 1:192:3], fr(r, "g"), -1.0, tab["g"])
+
+        def both(a, b):
+            return tt(xk2[:, 1024 + a:1024 + b], xk[:, 4 * AHEAD:512].indirect(T.zl[:, a // 16:b // 16]), xk[:, 8 * AHEAD + a:8 * AHEAD + b],
+                      A.add, tab["xk"], tab["zl"])
         third = (("x", tree, 2, "x"), ("x", climb, 2, "x"), ("x", top, 2, "x"), ("x", step, 2, "x"))
-        wrap3 = (("x", scan, fr(r, "s0", 64, 128), m16[:, 0:64], fr(r, "r0", 64, 128), "x"),
-                 ("x", wrap, wr(r, "l0", 4, 8), fr(r, "s0", 64 + 15, 128, 16), "x"))
+        behind = (("sp", tt, fr(r, "sp"), sg.indirect(k16[:, 0:4]), T.one[:, 0:128:2], A.add),
+                  ("sp", scan, fr(r, "ss"), m16[:, 0:64], fr(r, "sp"), "sp"),
+                  ("sp", ts, wr(r, "sp"), fr(r, "ss", 15, 64, 16), un16, 0.5, A.mult, A.subtract, "sp"))
+        wrapu = (("u", scan, fr(r, "su"), m16[:, 0:64], fr(r, "u"), "u"), ("u", wrap, wr(r, "u"), fr(r, "su", 15, 64, 16), "u"))
+        lower = ("g", tt, fr(r, "g"), fr(r, "m7"), T.ke[:], A.is_ge, "ke", "m")
         bit4 = ("sf", scan, fr(r, "sf"), m4, fr(r, "f"), "f")
-        base4 = ("b", tt, d1[:, 7:256:8], fr(r, "f1"), T.cc[:, 0:32], A.add, "f1", "cc")
+        base4 = ("b", tt, d1[:, 5:192:6], fr(r, "f1"), T.cc[:, 0:32], A.add, "f1", "cc")
         if r == 0:
             put("t1", "z", ts, yc[:, 128:192], T.one[:].indirect(yl[:, 12:16]), 1.0, None, A.subtract, None)
             put("r0", "z", tt, wt[:, 192:256], sgn.indirect(T.oq[:, 0:4]), yc[:, 128:192], A.mult, "z", g_w2)
             put("s0", "x", scan, fr(0, "st", 192, 288), m16[:, 0:96], fr(0, "kt", 192, 288), a_kt)
             put("l0", "eq", ts, mw[:, 32:36], im[:, 1:5], r_, None, A.is_equal, None)
             put("l0", "x", ts, wr(0, "tl", 12, 18), fr(0, "st", 192 + 15, 288, 16), un16, 1.0, A.mult, A.subtract, "x")
-            for name, call in zip(("m1", "m2", "m3", "s1"), third):
+            for name, call in zip(("a0", "l1", "a1", "l2"), third):
                 put(name, *call)
-            put("m2", "d1", fill, d1[:, 3:256:8], 0.0)
-            put("m3", "d0", fill, d0[:], -1.0)
-            put("s1", "d0", fill, d0[:, 0:256:8], 0.0, "d0")
-            put("m4", "kf", tt, T.kf[:], mw[:, 32:36].indirect(T.ot[:, 0:8]), T.cd[:], A.mult, "eq")
-            put("m5", "kf", fill, T.kf[:, 0:1], 0.0, "kf")
-            put("m6", "ke", tt, T.ke[:], T.kf[:, 0:128:2], T.kf[:, 1:128:2], A.add, "kf")
-            side["c2"] = [back, bits]
-            put("m7", *wrap3[0])
-            put("m8", *wrap3[1])
-            put("m8", *bit4)
-            side["m8"] += [place, lambda: tab.update(kk=partner_list(0))]
-            put("e", *base4)
-            for b, name in enumerate(("m9", "z2", "h1", "h2")):
-                put(name, "e", quant, T.eq[:, 128 * b:128 * b + 128], T.es[:, 128 * b:128 * b + 128], T.et[:, 512 * b:512 * b + 512], g_e[b])
+            for name, call in zip(("l1", "a1", "l2"), behind):
+                put(name, *call)
+            put("l2", *bit4)
+            put("a2", "kf", tt, T.kf[:], mw[:, 32:36].indirect(T.ot[:, 0:8]), T.cd[:], A.mult, "eq")
+            put("l3", "kf", fill, T.kf[:, 0:1], 0.0, "kf")
+            put("a3", *wrapu[0])
+            put("a3", "ke", tt, T.ke[:], T.kf[:, 0:128:2], T.kf[:, 1:128:2], A.add, "kf")
+            put("l4", *wrapu[1])
+            put("m9", *base4)
+            side.update(rb0=[bits], rb1=[lambda: halves(896, 1024)], ra2=[back], rb2=[other, place])
+            for b, name in zip((0, 2, 1, 3), ("f", "z2", "h1", "h2")):
+                at = 528 * (b % 2) + 2 - b // 2 * 2
+                put(name, "e", quant, T.eq[:, 128 * b:128 * b + 128], T.es[:, 128 * b:128 * b + 128], T.et[:, at:at + 512], g_e[b % 2])
+            put("z1", "zl", ts, T.zl[:], ci[:, 0:32], col(27), None, A.add, None)
+            put("z3", "fi", ts, fi[:, 24:30], yl[:, 0:6], 4.0, None, A.mult, None)
+            put("z3", "fi", ts, fi[:, 30:42], fi[:, 6:18], 4.0, None, A.mult, None)
         else:
             bits()
-            for name, call in zip(("t1", "r0", "s0", "l0"), third):
+            for name, call in zip(("t1", "r0", "s0", "s0"), third):
                 put(name, *call)
-            put("m1", *bit4)
-            side["c1"], side["c2"] = [back], [place]
-            put("m4", *wrap3[0])
-            put("m5", *wrap3[1])
-            put("m7", *base4)
+            for name, call in zip(("l0", "a0", "l1"), behind):
+                put(name, *call)
+            put("a0", *bit4)
+            put("l2", *wrapu[0])
+            put("l3", *base4)
+            put("l3", *wrapu[1])
+            at = 0
+            for name, n in (("l1", 32), ("a1", 96), ("l2", 64), ("a2", 96), ("a3", 96)):
+                put(name, "zc", both, at, at + n)
+                at += n
+            side.update(ra0=[back], ra1=[other], rb1=[place])
+        put("ra3", "kk", partner_list, r)
+        put("l4", *lower)
+        side["l4"] += [none_lower, lambda: tab.update(kk=read_by_own(r, tab["kk"], v_k16))]
         tg_ = step(1, tg_)
         t = vcopy(fr(r, "t1"), T.cd[:].indirect(wr(r, "bl", 0, 4)), tb_, g_cd)
         gap("t1")
@@ -426,35 +487,38 @@ def rank_program(g, core, T, topo):
         gap("l0")
 
         a_r, v_m = v_r, v_r
-        rw, mn = fr(r, "r0", 0, 64), fr(r, "r0", 0, 64)
-        for lv in range(3):
-            off = wr(r, "l%d" % lv, 0, 4)
-            base = mn
-            for k in range(3):
-                i = 3 * lv + k + 1
-                if lv < 2:
-                    a_r = act(fr(r, "r%d" % i), rw.indirect(off), None, v_l, a_r)
-                    rw = fr(r, "r%d" % i)
-                v_m = tt(fr(r, "m%d" % i), mn.indirect(off), base if k else fr(r, "c%d" % lv), A.min, v_l, v_m, v_cp)
-                mn = fr(r, "m%d" % i)
-                gap("m%d" % i)
-            if lv == 2:
-                break
-            t = scan(fr(r, "s%d" % (lv + 1)), m16[:, 0:64], rw, a_r)
-            v_cp = act(fr(r, "c%d" % (lv + 1)), mn, None, v_m)
-            gap("s%d" % (lv + 1))
-            gap("c%d" % (lv + 1))
+        rw = mn = fr(r, "r0", 0, 64)
+        base = (fr(r, "c0"), mn)
+        for lv in range(4):
+            off = wr(r, "l%d" % lv)
+            ra, rb, ma, mb = (fr(r, "%s%d" % (n, 2 * lv + i)) for n in "rm" for i in (1, 2))
+            a_ra = act(ra, rw.indirect(off), None, v_l, a_r)
+            gap("ra%d" % lv)
+            if lv < 3:
+                a_r = act(rb, ra.indirect(off), None, a_ra)
+                gap("rb%d" % lv)
+            tab["m"] = v_m = tt(ma, mn.indirect(off), base[0], A.min, v_l, v_m, v_cp)
+            gap("a%d" % lv)
+            t = scan(fr(r, "s%d" % (lv + 1)), m16[:, 0:64], ra, a_ra)
+            v_m = tt(mb, ma.indirect(off), base[1], A.min, v_m)
             v_l = wrap(wr(r, "l%d" % (lv + 1)), fr(r, "s%d" % (lv + 1), 15, 64, 16), t)
-        tt(d1[:, 0:256:2], mn.indirect(wr(r, "l0")), T.kf[:], A.is_equal, v_m, tab["ke"], tab["x"])
-        t = tt(d1[:, 1:256:4], mn, T.ke[:], A.is_equal)
-        gap("e")
-        t = chain(fr(r, "so"), d0[:], d1[:], t, tab["dd"], tab["b"])
-        tc = fr(r, "so", 7, 256, 8)
+            gap("l%d" % (lv + 1))
+            rw, mn, base = rb, mb, (ma, ma)
+        off = wr(r, "l4")
+        v_m = tt(fr(r, "m9"), mn.indirect(off), base[0], A.min, v_l, v_m)
+        gap("m9")
+        tt(d1[:, 0:192:3], mn.indirect(off), T.ke[:], A.is_equal)
+        t = tt(d1[:, 1:192:3], fr(r, "m9").indirect(wr(r, "u")), T.ke[:], A.is_equal, v_m, tab["u"])
+        gap("f")
+        t = chain(fr(r, "so", 0, 192), d0[:, 0:192], d1[:, 0:192], t, tab["dd"], tab["b"], tab["g"], g_d)
+        tc = fr(r, "so", 5, 192, 6)
         clo = ts(wr(r, "lo"), tc, 4.0, tau, A.mult, A.add, t)
         ctn = ts(wr(r, "tn"), tc, col(23), None, A.add, None)
         th = tt(fr(r, "hi"), T.cc[:, 32:64], tc, A.subtract)
-        if r:
-            a_n = act(fr(r + 1, "nn"), fr(r, "kk").indirect(wr(r, "tn")), None, ctn, tab["kk"])
+
+        def new_list():
+            return act(fr(r + 1, "nn"), fr(r, "kk").indirect(wr(r, "tn")), None, ctn, tab["kk"])
+
 
         def layer(qz, qzs, banks, tok):
             out = []
@@ -470,67 +534,66 @@ def rank_program(g, core, T, topo):
 
         def nm(s):
             return T["%s_%d" % (s, r)]
-        z1 = tt(Z[:, 0:512], xk[:].indirect(wr(r, "lo")), xk2[:, 0:512], A.add, clo, a_xk, d_xk)
+        pl = T["xs%d" % r]
+        n1 = 4 * AHEAD if two else 512
+        z0 = act(Z[:, n1:512], xk2[:, 1024 - 8 * AHEAD:2048 - 8 * AHEAD].indirect(wr(r, "lo", n1 // 16, 32)), None, clo, tab["zc"], tab["xj"]) if two else None
+        tab["kk"] = exchanged(r, tab["kk"])
+        z1 = tt(Z[:, 0:n1], xk[:].indirect(wr(r, "lo", 0, n1 // 16)), xk2[:, 0:n1], A.add, clo, tab["xk"], tab["xj"])
         chi = ts(wr(r, "hi"), fr(r, "hi"), 4.0, tau, A.mult, A.add, th)
-        tq = quant(nm("qz")[:, 0:128], nm("qzs")[:, 0:128], Z[:, 0:512], z1)
-        p1 = layer(nm("qz")[:, 0:128], nm("qzs")[:, 0:128], (0, 1, 2, 3), tq)
-        h1 = [scaled("a", H[:, b:512:4], b, 0, p1[b]) for b in range(3)]
-        z2 = tt(Z[:, 512:768], xk[:].indirect(wr(r, "hi", 0, 16)), xk2[:, 512:768], A.add, chi)
-        gap("z2")
-        tq = quant(nm("qz")[:, 128:256], nm("qzs")[:, 128:256], Z[:, 256:768], z2)
-        p2 = layer(nm("qz")[:, 128:256], nm("qzs")[:, 128:256], (4, 5, 6, 7), tq)
+        gap("z1")
+        tq = quant(nm("qz")[:, 0:128], pl[:, 256:384], Z[:, 0:512], z0, z1)
+        p1 = layer(nm("qz")[:, 0:128], pl[:, 256:384], (0, 1, 2, 3), tq)
+        if two:
+            z2 = tt(Z[:, 512:768], xk[:].indirect(wr(r, "hi", 0, 16)), xk2[:, 512:768], A.add, chi)
+            h1 = [scaled("ava"[b], H[:, b:512:4], b, 0, p1[b]) for b in range(3)]
+        else:
+            h1 = [scaled("a", H[:, b:512:4], b, 0, p1[b]) for b in range(3)]
+            z2 = tt(Z[:, 512:768], xk[:].indirect(wr(r, "hi", 0, 16)), xk2[:, 512:768], A.add, chi)
+            gap("z2")
+        tq = quant(nm("qz")[:, 128:256], pl[:, 640:768], Z[:, 256:768], z2)
+        p2 = layer(nm("qz")[:, 128:256], pl[:, 640:768], (4, 5, 6, 7), tq)
+
+        def rest(a, b):
+            return tt(Z[:, a:b], xk[:].indirect(wr(r, "hi", a // 16 - 32, b // 16 - 32)), xk2[:, a:b], A.add)
         h1.append(scaled("v", H[:, 3:512:4], 3, 0, p1[3]))
         gap("h1")
-        tq1 = quant(nm("qh")[:, 0:128], nm("qhs")[:, 0:128], H[:, 0:512], *h1)
+        tq1 = quant(nm("qh")[:, 0:128], pl[:, 384:512], H[:, 0:512], *h1)
         h2 = [scaled("aavv"[b], H[:, 512 + b:768:4], 4 + b, 64, p2[b]) for b in range(4)]
         gap("h2")
-        tq2 = quant(nm("qh")[:, 128:256], nm("qhs")[:, 128:256], H[:, 256:768], *h2)
-        if r == 0:
-            a_n = act(fr(r + 1, "nn"), fr(r, "kk").indirect(wr(r, "tn")), None, ctn, tab["kk"])
+        if r:
+            rest(768, 864)
+        tq2 = quant(nm("qh")[:, 128:256], pl[:, 512:640], H[:, 256:768], *h2)
+        a_n = new_list()
 
         wait("g", tq1)
         na = remote(r, nm("cin")[:, 0:128].bitcast(dt.uint8), nm("qh")[:, 0:128].bitcast(dt.uint8), "ra%d" % r)
-        na += remote(r, nm("cins")[:, 0:128], nm("qhs")[:, 0:128], "ra%d" % r)
+        na += remote(r, nm("la")[:, 0:128], pl[:, 384:512], "ra%d" % r)
         wait("g", tq2)
         nb = remote(r, nm("cin")[:, 128:192].bitcast(dt.uint8), nm("qh")[:, 192:256].bitcast(dt.uint8), "rb%d" % r)
-        nb += remote(r, nm("cins")[:, 128:192], nm("qhs")[:, 192:256], "rb%d" % r)
+        nb += remote(r, nm("la")[:, 128:192], pl[:, 576:640], "rb%d" % r)
 
-        z3 = tt(Z[:, 768:1024], xk[:].indirect(wr(r, "hi", 16, 32)), xk2[:, 768:1024], A.add)
-        if not last:
-            if r == 0:
-                ts(fi[:, 24:30], yl[:, 0:6], 4.0, None, A.mult, None)
-                v_fi = ts(fi[:, 30:42], fi[:, 6:18], 4.0, None, A.mult, None)
-            else:
-                scan(fr(r + 1, "n16", 0, 128), m16[:, 0:128], half(r + 1, 0), a_n)
-                s16 = scan(fr(r + 1, "n16", 128, 256), m16[:, 0:128], half(r + 1, 1))
-            a_kt = act(fr(r + 1, "kt"), fr(r + 1, "nn").indirect(fi[:, 24:42]), None, a_n, v_fi)
-        tq = quant(nm("qz")[:, 256:384], nm("qzs")[:, 256:384], Z[:, 512:1024], z3)
-        p = layer(nm("qz")[:, 256:384], nm("qzs")[:, 256:384], (0, 1, 2, 3), tq)
-        a_b = [scaled("a", B[:, 768 + b:1024:4], b, 64, p[b]) for b in range(4)][3]
+        z3 = rest(864 if r else 768, 1024)
+        gap("z3")
+        tq = quant(nm("qz")[:, 256:384], pl[:, 768:896], Z[:, 512:1024], z3)
+        p = layer(nm("qz")[:, 256:384], pl[:, 768:896], (0, 1, 2, 3), tq)
         if r == 0:
-            scan(fr(r + 1, "n16", 0, 128), m16[:, 0:128], half(r + 1, 0), a_n)
-            s16 = scan(fr(r + 1, "n16", 128, 256), m16[:, 0:128], half(r + 1, 1))
+            t = scan(T.pf[:, 96:192], m16[:, 0:96], T.pf[:, 0:96], g_pf)
+            t2 = fill(T.tk[:, 80:160], 1.0)
         four(r + 1, 0, a_n)
         t4 = four(r + 1, 1)
-        if not last:
-            v_k16 = ts(T["k16_%d" % (r + 1)][:], fr(r + 1, "n16", 15, 256, 16), un16, 1.0, A.mult, A.subtract, s16)
-            wait("g", v_k16)
-            rk[r + 1] = remote(r + 1, T["kin%d" % (r + 1)][:], T["k16_%d" % (r + 1)][:], "rk%d" % (r + 1))
-            scan(fr(r + 1, "st", 0, 192), m16, fr(r + 1, "kt", 0, 192), a_kt)
-            t = scan(fr(r + 1, "st", 192, 288), m16[:, 0:96], fr(r + 1, "kt", 192, 288))
+        if r == 0:
+            v_pf = ts(T.pl[:, 0:6], T.pf[:, 111:192:16], un16, 1.0, A.mult, A.subtract, t)
+            v_tk = fill(T.tk[:, 80:160:20], 0.0, t2)
+        bt = [scaled("av"[b], B[:, 768 + b:1024:4], b, 64, p[b]) for b in range(2)]
         v_k4 = four_end(r + 1, t4)
+        bt += [scaled("av"[b - 2], B[:, 768 + b:1024:4], b, 64, p[b]) for b in range(2, 4)]
         if r == 1:
             v_v = quant(T.vq[:, 0:128], T.vqs[:, 0:128], T.vt[:], t_v)
-        if not last:
-            v_tl = ts(wr(r + 1, "tl"), fr(r + 1, "st", 15, 288, 16), un16, 1.0, A.mult, A.subtract, t)
-        else:
-            ts(T.kyf[:, 0:128], half(r + 1, 0), 1.0, None, A.subtract, None)
-            v_ky = ts(T.kyf[:, 128:256], half(r + 1, 1), 1.0, None, A.subtract, None)
 
-        cin, cins = nm("cin"), nm("cins")
-        p, bt = [], []
+        cin = nm("cin")
+        p = []
         for b in range(4):
-            p.append(mm(4 + b, 128, T.eq[:, 128 * b:128 * b + 128], T.es[:, 128 * b:128 * b + 128], cin[:, 0:128], cins[:, 0:128],
+            p.append(mm(4 + b, 128, T.eq[:, 128 * b:128 * b + 128], T.es[:, 128 * b:128 * b + 128], cin[:, 0:128], nm("la")[:, 0:128],
                         ("ra%d" % r, na), tab["e"], *bankuse[4 + b]))
         for b in range(4):
             o, i = B[:, b:512:4], psv(4 + b, 0, 128)
@@ -539,7 +602,7 @@ def rank_program(g, core, T, topo):
             bt.append(t)
         p = []
         for b in range(4):
-            p.append(mm(b, 128, T.eq[:, 128 * b:128 * b + 128], T.es[:, 128 * b:128 * b + 128], cin[:, 64:192], cins[:, 64:192],
+            p.append(mm(b, 128, T.eq[:, 128 * b:128 * b + 128], T.es[:, 128 * b:128 * b + 128], cin[:, 64:192], nm("la")[:, 64:192],
                         ("rb%d" % r, nb), *bankuse[b]))
         for b in range(4):
             o, i = B[:, 512 + b:768:4], psv(b, 64, 128)
@@ -549,13 +612,31 @@ def rank_program(g, core, T, topo):
 
         nx = T["x%d" % (r + 1)]
         nq, ns = T["xq%d" % (r + 1)], T["xs%d" % (r + 1)]
-        g1 = tt(nx[:, 0:512], B[:].indirect(wr(r + 1, "k4", 0, 32)), X[:, 0:512], A.add, v_k4, a_b, *bt)
-        g2 = tt(nx[:, 512:1024], B[:].indirect(wr(r + 1, "k4", 32, 64)), X[:, 512:1024], A.add)
+        g1 = tt(nx[:, 0:512], B[:].indirect(wr(r + 1, "k4", 0, 32)), X[:, 0:512], A.add, v_k4, *bt)
+        if last:
+            tt(nx[:, 512:640], B[:].indirect(wr(r + 1, "k4", 32, 40)), X[:, 512:640], A.add)
+            v_q1 = quant(nq[:, 0:128], ns[:, 0:128], nx[:, 0:512], g1)
+            g2 = tt(nx[:, 640:1024], B[:].indirect(wr(r + 1, "k4", 40, 64)), X[:, 640:1024], A.add)
+        else:
+            g2 = tt(nx[:, 512:1024], B[:].indirect(wr(r + 1, "k4", 32, 64)), X[:, 512:1024], A.add)
         if not last:
-            tab["kk"] = partner_list(r + 1, v_k16)
-        v_q1 = quant(nq[:, 0:128], ns[:, 0:128], nx[:, 0:512], g1)
+            t = act(fr(r + 1, "kt"), fr(r + 1, "nn").indirect(fi[:, 24:42]), None, a_n, tab["fi"])
+            if r == 0:
+                for a in range(3):
+                    v_wt = act(T.w2[:, 96 * a:96 * a + 80], wt[:, 96 * a:96 * a + 80].indirect(T.pl[:, 0:5]), None, v_pf)
+            for a in range(3):
+                a_kt = act(fr(r + 1, "k2", 96 * a, 96 * a + 96), fr(r + 1, "kt", 96 * a, 96 * a + 96).indirect(T.pl[:, 0:6]), None, t)
+        else:
+            fun(ID, T.kyf[:, 0:128], half(r + 1, 0), 1.0, -1.0)
+            a_ky = fun(ID, T.kyf[:, 128:256], half(r + 1, 1), 1.0, -1.0)
+        if not last:
+            v_q1 = quant(nq[:, 0:128], ns[:, 0:128], nx[:, 0:512], g1)
         v_q2 = quant(nq[:, 128:256], ns[:, 128:256], nx[:, 512:1024], g2)
         x_done = (g1, g2)
+        if not last:
+            tab["tl"] = scan(fr(r + 1, "st", 0, 192), m16, fr(r + 1, "k2", 0, 192), a_kt)
+            scan(fr(r + 1, "n16", 0, 128), m16[:, 0:128], half(r + 1, 0))
+            tab["n16"] = scan(fr(r + 1, "n16", 128, 256), m16[:, 0:128], half(r + 1, 1))
 
     nd = [0]
 
@@ -566,15 +647,16 @@ def rank_program(g, core, T, topo):
     xq, xs = T["xq%d" % ROUNDS], T["xs%d" % ROUNDS]
     p1 = scores(T.vq, T.vqs, ROUNDS, 0, v_q1, v_v)
     p2 = scores(T.vq, T.vqs, ROUNDS, 1, v_q2)
-    y1 = vcopy(T.yo[:, 0:128], psv(4, 0, 128), p1)
+    y1 = act(T.yo[:, 0:128], psv(4, 0, 128), None, p1)
     y2 = vcopy(T.yo[:, 128:256], psv(5, 0, 128), p2)
-    out("y", T.kp[:], T.kyf[0:128:16, :], v_ky)
-    out("y", T.oc[:], xq[:, 0:256].bitcast(dt.uint8), v_q2)
+    out("y", T.kp[:], T.kyf[0:128:16, :], a_ky)
+    out("y", T.oc[:, 0:512], xq[:, 0:128].bitcast(dt.uint8), v_q1)
+    out("a", T.y[:, 0:128], T.yo[:, 0:128], y1)
+    out("y", T.oc[:, 512:1024], xq[:, 128:256].bitcast(dt.uint8), v_q2)
     out("a", T.osc[0:4, :], xs[0:4, :], v_q2)
     out("y", T.osc[4:8, :], xs[32:36, :])
     out("a", T.osc[8:12, :], xs[64:68, :])
-    out("y", T.osc[12:16, :], xs[96:100, :])
-    out("a", T.y[:, 0:128], T.yo[:, 0:128], y1)
+    out("a", T.osc[12:16, :], xs[96:100, :])
     out("y", T.y[:, 128:256], T.yo[:, 128:256], y2)
 
     wait("g", ("dout", nd[0]), ("loc", loc[0]), *[(s, n) for s, n in done.items()])

@@ -3,7 +3,7 @@ from concourse.mybir import dt, AluOpType, ActivationFunctionType
 
 ROUNDS = 3
 LIFT = 512.0
-AHEAD = 80
+AHEAD = 64
 A = AluOpType
 F = ActivationFunctionType
 CP, ID, SG = F.Copy, F.Identity, F.Sign
@@ -17,11 +17,11 @@ def lay(*parts):
     return out, at
 
 
-FREE, NFREE = lay(("sg", 256), ("tg", 288), ("ts", 288), ("tm", 16), ("t1", 64), ("r0", 128), ("c0", 64), ("s0", 128),
+FREE, NFREE = lay(("sg", 256), ("tg", 288), ("ts", 288), ("tm", 16), ("t1", 64), ("t2", 64), ("r0", 128), ("c0", 64), ("s0", 128),
                   *[("r%d" % i, 64) for i in range(1, 9)], *[("m%d" % i, 64) for i in range(1, 10)],
                   *[("s%d" % i, 64) for i in range(1, 5)], ("f", 128), ("sf", 128), ("f1", 32), ("hi", 32), ("so", 192), ("sp", 64), ("ss", 64), ("u", 64), ("su", 64), ("g", 64),
                   ("nn", 512), ("kp", 256), ("kk", 512), ("n4", 256), ("n16", 256), ("kt", 288), ("k2", 288), ("st", 288))
-WRAP, NWRAP = lay(("bl", 12), *[("l%d" % i, 4) for i in range(5)], ("sp", 4), ("u", 4), ("lo", 32), ("hi", 32), ("tn", 32), ("k4", 64), ("tl", 18))
+WRAP, NWRAP = lay(("bl", 12), *[("l%d" % i, 4) for i in range(5)], ("sp", 4), ("u", 4), ("ba", 4), ("n8", 8), ("n4", 32), ("lo", 32), ("hi", 32), ("tn", 32), ("k4", 64), ("tl", 18))
 
 SCRATCH = {
     "ps": ("psum", [128, 4096], "float32"),
@@ -47,9 +47,9 @@ SCRATCH = {
     "wt": ("sbuf", [128, 288], "bfloat16"), "tk": ("sbuf", [128, 160], "bfloat16"),
     "w2": ("sbuf", [128, 288], "bfloat16"), "pf": ("sbuf", [128, 192], "bfloat16"), "pl": ("sbuf", [128, 8], "uint16"),
     "tr": ("sbuf", [128, 80], "bfloat16"),
-    "kf": ("sbuf", [128, 128], "bfloat16"), "ke": ("sbuf", [128, 64], "bfloat16"),
+    "kf": ("sbuf", [128, 64], "bfloat16"), "ke": ("sbuf", [128, 64], "bfloat16"),
     "d0": ("sbuf", [128, 256], "bfloat16"), "d1": ("sbuf", [128, 256], "bfloat16"),
-    "uo": ("sbuf", [128, 8], "uint16"), "zl": ("sbuf", [128, 32], "uint16"),
+    "uo": ("sbuf", [128, 12], "uint16"), "zl": ("sbuf", [128, 32], "uint16"),
     "kyf": ("sbuf", [128, 256], "float32"),
     "yo": ("sbuf", [128, 256], "float32"),
 }
@@ -66,9 +66,10 @@ for _r in range(ROUNDS):
     for _n, _w in (("qz", 384), ("qh", 256), ("cin", 192)):
         SCRATCH["%s_%d" % (_n, _r)] = ("sbuf", [128, _w], "float8_e4m3fn_x4")
     SCRATCH["la_%d" % _r] = ("sbuf", [128, 192], "uint8")
+    SCRATCH["zh%d" % _r] = ("sbuf", [128, 512], "bfloat16")
 
-SEMAPHORES = ["sv", "sa", "st", "sg", "dx", "du", "dk", "dwc", "dws", "dv", "dxk", "dout", "loc"]
-SEMAPHORES += ["%s%d" % (n, r) for r in range(ROUNDS) for n in ("rk", "ra", "rb")]
+SEMAPHORES = ["sv", "sa", "st", "sg", "dx", "du", "dk", "dwc", "dws", "dv", "dxk", "dxl", "dout", "loc"]
+SEMAPHORES += ["%s%d" % (n, r) for r in range(ROUNDS) for n in ("rk", "ra", "rb", "dz", "dy")]
 
 
 def rank_program(g, core, T, topo):
@@ -191,15 +192,14 @@ def rank_program(g, core, T, topo):
     wait("y", t_x)
     t_wc = dma("y", "dwc", 16, T.wq[:, 0:512].bitcast(dt.uint8), T.wc[:])
     t_ws = dma("y", "dws", 16, T.wqs[:], T.ws[:])
-    t_v = dma("y", "dv", 16, T.vt[:], T.v[:])
 
     g_pi = iota(pi[:, 0:1], [[0, 1]], 0, 1, False)
     g_im = iota(im[:, 0:17], [[1, 17]], -1, 0)
     iota(ci[:, 40:52], [[0, 2], [-1, 6]], 6, 0)
     g_tm = iota(ci[:, 52:58], [[-1, 6]], 2, 0)
     g_ci = iota(ci[:, 32:40], [[16, 8]], 0, 0)
-    g_one = iota(T.one[:], [[1, 256]], 1, 0)
     g_dn = iota(im[:, 24:40], [[-1, 16]], 15, 0)
+    g_one = iota(T.one[:], [[1, 256]], 1, 0)
     iota(T.tr[:, 0:64], [[0, 4], [1, 16]], 0, 0)
     g_tr = iota(T.tr[:, 64:80], [[0, 4], [1, 4]], 0, 0)
     i0 = im[:, 1:17]
@@ -210,7 +210,8 @@ def rank_program(g, core, T, topo):
         ts(pi[:, 2 + d:3 + d], pi[:, 0:1], 3 - d, (2 << d) - 1, A.logical_shift_right, A.bitwise_and, g_pi)
     t = ts(pi[:, 6:7], pi[:, 0:1], 3, None, A.bitwise_and, None)
     v_c = vcopy(cs[:, 0:5], pi[:, 2:7], t)
-    v_uo = vcopy(T.uo[:], ci[:, 32:40], g_ci)
+    v_uo = vcopy(T.uo[:, 0:8], ci[:, 32:40], g_ci)
+    wait("v", g_im)
     q_, r_, tau = col(3), col(1), col(4)
 
     def on_top(a):
@@ -246,45 +247,34 @@ def rank_program(g, core, T, topo):
     a_un = fun(ID, col(12), col(9), 2.0 - 2.0 / LIFT, 2.0 + 2.0 / LIFT)
     un16, un4x4, tau4 = col(11), col(12), col(13)
 
-    ts(ms[:, 0:16], im[:, 0:16], q_, LIFT, A.is_equal, A.mult, v_c, g_im)
-    tb = ts(ms[:, 32:48], im[:, 0:16], q_, None, A.is_ge, None)
-    t3 = ts(yw[:, 0:3], ci[:, 40:58:6], r_, 1.0, A.subtract, A.add, g_tm)
-    ts(T.oq[:], i0, 0.0, q_, A.mult, A.add)
-    tb = tt(mw[:, 0:16], ms[:, 0:16], ms[:, 32:48], A.max, tb)
-    a_m16 = act(m16, mw[:, 0:16].indirect(T.oq[:, 0:12]), None, tb)
-    ts(ms[:, 16:20], im[:, 0:4], r_, LIFT, A.is_equal, A.mult)
-    t3 = ts(yw[:, 4:7], yw[:, 0:3], col(14), -0.4375, A.mult, A.add, t3, a_my)
-    tb = ts(ms[:, 48:52], im[:, 0:4], r_, None, A.is_ge, None)
-    t = ts(yl[:, 0:18], ci[:, 40:58], col(19), q_, A.mult, A.add, td)
-    t3 = vcopy(pi[:, 10:13], yw[:, 4:7], t3)
-    for d in range(2):
-        ts(mark[:, 2 << d:4 << d], im[:, 40 - (2 << d):40], col(d), 2.0, A.is_equal, A.mult, g_dn)
-    v_yl = vcopy(yl[:, 4:18:6], pi[:, 10:13], t3, t)
-    for d in range(2, 4):
-        tm = ts(mark[:, 2 << d:4 << d], im[:, 40 - (2 << d):40], col(d), 2.0, A.is_equal, A.mult)
-    v_k16 = vcopy(T.k16_0[:], T.kli[:], t_kl)
+    t3 = ts(yw[:, 0:3], ci[:, 40:58:6], r_, 1.0, A.subtract, A.add, v_c, g_tm)
+    ts(T.oq[:], i0, 0.0, q_, A.mult, A.add, g_im)
+    for d in range(4):
+        tm = ts(mark[:, 2 << d:4 << d], im[:, 40 - (2 << d):40], col(d), 2.0, A.is_equal, A.mult, g_dn)
     v_uq = quant(T.uq[:, 0:128], T.us[:, 0:128], T.ut[:, 0:512], t_u)
-    v_fi = ts(fi[:, 6:18], yl[:, 6:18], -1.0, 127.0, A.mult, A.add, v_yl)
     v_sg = tt(mark[:, 32:48], mark[:, 1:32:2], mark[:, 0:32:2], A.subtract, tm)
     sgn = mark[:, 32:48]
-    v_tk = fun(SG, T.tk[:, 0:80], T.tr[:], 1.0, 0.0, g_tr)
-    a_yc = fun(ID, yc[:, 64:128], T.one[:].indirect(yl[:, 0:4]), 1.0, -1.0, v_yl, g_one)
-    a_n = act(half(0, 0), T.one[:].indirect(T.k16_0[:, 0:8]), None, v_k16)
-    a_up = act(T.ups[:, 0:128], T.us[:, 0:128].indirect(T.uo[:, 0:8]), None, v_uq, v_uo)
-    act(fr(0, "kt", 0, 96), half(0, 0).indirect(yl[:, 0:6]), None, a_n)
-    a_kt = act(fr(0, "kt", 96, 192), half(0, 0).indirect(fi[:, 6:12]), None, v_fi)
-    fun(F.Relu, wa[:, 64:128], sgn.indirect(T.oq[:, 0:4]), 1.0, 0.0, v_sg)
+    t = ts(yl[:, 0:18], ci[:, 40:58], col(19), q_, A.mult, A.add, td)
+    v_k16 = vcopy(T.k16_0[:], T.kli[:], t_kl)
     v_up = vcopy(T.up[:, 0:128].bitcast(dt.uint32), T.uq[:, 0:128].bitcast(dt.uint32).indirect(T.uo[:, 0:8]), v_uq, v_uo)
-    tw = tt(wt[:, 96:160], sgn.indirect(T.oq[:, 0:4]), yc[:, 64:128], A.mult, v_w0, a_yc, v_sg)
-    ts(T.ot[:], i0, 0.0, tau, A.mult, A.add)
-    v_ot = tt(mw[:, 16:20], ms[:, 16:20], ms[:, 48:52], A.max, tb)
-    a_wa = act(wa[:, 0:64], wt[:, 96:160], 2.0, tw)
-    a_m4 = act(m4, mw[:, 16:20].indirect(T.ot[:, 0:8]), None, v_ot)
-    a_n = act(half(0, 1), T.one[:].indirect(T.k16_0[:, 8:16]), None)
-    tab["un"] = fun(ID, col(20), col(8), 0.125 - 0.125 / LIFT, 0.125 + 0.125 / LIFT)
+    v_yl = ts(yl[:, 4:18:6], yw[:, 0:3], col(14), -0.4375, A.mult, A.add, t3, a_my, t)
+    a_up = act(T.ups[:, 0:128], T.us[:, 0:128].indirect(T.uo[:, 0:8]), None, v_uq, v_uo)
+    a_yc = fun(ID, yc[:, 64:128], T.one[:].indirect(yl[:, 0:4]), 1.0, -1.0, t, g_one)
+    fun(F.Relu, wa[:, 64:128], sgn.indirect(T.oq[:, 0:4]), 1.0, 0.0, v_sg)
+    a_n = act(half(0, 0), T.one[:].indirect(T.k16_0[:, 0:8]), None, v_k16)
+    ts(ms[:, 16:20], im[:, 0:4], r_, LIFT, A.is_equal, A.mult)
+    tb = ts(ms[:, 48:52], im[:, 0:4], r_, None, A.is_ge, None)
     v_q1 = quant(T.xq0[:, 0:128], T.xs0[:, 0:128], T.x0[:, 0:512], t_x)
     v_q2 = quant(T.xq0[:, 128:256], T.xs0[:, 128:256], T.x0[:, 512:1024])
-    tab["tl"] = scan(fr(0, "st", 0, 192), m16, fr(0, "kt", 0, 192), a_kt, a_m16)
+    tw = tt(wt[:, 96:160], sgn.indirect(T.oq[:, 0:4]), yc[:, 64:128], A.mult, v_w0, a_yc, v_sg)
+    a_n = act(half(0, 1), T.one[:].indirect(T.k16_0[:, 8:16]), None)
+    a_wa = act(wa[:, 0:64], wt[:, 96:160], 2.0, tw)
+    ts(T.ot[:], i0, 0.0, tau, A.mult, A.add)
+    v_ot = tt(mw[:, 16:20], ms[:, 16:20], ms[:, 48:52], A.max, tb)
+    v_fi = ts(fi[:, 6:18], yl[:, 6:18], -1.0, 127.0, A.mult, A.add, v_yl)
+    a_m4 = act(m4, mw[:, 16:20].indirect(T.ot[:, 0:8]), None, v_ot)
+    v_tk = fun(SG, T.tk[:, 0:80], T.tr[:], 1.0, 0.0, g_tr)
+    tab["un"] = fun(ID, col(20), col(8), 0.125 - 0.125 / LIFT, 0.125 + 0.125 / LIFT)
 
     def four(r, h, *toks):
         return scan(fr(r, "n4", 128 * h, 128 * h + 128), m4, half(r, h), *toks)
@@ -314,9 +304,8 @@ def rank_program(g, core, T, topo):
     def read_by_own(r, f1, *toks):
         return act(fr(r, "kk", 0, 256), fr(r, "kp").indirect(T["k16_%d" % r][:, 0:16]), None, f1, *toks)
 
-    def exchanged(r, f2):
-        act(fr(r, "kk", 256, 512, 2), fr(r, "kk", 1, 256, 2), None, f2)
-        return act(fr(r, "kk", 257, 512, 2), fr(r, "kk", 0, 256, 2), None)
+    def exchanged(r, odd, *toks):
+        return act(fr(r, "kk", 256 + odd, 512, 2), fr(r, "kk", 1 - odd, 256, 2), None, *toks)
 
     def scores(lq, ls, r, h, *toks):
         a, b = 128 * h, 128 * h + 128
@@ -335,7 +324,8 @@ def rank_program(g, core, T, topo):
         tg, tsc, sg = fr(r, "tg"), fr(r, "ts"), fr(r, "sg")
 
         def tree(a, *toks):
-            return tt(tg[:, 96 * a:96 * a + 80], sg.indirect(wr(r, "tl", 6 * a, 6 * a + 5)), (T.w2 if r else wt)[:, 96 * a:96 * a + 80], A.mult, *toks)
+            signs = sg.indirect(wr(r, "tl", 6 * a, 6 * a + 5)) if r else fr(0, "kt", 0, 128).indirect((fi if a else yl)[:, 6 * a:6 * a + 5])
+            return tt(tg[:, 96 * a:96 * a + 80], signs, (T.w2 if r else wt)[:, 96 * a:96 * a + 80], A.mult, *toks)
 
         def climb(a, *toks):
             return scan(tsc[:, 96 * a:96 * a + 80], T.tk[:, 80:160] if r else T.tk[:, 0:80], tg[:, 96 * a:96 * a + 80], *toks)
@@ -355,25 +345,28 @@ def rank_program(g, core, T, topo):
             p = scores(T.up, T.ups, r, h, (v_q1, v_q2)[h], v_up, a_up)
             s = ts(sg[:, 128 * h:128 * h + 128], psv(4 + h, 0, 128), 0.0, 0.5, A.is_le, A.subtract, p)
             bankuse[4 + h] = [s]
-            if h == 0:
-                v_tl = ts(wr(r, "tl", 0, 12), fr(r, "st", 15, 192, 16), un16, 1.0, A.mult, A.subtract, tab["tl"], a_un)
+            if r and h == 0:
+                v_tl = ts(wr(r, "tl", 0, 12), fr(r, "st", 15, 192, 16), un16, 1.0, A.mult, A.subtract, tab["tl"])
         if r == 0:
             v_wt = tt(wt[:, 0:64], wa[:, 0:64], wa[:, 64:128], A.add, a_wa)
+            v_fs = vcopy(fr(0, "kt", 0, 128), sg.indirect(k16[:, 0:8]), s)
+            four(0, 0, a_m4)
+            t4 = four(0, 1, a_n)
         else:
             v_k16 = ts(k16[:], fr(r, "n16", 15, 256, 16), un16, 1.0, A.mult, A.subtract, tab["n16"])
             wait("g", v_k16)
             rk[r] = remote(r, T["kin%d" % r][:], k16[:], "rk%d" % r)
             t3 = scan(fr(r, "st", 192, 288), m16[:, 0:96], fr(r, "k2", 192, 288))
         if r == 0:
-            tg_ = tree(1, s, v_tl, g_wt)
-            tb_ = tree(0, v_wt)
-            four(0, 0, a_m4)
-            t4 = four(0, 1, a_n)
-            tg_ = climb(1, tg_, v_tk)
-            tb_ = climb(0, tb_)
+            tb_ = tree(0, v_fs, v_wt, g_wt)
             v_k4 = four_end(0, t4)
-            tg_ = top(1, tg_)
+            tg_ = tree(1, v_fi)
+            tb_ = climb(0, tb_, v_tk)
+            ts(ms[:, 0:16], im[:, 0:16], q_, LIFT, A.is_equal, A.mult)
+            tg_ = climb(1, tg_)
             tb_ = top(0, tb_)
+            tb = ts(ms[:, 32:48], im[:, 0:16], q_, None, A.is_ge, None)
+            tg_ = top(1, tg_)
         else:
             tb_ = tree(0, s, v_tl, v_wt)
             tg_ = tree(1)
@@ -382,9 +375,10 @@ def rank_program(g, core, T, topo):
             tg_ = climb(1, tg_)
         tb_ = step(0, tb_)
         if r == 0:
-            a_kt = act(fr(0, "kt", 192, 288), half(0, 0).indirect(fi[:, 12:18]), None)
+            tb16 = tt(mw[:, 0:16], ms[:, 0:16], ms[:, 32:48], A.max, tb)
             ta = fun(F.Abs, col(5), tau, 1.0, -2.0)
             fun(ID, col(24), r_, 2.0, -1.0)
+            fun(ID, col(26), tau, 256.0, -1.0)
             tb = fun(ID, col(25), r_, 4.0, 1.0)
             fun(ID, col(21), col(9), 0.5 - 0.5 / LIFT, 0.5 + 0.5 / LIFT)
             tab["a"] = fun(F.Abs, col(6), col(5), 256.0, -256.0, ta)
@@ -397,17 +391,21 @@ def rank_program(g, core, T, topo):
 
         def halves(a, b):
             tab["xk"] = act(xk[:, a:b], X[:].indirect(wr(r, "k4", a // 16, b // 16)), 0.5, v_k4, *x_done)
-            if b == 1024:
+            if b == (1024 if r else 800):
                 wait("y", tab["xk"])
-                tab["xj"] = dma("y", "dxk", 16 * (r + 1), xk2[:, 0:1024], xk[:])
-        halves(0, 1024 if r else 896)
+                tab["xj"] = tab["xl"] = dma("y", "dxk", 16 * (r + 1), xk2[:, 0:b], xk[:, 0:b])
+            elif b == 1024:
+                wait("y", tab["xk"])
+                tab["xl"] = dma("y", "dxl", 16, xk2[:, 800:b], xk[:, 800:b])
+        if r == 0:
+            halves(0, 448)
+            a_m16 = act(m16[:, 0:64], mw[:, 0:16].indirect(T.oq[:, 0:4]), None, tb16)
+            put("kk", "m16", act, m16[:, 64:192], mw[:, 0:16].indirect(T.oq[:, 0:8]), None)
+        halves(0 if r else 448, 1024 if r else 672)
 
         def bits():
-            t = fun(ID, fr(r, "f"), sg.indirect(k16[:, 0:8]), -1.0, 1.5, s, v_k16)
-            if r:
-                tab["f"] = fun(ID, fr(r, "f", 127, 128), q_, 0.0, 2.0, t)
-            else:
-                put("ra1", "f", fun, ID, fr(r, "f", 127, 128), q_, 0.0, 2.0, t)
+            t = fun(ID, fr(r, "f"), sg.indirect(k16[:, 0:8]) if r else fr(0, "kt", 0, 128), -1.0, 1.5, s, v_k16)
+            put("bits" if r else "ra1", "f", fun, ID, fr(r, "f", 127, 128), q_, 0.0, 2.0, t)
 
         def back():
             tab["x"] = act(fr(r, "r0", 64, 128), fr(r, "t1").indirect(wr(r, "bl", 8, 12)), None, tab["x"])
@@ -436,21 +434,26 @@ def rank_program(g, core, T, topo):
         if r == 0:
             put("t1", "z", ts, yc[:, 128:192], T.one[:].indirect(yl[:, 12:16]), 1.0, None, A.subtract, None)
             put("r0", "z", tt, wt[:, 192:256], sgn.indirect(T.oq[:, 0:4]), yc[:, 128:192], A.mult, "z", g_w2)
-            put("s0", "x", scan, fr(0, "st", 192, 288), m16[:, 0:96], fr(0, "kt", 192, 288), a_kt)
-            put("l0", "eq", ts, mw[:, 32:36], im[:, 1:5], r_, None, A.is_equal, None)
-            put("l0", "x", ts, wr(0, "tl", 12, 18), fr(0, "st", 192 + 15, 288, 16), un16, 1.0, A.mult, A.subtract, "x")
-            for name, call in zip(("a0", "l1", "a1", "l2"), third):
+            tab["ba"] = ts(wr(r, "ba"), fr(r, "tm", 0, 4), 0.5, 0.25, A.mult, A.subtract)
+            put("l0", "x", tree, 2, "z")
+            for name, call in zip(("l1", "a1", "l2"), third[1:]):
                 put(name, *call)
             for name, call in zip(("l1", "a1", "l2"), behind):
                 put(name, *call)
-            put("l2", *bit4)
-            put("a2", "kf", tt, T.kf[:], mw[:, 32:36].indirect(T.ot[:, 0:8]), T.cd[:], A.mult, "eq")
-            put("l3", "kf", fill, T.kf[:, 0:1], 0.0, "kf")
+            put("s0", "eq", ts, mw[:, 32:34], im[:, 1:3], col(0), None, A.is_equal, None)
+            put("ra1", "c", fun, ID, col(28), col(23), 1.0 / 256, 0.0, "cc")
+            put("ra1", "c", fun, ID, col(29), col(0), -2.0, r_)
+            put("a2", *bit4)
+            put("a2", "ol", ts, T.uo[:, 8:12], im[:, 1:5], 0.0, col(28), A.mult, A.add, "c")
+            put("a2", "kf", ts, T.kf[:], T.cd[:, 0:128:2], col(29), None, A.add, None)
+            put("l3", "ke", tt, T.ke[:], mw[:, 32:34].indirect(T.uo[:, 8:12]), T.kf[:], A.mult, "kf", "eq")
             put("a3", *wrapu[0])
-            put("a3", "ke", tt, T.ke[:], T.kf[:, 0:128:2], T.kf[:, 1:128:2], A.add, "kf")
+            put("a3", *base4)
+            put("a3", "ke", ts, T.ke[:, 0:1], T.ke[:, 0:1], col(17), None, A.mult, None, "ke")
             put("l4", *wrapu[1])
-            put("m9", *base4)
-            side.update(rb0=[bits], rb1=[lambda: halves(896, 1024)], ra2=[back], rb2=[other, place])
+            side.update(t2=[lambda: halves(672, 736)], rb0=[bits, lambda: halves(736, 800)], rb1=[lambda: halves(800, 960)], ra2=[back], rb2=[other])
+            side["ra3"] = [lambda: halves(960, 1024)]
+            side["a2"].append(place)
             for b, name in zip((0, 2, 1, 3), ("f", "z2", "h1", "h2")):
                 at = 528 * (b % 2) + 2 - b // 2 * 2
                 put(name, "e", quant, T.eq[:, 128 * b:128 * b + 128], T.es[:, 128 * b:128 * b + 128], T.et[:, at:at + 512], g_e[b % 2])
@@ -458,29 +461,44 @@ def rank_program(g, core, T, topo):
             put("z3", "fi", ts, fi[:, 24:30], yl[:, 0:6], 4.0, None, A.mult, None)
             put("z3", "fi", ts, fi[:, 30:42], fi[:, 6:18], 4.0, None, A.mult, None)
         else:
+            zh = T["zh%d" % r]
+
+            def twice(a, b):
+                t = act(zh[:, a:b], xk[:, 512:768].indirect(T.zl[:, a // 16:b // 16]), None, tab["xk"])
+                if b == 512:
+                    wait("g", t)
+                    g.dma_start(zh[:], xk[:, 0:512], accum_op=A.add).then_inc(T.sem["dz%d" % r], 16)
+                return ("dz%d" % r, 16)
             bits()
+            wait("g", act(xk2[:, 1024:1152], xk[:, 256:512].indirect(T.zl[:, 0:8]), None, tab["xk"]))
+            g.dma_start(xk2[:, 1024:1152], xk[:, 512:640], accum_op=A.add).then_inc(T.sem["dy%d" % r], 16)
+            gap("bits")
+            for name, a, b in (("t2", 0, 64), ("ra0", 64, 128), ("rb0", 128, 288), ("ra1", 288, 352), ("rb1", 352, 512)):
+                put(name, "zh", twice, a, b)
+            tab["ba"] = ts(wr(r, "ba"), tsc[:, 19:80:20], 0.5, 0.25, A.mult, A.subtract)
             for name, call in zip(("t1", "r0", "s0", "s0"), third):
                 put(name, *call)
-            for name, call in zip(("l0", "a0", "l1"), behind):
+            for name, call in zip(("l0", "l1", "a1"), behind):
                 put(name, *call)
-            put("a0", *bit4)
-            put("l2", *wrapu[0])
-            put("l3", *base4)
-            put("l3", *wrapu[1])
-            at = 0
-            for name, n in (("l1", 32), ("a1", 96), ("l2", 64), ("a2", 96), ("a3", 96)):
+            put("a2", *bit4)
+            put("a3", *wrapu[0])
+            put("a3", *base4)
+            put("l4", *wrapu[1])
+            at = 128
+            for name, n in (("r0", 32), ("l1", 32), ("a1", 32), ("l2", 96), ("a2", 32), ("l3", 96), ("f", 64)):
                 put(name, "zc", both, at, at + n)
                 at += n
-            side.update(ra0=[back], ra1=[other], rb1=[place])
+            side.update(ra2=[back], rb2=[other])
+            side["a2"].append(place)
         put("ra3", "kk", partner_list, r)
         put("l4", *lower)
-        side["l4"] += [none_lower, lambda: tab.update(kk=read_by_own(r, tab["kk"], v_k16))]
+        side["l4"] += [none_lower, lambda: tab.update(kk=read_by_own(r, tab["kk"], v_k16)), lambda: gap("kk")]
         tg_ = step(1, tg_)
         t = vcopy(fr(r, "t1"), T.cd[:].indirect(wr(r, "bl", 0, 4)), tb_, g_cd)
         gap("t1")
         v_r = vcopy(fr(r, "r0", 0, 64), fr(r, "t1").indirect(wr(r, "bl", 4, 8)), t, tg_)
         gap("r0")
-        t = scan(fr(r, "s0", 0, 64), m16[:, 0:64], fr(r, "r0", 0, 64), v_r)
+        t = scan(fr(r, "s0", 0, 64), m16[:, 0:64], fr(r, "r0", 0, 64), v_r, a_m16)
         v_cp = vcopy(fr(r, "c0"), fr(r, "r0", 0, 64))
         gap("s0")
         v_l = wrap(wr(r, "l0", 0, 4), fr(r, "s0", 15, 64, 16), t, tab["un"])
@@ -492,10 +510,16 @@ def rank_program(g, core, T, topo):
         for lv in range(4):
             off = wr(r, "l%d" % lv)
             ra, rb, ma, mb = (fr(r, "%s%d" % (n, 2 * lv + i)) for n in "rm" for i in (1, 2))
-            a_ra = act(ra, rw.indirect(off), None, v_l, a_r)
+            if lv == 0:
+                t = act(fr(r, "t2"), rw.indirect(wr(r, "ba")), None, a_r, tab["ba"])
+                gap("t2")
+                a_ra = act(ra, fr(r, "t2").indirect(wr(r, "bl", 4, 8)), None, t)
+                a_r = v_l
+            else:
+                a_ra = act(ra, rw.indirect(off), None, v_l, a_r)
             gap("ra%d" % lv)
             if lv < 3:
-                a_r = act(rb, ra.indirect(off), None, a_ra)
+                a_r = act(rb, ra.indirect(off), None, a_ra, a_r)
                 gap("rb%d" % lv)
             tab["m"] = v_m = tt(ma, mn.indirect(off), base[0], A.min, v_l, v_m, v_cp)
             gap("a%d" % lv)
@@ -513,8 +537,8 @@ def rank_program(g, core, T, topo):
         t = chain(fr(r, "so", 0, 192), d0[:, 0:192], d1[:, 0:192], t, tab["dd"], tab["b"], tab["g"], g_d)
         tc = fr(r, "so", 5, 192, 6)
         clo = ts(wr(r, "lo"), tc, 4.0, tau, A.mult, A.add, t)
-        ctn = ts(wr(r, "tn"), tc, col(23), None, A.add, None)
         th = tt(fr(r, "hi"), T.cc[:, 32:64], tc, A.subtract)
+        ctn = ts(wr(r, "tn"), tc, col(23), None, A.add, None)
 
         def new_list():
             return act(fr(r + 1, "nn"), fr(r, "kk").indirect(wr(r, "tn")), None, ctn, tab["kk"])
@@ -536,34 +560,42 @@ def rank_program(g, core, T, topo):
             return T["%s_%d" % (s, r)]
         pl = T["xs%d" % r]
         n1 = 4 * AHEAD if two else 512
-        z0 = act(Z[:, n1:512], xk2[:, 1024 - 8 * AHEAD:2048 - 8 * AHEAD].indirect(wr(r, "lo", n1 // 16, 32)), None, clo, tab["zc"], tab["xj"]) if two else None
-        tab["kk"] = exchanged(r, tab["kk"])
+
+        def rest(a, b):
+            return tt(Z[:, a:b], xk[:].indirect(wr(r, "hi", a // 16 - 32, b // 16 - 32)), xk2[:, a:b], A.add, tab["xl"])
+        z0 = None
+        if two:
+            z0 = act(Z[:, n1:512], xk2[:, 1024 - 8 * AHEAD:2048 - 8 * AHEAD].indirect(wr(r, "lo", n1 // 16, 32)), None, clo, tab["zc"], tab["xj"], ("dy%d" % r, 16))
+        exchanged(r, 0, tab["kk"])
         z1 = tt(Z[:, 0:n1], xk[:].indirect(wr(r, "lo", 0, n1 // 16)), xk2[:, 0:n1], A.add, clo, tab["xk"], tab["xj"])
         chi = ts(wr(r, "hi"), fr(r, "hi"), 4.0, tau, A.mult, A.add, th)
         gap("z1")
         tq = quant(nm("qz")[:, 0:128], pl[:, 256:384], Z[:, 0:512], z0, z1)
         p1 = layer(nm("qz")[:, 0:128], pl[:, 256:384], (0, 1, 2, 3), tq)
         if two:
-            z2 = tt(Z[:, 512:768], xk[:].indirect(wr(r, "hi", 0, 16)), xk2[:, 512:768], A.add, chi)
-            h1 = [scaled("ava"[b], H[:, b:512:4], b, 0, p1[b]) for b in range(3)]
+            z0 = act(Z[:, 608:768], zh[:].indirect(wr(r, "hi", 6, 16)), None, chi, tab["zh"])
+            z2 = vcopy(Z[:, 512:608], zh[:].indirect(wr(r, "hi", 0, 6)), chi, tab["zh"])
+        tab["kk"] = exchanged(r, 1)
+        if two:
+            h1 = [scaled("a", H[:, 0:512:4], 0, 0, p1[0])]
         else:
-            h1 = [scaled("a", H[:, b:512:4], b, 0, p1[b]) for b in range(3)]
+            a_n = new_list()
             z2 = tt(Z[:, 512:768], xk[:].indirect(wr(r, "hi", 0, 16)), xk2[:, 512:768], A.add, chi)
-            gap("z2")
-        tq = quant(nm("qz")[:, 128:256], pl[:, 640:768], Z[:, 256:768], z2)
+            h1 = [scaled("a", H[:, b:512:4], b, 0, p1[b]) for b in range(3)]
+        gap("z2")
+        tq = quant(nm("qz")[:, 128:256], pl[:, 640:768], Z[:, 256:768], z2, z0)
         p2 = layer(nm("qz")[:, 128:256], pl[:, 640:768], (4, 5, 6, 7), tq)
-
-        def rest(a, b):
-            return tt(Z[:, a:b], xk[:].indirect(wr(r, "hi", a // 16 - 32, b // 16 - 32)), xk2[:, a:b], A.add)
+        if two:
+            h1 += [scaled("va"[b - 1], H[:, b:512:4], b, 0, p1[b]) for b in (1, 2)]
         h1.append(scaled("v", H[:, 3:512:4], 3, 0, p1[3]))
         gap("h1")
         tq1 = quant(nm("qh")[:, 0:128], pl[:, 384:512], H[:, 0:512], *h1)
         h2 = [scaled("aavv"[b], H[:, 512 + b:768:4], 4 + b, 64, p2[b]) for b in range(4)]
         gap("h2")
-        if r:
-            rest(768, 864)
+        if two:
+            rest(768, 832)
+            a_n = new_list()
         tq2 = quant(nm("qh")[:, 128:256], pl[:, 512:640], H[:, 256:768], *h2)
-        a_n = new_list()
 
         wait("g", tq1)
         na = remote(r, nm("cin")[:, 0:128].bitcast(dt.uint8), nm("qh")[:, 0:128].bitcast(dt.uint8), "ra%d" % r)
@@ -571,22 +603,33 @@ def rank_program(g, core, T, topo):
         wait("g", tq2)
         nb = remote(r, nm("cin")[:, 128:192].bitcast(dt.uint8), nm("qh")[:, 192:256].bitcast(dt.uint8), "rb%d" % r)
         nb += remote(r, nm("la")[:, 128:192], pl[:, 576:640], "rb%d" % r)
+        if r == 0:
+            t_v = dma("g", "dv", 16, T.vt[:], T.v[:])
 
-        z3 = rest(864 if r else 768, 1024)
-        gap("z3")
+        z3 = rest(832 if r else 768, 1024)
+
+        def latch():
+            t16 = scan(fr(r + 1, "n16", 0, 128), m16[:, 0:128], half(r + 1, 0), a_n)
+            t4 = four(r + 1, 1)
+            return t16, (t4 if last else four(r + 1, 0))
+        if r == 0:
+            t16, t4 = latch()
         tq = quant(nm("qz")[:, 256:384], pl[:, 768:896], Z[:, 512:1024], z3)
         p = layer(nm("qz")[:, 256:384], pl[:, 768:896], (0, 1, 2, 3), tq)
+        gap("z3")
         if r == 0:
             t = scan(T.pf[:, 96:192], m16[:, 0:96], T.pf[:, 0:96], g_pf)
             t2 = fill(T.tk[:, 80:160], 1.0)
-        four(r + 1, 0, a_n)
-        t4 = four(r + 1, 1)
+        else:
+            t16, t4 = latch()
+        ts(wr(r + 1, "n8"), fr(r + 1, "n16", 15, 128, 16), un16, 1.0, A.mult, A.subtract, t16)
+        v_n = ts(wr(r + 1, "n4"), fr(r + 1, "n4", 128 + 3, 256, 4), col(21), col(26), A.mult, A.add, t4)
+        if not last:
+            v_k4 = four_end(r + 1, t4)
         if r == 0:
             v_pf = ts(T.pl[:, 0:6], T.pf[:, 111:192:16], un16, 1.0, A.mult, A.subtract, t)
             v_tk = fill(T.tk[:, 80:160:20], 0.0, t2)
-        bt = [scaled("av"[b], B[:, 768 + b:1024:4], b, 64, p[b]) for b in range(2)]
-        v_k4 = four_end(r + 1, t4)
-        bt += [scaled("av"[b - 2], B[:, 768 + b:1024:4], b, 64, p[b]) for b in range(2, 4)]
+        bt = [[scaled("vava"[b], B[:, 256 * b + 192:256 * b + 256], b, 64, p[b])] for b in range(4)]
         if r == 1:
             v_v = quant(T.vq[:, 0:128], T.vqs[:, 0:128], T.vt[:], t_v)
 
@@ -596,29 +639,25 @@ def rank_program(g, core, T, topo):
             p.append(mm(4 + b, 128, T.eq[:, 128 * b:128 * b + 128], T.es[:, 128 * b:128 * b + 128], cin[:, 0:128], nm("la")[:, 0:128],
                         ("ra%d" % r, na), tab["e"], *bankuse[4 + b]))
         for b in range(4):
-            o, i = B[:, b:512:4], psv(4 + b, 0, 128)
-            t = act(o, i, None, p[b]) if b % 2 == 0 else vcopy(o, i, p[b])
+            o, i = B[:, 256 * b:256 * b + 128], psv(4 + b, 0, 128)
+            t = act(o, i, None, p[b]) if b % 2 else vcopy(o, i, p[b])
             bankuse[4 + b] = [t]
-            bt.append(t)
+            bt[b].append(t)
         p = []
         for b in range(4):
             p.append(mm(b, 128, T.eq[:, 128 * b:128 * b + 128], T.es[:, 128 * b:128 * b + 128], cin[:, 64:192], nm("la")[:, 64:192],
                         ("rb%d" % r, nb), *bankuse[b]))
         for b in range(4):
-            o, i = B[:, 512 + b:768:4], psv(b, 64, 128)
-            t = act(o, i, None, p[b]) if b == 1 else vcopy(o, i, p[b])
+            o, i = B[:, 256 * b + 128:256 * b + 192], psv(b, 64, 128)
+            t = act(o, i, None, p[b]) if b else vcopy(o, i, p[b])
             bankuse[b] = [t]
-            bt.append(t)
+            bt[b].append(t)
 
         nx = T["x%d" % (r + 1)]
         nq, ns = T["xq%d" % (r + 1)], T["xs%d" % (r + 1)]
-        g1 = tt(nx[:, 0:512], B[:].indirect(wr(r + 1, "k4", 0, 32)), X[:, 0:512], A.add, v_k4, *bt)
-        if last:
-            tt(nx[:, 512:640], B[:].indirect(wr(r + 1, "k4", 32, 40)), X[:, 512:640], A.add)
-            v_q1 = quant(nq[:, 0:128], ns[:, 0:128], nx[:, 0:512], g1)
-            g2 = tt(nx[:, 640:1024], B[:].indirect(wr(r + 1, "k4", 40, 64)), X[:, 640:1024], A.add)
-        else:
-            g2 = tt(nx[:, 512:1024], B[:].indirect(wr(r + 1, "k4", 32, 64)), X[:, 512:1024], A.add)
+        for b in range(4):
+            g1 = tt(nx[:, b:512:4], B[:, 256 * b:256 * b + 256].indirect(wr(r + 1, "n8")), X[:, b:512:4], A.add, v_n, *bt[b])
+        g2 = tt(nx[:, 512:1024], B[:].indirect(wr(r + 1, "n4")), X[:, 512:1024], A.add)
         if not last:
             t = act(fr(r + 1, "kt"), fr(r + 1, "nn").indirect(fi[:, 24:42]), None, a_n, tab["fi"])
             if r == 0:
@@ -629,13 +668,11 @@ def rank_program(g, core, T, topo):
         else:
             fun(ID, T.kyf[:, 0:128], half(r + 1, 0), 1.0, -1.0)
             a_ky = fun(ID, T.kyf[:, 128:256], half(r + 1, 1), 1.0, -1.0)
-        if not last:
-            v_q1 = quant(nq[:, 0:128], ns[:, 0:128], nx[:, 0:512], g1)
+        v_q1 = quant(nq[:, 0:128], ns[:, 0:128], nx[:, 0:512], g1)
         v_q2 = quant(nq[:, 128:256], ns[:, 128:256], nx[:, 512:1024], g2)
         x_done = (g1, g2)
         if not last:
             tab["tl"] = scan(fr(r + 1, "st", 0, 192), m16, fr(r + 1, "k2", 0, 192), a_kt)
-            scan(fr(r + 1, "n16", 0, 128), m16[:, 0:128], half(r + 1, 0))
             tab["n16"] = scan(fr(r + 1, "n16", 128, 256), m16[:, 0:128], half(r + 1, 1))
 
     nd = [0]
@@ -647,16 +684,15 @@ def rank_program(g, core, T, topo):
     xq, xs = T["xq%d" % ROUNDS], T["xs%d" % ROUNDS]
     p1 = scores(T.vq, T.vqs, ROUNDS, 0, v_q1, v_v)
     p2 = scores(T.vq, T.vqs, ROUNDS, 1, v_q2)
-    y1 = act(T.yo[:, 0:128], psv(4, 0, 128), None, p1)
+    y1 = vcopy(T.yo[:, 0:128], psv(4, 0, 128), p1)
     y2 = vcopy(T.yo[:, 128:256], psv(5, 0, 128), p2)
-    out("y", T.kp[:], T.kyf[0:128:16, :], a_ky)
-    out("y", T.oc[:, 0:512], xq[:, 0:128].bitcast(dt.uint8), v_q1)
-    out("a", T.y[:, 0:128], T.yo[:, 0:128], y1)
-    out("y", T.oc[:, 512:1024], xq[:, 128:256].bitcast(dt.uint8), v_q2)
     out("a", T.osc[0:4, :], xs[0:4, :], v_q2)
-    out("y", T.osc[4:8, :], xs[32:36, :])
     out("a", T.osc[8:12, :], xs[64:68, :])
-    out("a", T.osc[12:16, :], xs[96:100, :])
+    out("y", T.kp[:], T.kyf[0:128:16, :], a_ky)
+    out("y", T.oc[:], xq[:, 0:256].bitcast(dt.uint8), v_q2)
+    out("y", T.osc[4:8, :], xs[32:36, :])
+    out("y", T.osc[12:16, :], xs[96:100, :])
+    out("a", T.y[:, 0:128], T.yo[:, 0:128], y1)
     out("y", T.y[:, 128:256], T.yo[:, 128:256], y2)
 
     wait("g", ("dout", nd[0]), ("loc", loc[0]), *[(s, n) for s, n in done.items()])

from concourse.bass import DstId, RemoteDMATransfer
from concourse.mybir import dt, AluOpType, ActivationFunctionType

ROUNDS = 3
LIFT = 512.0
AHEAD = 64
A = AluOpType
F = ActivationFunctionType
CP, ID, SG = F.Copy, F.Identity, F.Sign


def lay(*parts):
    at, out = 0, {}
    for n, w in parts:
        out[n] = (at, at + w)
        at += (w + 15) // 16 * 16
    return out, at


FREE, NFREE = lay(("sg", 256), ("tg", 288), ("ts", 288), ("tm", 16), ("t1", 64), ("t2", 64), ("r0", 128), ("c0", 64), ("s0", 128),
                  *[("r%d" % i, 64) for i in range(1, 9)], *[("m%d" % i, 64) for i in range(1, 10)],
                  *[("s%d" % i, 64) for i in range(1, 5)], ("f", 128), ("sf", 128), ("f1", 32), ("hi", 32), ("so", 192), ("sp", 64), ("ss", 64), ("u", 64), ("su", 64), ("g", 64),
                  ("nn", 512), ("kp", 256), ("kk", 512), ("n4", 256), ("n16", 256), ("kt", 288), ("k2", 288), ("st", 288))
WRAP, NWRAP = lay(("bl", 12), *[("l%d" % i, 4) for i in range(5)], ("sp", 4), ("u", 4), ("ba", 4), ("n8", 8), ("n4", 32), ("lo", 32), ("hi", 32), ("tn", 32), ("k4", 64), ("tl", 18))

SCRATCH = {
    "ps": ("psum", [128, 4096], "float32"),
    "kli": ("sbuf", [128, 16], "int32"),
    "ut": ("sbuf", [128, 512], "bfloat16"),
    "vt": ("sbuf", [128, 512], "bfloat16"),
    "uq": ("sbuf", [128, 128], "float8_e4m3fn_x4"), "us": ("sbuf", [128, 128], "uint8"),
    "up": ("sbuf", [128, 128], "float8_e4m3fn_x4"), "ups": ("sbuf", [128, 128], "uint8"),
    "vq": ("sbuf", [128, 128], "float8_e4m3fn_x4"), "vqs": ("sbuf", [128, 128], "uint8"),
    "wq": ("sbuf", [128, 512], "float8_e4m3fn_x4"), "wqs": ("sbuf", [128, 512], "uint8"),
    "ones": ("sbuf", [128, 514], "bfloat16"),
    "et": ("sbuf", [128, 1056], "bfloat16"),
    "eq": ("sbuf", [128, 512], "float8_e4m3fn_x4"), "es": ("sbuf", [128, 512], "uint8"),
    "pi": ("sbuf", [128, 16], "int32"),
    "cs": ("sbuf", [128, 32], "float32"),
    "im": ("sbuf", [128, 40], "float32"), "ms": ("sbuf", [128, 64], "bfloat16"), "mw": ("sbuf", [128, 48], "bfloat16"),
    "oq": ("sbuf", [128, 16], "uint16"), "ot": ("sbuf", [128, 16], "uint16"),
    "mt": ("sbuf", [128, 320], "bfloat16"),
    "one": ("sbuf", [128, 256], "bfloat16"), "cd": ("sbuf", [128, 128], "bfloat16"),
    "ci": ("sbuf", [128, 64], "float32"), "cc": ("sbuf", [128, 64], "float32"),
    "mark": ("sbuf", [128, 48], "bfloat16"), "yw": ("sbuf", [128, 32], "float32"), "yl": ("sbuf", [128, 32], "uint16"),
    "fi": ("sbuf", [128, 48], "uint16"), "yc": ("sbuf", [128, 192], "bfloat16"), "wa": ("sbuf", [128, 128], "bfloat16"),
    "wt": ("sbuf", [128, 288], "bfloat16"), "tk": ("sbuf", [128, 160], "bfloat16"),
    "w2": ("sbuf", [128, 288], "bfloat16"), "pf": ("sbuf", [128, 192], "bfloat16"), "pl": ("sbuf", [128, 8], "uint16"),
    "tr": ("sbuf", [128, 80], "bfloat16"),
    "kf": ("sbuf", [128, 64], "bfloat16"), "ke": ("sbuf", [128, 64], "bfloat16"),
    "d0": ("sbuf", [128, 256], "bfloat16"), "d1": ("sbuf", [128, 256], "bfloat16"),
    "uo": ("sbuf", [128, 12], "uint16"), "zl": ("sbuf", [128, 32], "uint16"),
    "kyf": ("sbuf", [128, 256], "float32"),
    "yo": ("sbuf", [128, 256], "float32"),
}
for _r in range(ROUNDS + 1):
    SCRATCH["x%d" % _r] = ("sbuf", [128, 1024], "bfloat16")
    SCRATCH["xq%d" % _r] = ("sbuf", [128, 256], "float8_e4m3fn_x4")
    SCRATCH["xs%d" % _r] = ("sbuf", [128, 896 if _r < ROUNDS else 256], "uint8")
    SCRATCH["fr%d" % _r] = ("sbuf", [128, NFREE], "bfloat16")
    SCRATCH["wr%d" % _r] = ("sbuf", [128, NWRAP], "uint16")
for _r in range(ROUNDS):
    for _n, _w, _d in (("xk", 1024, "bfloat16"), ("xj", 1536, "bfloat16"), ("z", 1024, "bfloat16"), ("h", 768, "bfloat16"), ("b", 1024, "bfloat16"),
                       ("k16_", 16, "uint16"), ("kin", 16, "uint16")):
        SCRATCH["%s%d" % (_n, _r)] = ("sbuf", [128, _w], _d)
    for _n, _w in (("qz", 384), ("qh", 256), ("cin", 192)):
        SCRATCH["%s_%d" % (_n, _r)] = ("sbuf", [128, _w], "float8_e4m3fn_x4")
    SCRATCH["la_%d" % _r] = ("sbuf", [128, 192], "uint8")
    SCRATCH["zh%d" % _r] = ("sbuf", [128, 512], "bfloat16")

SEMAPHORES = ["sv", "sa", "st", "sg", "dx", "du", "dk", "dwc", "dws", "dv", "dxk", "dxl", "dout", "loc"]
SEMAPHORES += ["%s%d" % (n, r) for r in range(ROUNDS) for n in ("rk", "ra", "rb", "dz", "dy")]


def rank_program(g, core, T, topo):
    rank = T.rank_of(core)
    if rank is None:
        return
    queues = {"v": g.vector, "a": g.scalar, "t": g.tensor, "g": g, "y": g.sync}
    own = {"v": "sv", "a": "sa", "t": "st", "g": "sg"}
    done = {"sv": 0, "sa": 0, "st": 0, "sg": 0}
    seen = {q: {} for q in queues}

    def wait(q, *toks):
        need = {}
        for t in toks:
            if t is not None:
                need[t[0]] = max(need.get(t[0], 0), t[1])
        for s, n in need.items():
            if seen[q].get(s, 0) < n:
                queues[q].wait_ge(T.sem[s], n)
                seen[q][s] = n

    def fin(q, ins):
        s = own[q]
        ins.then_inc(T.sem[s], 1)
        done[s] += 1
        return (s, done[s])

    def dma(q, sem, total, out, in_):
        queues[q].dma_start(out, in_).then_inc(T.sem[sem], 16)
        return (sem, total)

    def ts(out, in0, s1, s2, op0, op1, *toks):
        wait("v", *toks)
        if op1 is None:
            return fin("v", g.vector.tensor_scalar(out, in0, s1, None, op0))
        return fin("v", g.vector.tensor_scalar(out, in0, s1, s2, op0, op1))

    def tt(out, in0, in1, op, *toks):
        wait("v", *toks)
        return fin("v", g.vector.tensor_tensor(out, in0, in1, op))

    def vcopy(out, in_, *toks):
        wait("v", *toks)
        return fin("v", g.vector.tensor_copy(out, in_))

    def fill(out, c, *toks):
        wait("v", *toks)
        return fin("v", g.vector.memset(out, c))

    def scan(out, mask, data, *toks):
        wait("v", *toks)
        return fin("v", g.vector.tensor_tensor_scan(out, mask, data, 0.0, A.mult, A.max))

    def chain(out, mul, add, *toks):
        wait("v", *toks)
        return fin("v", g.vector.tensor_tensor_scan(out, mul, add, 0.0, A.mult, A.add))

    def quant(codes, plane, tile, *toks):
        wait("v", *toks)
        return fin("v", g.vector.quantize_mx(codes, plane, tile))

    def act(out, in_, scale, *toks):
        wait("a", *toks)
        if scale is None:
            return fin("a", g.scalar.activation(out, in_, CP))
        return fin("a", g.scalar.activation(out, in_, CP, scale=scale))

    def fun(f, out, in_, scale, bias, *toks):
        wait("a", *toks)
        return fin("a", g.scalar.activation(out, in_, f, bias=bias, scale=scale))

    def mm(bank, n, lq, ls, rq, rs, *toks):
        wait("t", *toks)
        return fin("t", g.tensor.matmul_mx(T.ps[:, 512 * bank:512 * bank + n], lq, ls, rq, rs, True, True))

    def psv(bank, a, b):
        return T.ps[:, 512 * bank + a:512 * bank + b]

    def remote(r, out, in_, sem):
        dst = T.cores[rank ^ (1 << r)]
        rid, pid, _ = topo.addr(dst)
        ne = len(topo.engines(core, dst))
        g.remote_dma(out, in_, T.sem[sem], T.sem.loc, pid, rid, topo.mask(core, dst))
        loc[0] += ne
        return ne

    def iota(out, pat, base, ch, small=True):
        if small:
            return fin("g", g.iota(out, pat, base, ch, allow_small_or_imprecise_dtypes=True))
        return fin("g", g.iota(out, pat, base, ch))

    def fr(r, name, a=0, b=None, step=1):
        lo, hi = FREE[name]
        return T["fr%d" % r][:, lo + a:(hi if b is None else lo + b):step]

    def wr(r, name, a=0, b=None):
        lo, hi = WRAP[name]
        return T["wr%d" % r][:, lo + a:(hi if b is None else lo + b)]

    def half(r, h):
        return fr(r, "nn", h, 512, 4) if r else fr(0, "nn", 128 * h, 128 * h + 128)

    loc = [0]
    tab = {}
    side = {}

    def gap(name):
        for f in side.pop(name, []):
            f()

    cs, d0, d1, pi, im, mark, yw, yl, wa, wt, yc, ci = T.cs, T.d0, T.d1, T.pi, T.im, T.mark, T.yw, T.yl, T.wa, T.wt, T.yc, T.ci
    ms, mw, m16, m4, fi = T.ms, T.mw, T.mt[:, 0:192], T.mt[:, 192:320], T.fi

    def col(i):
        return cs[:, i:i + 1]

    t_kl = dma("y", "dk", 16, T.kli[:], T.kl[:])
    t_x = dma("y", "dx", 16, T.x0[:], T.x[:])
    t_u = dma("a", "du", 16, T.ut[:], T.u[:])
    wait("y", t_x)
    t_wc = dma("y", "dwc", 16, T.wq[:, 0:512].bitcast(dt.uint8), T.wc[:])
    t_ws = dma("y", "dws", 16, T.wqs[:], T.ws[:])

    g_pi = iota(pi[:, 0:1], [[0, 1]], 0, 1, False)
    g_im = iota(im[:, 0:17], [[1, 17]], -1, 0)
    iota(ci[:, 40:52], [[0, 2], [-1, 6]], 6, 0)
    g_tm = iota(ci[:, 52:58], [[-1, 6]], 2, 0)
    g_ci = iota(ci[:, 32:40], [[16, 8]], 0, 0)
    g_dn = iota(im[:, 24:40], [[-1, 16]], 15, 0)
    g_one = iota(T.one[:], [[1, 256]], 1, 0)
    iota(T.tr[:, 0:64], [[0, 4], [1, 16]], 0, 0)
    g_tr = iota(T.tr[:, 64:80], [[0, 4], [1, 4]], 0, 0)
    i0 = im[:, 1:17]

    fill(mark[:, 0:2], 0.0)
    v_w0 = fill(wt[:], 0.0)
    for d in range(4):
        ts(pi[:, 2 + d:3 + d], pi[:, 0:1], 3 - d, (2 << d) - 1, A.logical_shift_right, A.bitwise_and, g_pi)
    t = ts(pi[:, 6:7], pi[:, 0:1], 3, None, A.bitwise_and, None)
    v_c = vcopy(cs[:, 0:5], pi[:, 2:7], t)
    v_uo = vcopy(T.uo[:, 0:8], ci[:, 32:40], g_ci)
    wait("v", g_im)
    q_, r_, tau = col(3), col(1), col(4)

    def on_top(a):
        for e in range(3):
            w = []
            for lead in range(7 - 4 * (a // 2), 3 - 4 * (a // 2), -1):
                child = lead >> (2 - e)
                w.append((4 * (child & 1) - 2) * (child if a == 0 else child >> 1))
            at = 96 * a + 64 + e
            if w[0] - w[1] == w[2] - w[3] and any(w):
                t = iota(wt[:, at:at + 16:4], [[w[2] - w[0], 2], [w[1] - w[0], 2]], w[0], 0)
            elif any(w):
                iota(wt[:, at:at + 16:8], [[w[2] - w[0], 2]], w[0], 0)
                t = iota(wt[:, at + 4:at + 16:8], [[w[3] - w[1], 2]], w[1], 0)
        return t
    wait("g", v_w0)
    on_top(0)
    g_wt = on_top(1)
    g_c8 = iota(ci[:, 0:32], [[8, 32]], 0, 0)
    g_cd = iota(T.cd[:], [[4, 64], [1, 2]], 1, 0)

    a_tau = fun(F.Square, col(10), tau, 0.25, 0.125, v_c)
    fun(SG, cs[:, 15:17], cs[:, 1:3], 1.0, 0.0)
    fun(SG, col(17), r_, 1.0, 0.0)
    td = fun(ID, col(18), col(0), 4.0, 1.0)
    a_my = fun(ID, col(14), col(10), 1.0, 0.109375, a_tau)
    fun(SG, col(8), q_, 1.0, -14.5)
    a_sg = fun(SG, col(9), r_, 1.0, -2.5)
    wait("a", td)
    td = fin("a", g.scalar.activation(cs[:, 28:32], cs[:, 15:19], ID, accum_out=col(19)))
    fun(ID, col(13), tau, 1.0, -4.0)
    fun(ID, col(11), col(8), 0.5 - 0.5 / LIFT, 0.5 + 0.5 / LIFT, a_sg)
    a_un = fun(ID, col(12), col(9), 2.0 - 2.0 / LIFT, 2.0 + 2.0 / LIFT)
    un16, un4x4, tau4 = col(11), col(12), col(13)

    t3 = ts(yw[:, 0:3], ci[:, 40:58:6], r_, 1.0, A.subtract, A.add, v_c, g_tm)
    ts(T.oq[:], i0, 0.0, q_, A.mult, A.add, g_im)
    for d in range(4):
        tm = ts(mark[:, 2 << d:4 << d], im[:, 40 - (2 << d):40], col(d), 2.0, A.is_equal, A.mult, g_dn)
    v_uq = quant(T.uq[:, 0:128], T.us[:, 0:128], T.ut[:, 0:512], t_u)
    v_sg = tt(mark[:, 32:48], mark[:, 1:32:2], mark[:, 0:32:2], A.subtract, tm)
    sgn = mark[:, 32:48]
    t = ts(yl[:, 0:18], ci[:, 40:58], col(19), q_, A.mult, A.add, td)
    v_k16 = vcopy(T.k16_0[:], T.kli[:], t_kl)
    v_up = vcopy(T.up[:, 0:128].bitcast(dt.uint32), T.uq[:, 0:128].bitcast(dt.uint32).indirect(T.uo[:, 0:8]), v_uq, v_uo)
    v_yl = ts(yl[:, 4:18:6], yw[:, 0:3], col(14), -0.4375, A.mult, A.add, t3, a_my, t)
    a_up = act(T.ups[:, 0:128], T.us[:, 0:128].indirect(T.uo[:, 0:8]), None, v_uq, v_uo)
    a_yc = fun(ID, yc[:, 64:128], T.one[:].indirect(yl[:, 0:4]), 1.0, -1.0, t, g_one)
    fun(F.Relu, wa[:, 64:128], sgn.indirect(T.oq[:, 0:4]), 1.0, 0.0, v_sg)
    a_n = act(half(0, 0), T.one[:].indirect(T.k16_0[:, 0:8]), None, v_k16)
    ts(ms[:, 16:20], im[:, 0:4], r_, LIFT, A.is_equal, A.mult)
    tb = ts(ms[:, 48:52], im[:, 0:4], r_, None, A.is_ge, None)
    v_q1 = quant(T.xq0[:, 0:128], T.xs0[:, 0:128], T.x0[:, 0:512], t_x)
    v_q2 = quant(T.xq0[:, 128:256], T.xs0[:, 128:256], T.x0[:, 512:1024])
    tw = tt(wt[:, 96:160], sgn.indirect(T.oq[:, 0:4]), yc[:, 64:128], A.mult, v_w0, a_yc, v_sg)
    a_n = act(half(0, 1), T.one[:].indirect(T.k16_0[:, 8:16]), None)
    a_wa = act(wa[:, 0:64], wt[:, 96:160], 2.0, tw)
    ts(T.ot[:], i0, 0.0, tau, A.mult, A.add)
    v_ot = tt(mw[:, 16:20], ms[:, 16:20], ms[:, 48:52], A.max, tb)
    v_fi = ts(fi[:, 6:18], yl[:, 6:18], -1.0, 127.0, A.mult, A.add, v_yl)
    a_m4 = act(m4, mw[:, 16:20].indirect(T.ot[:, 0:8]), None, v_ot)
    v_tk = fun(SG, T.tk[:, 0:80], T.tr[:], 1.0, 0.0, g_tr)
    tab["un"] = fun(ID, col(20), col(8), 0.125 - 0.125 / LIFT, 0.125 + 0.125 / LIFT)

    def four(r, h, *toks):
        return scan(fr(r, "n4", 128 * h, 128 * h + 128), m4, half(r, h), *toks)

    def four_end(r, t):
        return ts(wr(r, "k4"), fr(r, "n4", 3, 256, 4), un4x4, tau4, A.mult, A.add, t)

    g_w2 = on_top(2)
    wait("g", v_k16)
    rk = [remote(0, T.kin0[:], T.k16_0[:], "rk0"), 0, 0]
    tab["x"] = None
    iota(d1[:, 2:192:6], [[0, 32]], 0, 0)
    for at, c in ((0, 0), (2, -1), (3, 1)):
        g_d = iota(d0[:, at:192:6], [[0, 32]], c, 0)
    g_e = []
    wait("g", iota(T.ones[:], [[0, 514]], 1, 0))
    for b in range(2):
        g_e.append(fin("g", g.affine_select(T.et[:, 528 * b:528 * b + 514], T.ones[:], [[-1, 514]], A.is_equal, 0.0, b + 2, 4)))
    iota(T.pf[:, 80:96], [[1, 16]], 81, 0)
    for b in range(4):
        iota(T.pf[:, 20 * b:20 * b + 4], [[1, 4]], 65 + 4 * b, 0)
        g_pf = iota(T.pf[:, 20 * b + 4:20 * b + 20], [[1, 16]], 1 + 16 * b, 0)

    def partner_list(r, *toks):
        return act(fr(r, "kp"), T.one[:].indirect(T["kin%d" % r][:, 0:16]), None, ("rk%d" % r, rk[r]))

    def read_by_own(r, f1, *toks):
        return act(fr(r, "kk", 0, 256), fr(r, "kp").indirect(T["k16_%d" % r][:, 0:16]), None, f1, *toks)

    def exchanged(r, odd, *toks):
        return act(fr(r, "kk", 256 + odd, 512, 2), fr(r, "kk", 1 - odd, 256, 2), None, *toks)

    def scores(lq, ls, r, h, *toks):
        a, b = 128 * h, 128 * h + 128
        return mm(4 + h, 128, lq[:, 0:128], ls[:, 0:128], T["xq%d" % r][:, a:b], T["xs%d" % r][:, a:b], *toks, *bankuse[4 + h])

    def put(name, key, f, *a):
        side.setdefault(name, []).append(lambda: tab.update({key: f(*[tab[x] if isinstance(x, str) else x for x in a])}))

    bankuse = [[] for _ in range(8)]
    x_done = (t_x,)
    for r in range(ROUNDS):
        X, xk, Z, H, B = T["x%d" % r], T["xk%d" % r], T["z%d" % r], T["h%d" % r], T["b%d" % r]
        last = r == ROUNDS - 1
        two = r > 0
        k16 = T["k16_%d" % r]
        tg, tsc, sg = fr(r, "tg"), fr(r, "ts"), fr(r, "sg")

        def tree(a, *toks):
            signs = sg.indirect(wr(r, "tl", 6 * a, 6 * a + 5)) if r else fr(0, "kt", 0, 128).indirect((fi if a else yl)[:, 6 * a:6 * a + 5])
            return tt(tg[:, 96 * a:96 * a + 80], signs, (T.w2 if r else wt)[:, 96 * a:96 * a + 80], A.mult, *toks)

        def climb(a, *toks):
            return scan(tsc[:, 96 * a:96 * a + 80], T.tk[:, 80:160] if r else T.tk[:, 0:80], tg[:, 96 * a:96 * a + 80], *toks)

        def top(a, t):
            if r:
                return t
            return tt(fr(r, "tm", 4 * a, 4 * a + 4), tsc[:, 96 * a + 15:96 * a + 64:16], tsc[:, 96 * a + 67:96 * a + 80:4], A.max, t)

        def step(a, t):
            return vcopy(wr(r, "bl", 4 * a, 4 * a + 4), tsc[:, 96 * a + 19:96 * a + 80:20] if r else fr(r, "tm", 4 * a, 4 * a + 4), t)

        def wrap(out, src, *toks):
            return ts(out, src, col(20), 0.2, A.mult, A.subtract, *toks)

        for h in range(2):
            p = scores(T.up, T.ups, r, h, (v_q1, v_q2)[h], v_up, a_up)
            s = ts(sg[:, 128 * h:128 * h + 128], psv(4 + h, 0, 128), 0.0, 0.5, A.is_le, A.subtract, p)
            bankuse[4 + h] = [s]
            if r and h == 0:
                v_tl = ts(wr(r, "tl", 0, 12), fr(r, "st", 15, 192, 16), un16, 1.0, A.mult, A.subtract, tab["tl"])
        if r == 0:
            v_wt = tt(wt[:, 0:64], wa[:, 0:64], wa[:, 64:128], A.add, a_wa)
            v_fs = vcopy(fr(0, "kt", 0, 128), sg.indirect(k16[:, 0:8]), s)
            four(0, 0, a_m4)
            t4 = four(0, 1, a_n)
        else:
            v_k16 = ts(k16[:], fr(r, "n16", 15, 256, 16), un16, 1.0, A.mult, A.subtract, tab["n16"])
            wait("g", v_k16)
            rk[r] = remote(r, T["kin%d" % r][:], k16[:], "rk%d" % r)
            t3 = scan(fr(r, "st", 192, 288), m16[:, 0:96], fr(r, "k2", 192, 288))
        if r == 0:
            tb_ = tree(0, v_fs, v_wt, g_wt)
            v_k4 = four_end(0, t4)
            tg_ = tree(1, v_fi)
            tb_ = climb(0, tb_, v_tk)
            ts(ms[:, 0:16], im[:, 0:16], q_, LIFT, A.is_equal, A.mult)
            tg_ = climb(1, tg_)
            tb_ = top(0, tb_)
            tb = ts(ms[:, 32:48], im[:, 0:16], q_, None, A.is_ge, None)
            tg_ = top(1, tg_)
        else:
            tb_ = tree(0, s, v_tl, v_wt)
            tg_ = tree(1)
            tb_ = climb(0, tb_, v_tk)
            tab["x"] = ts(wr(r, "tl", 12, 18), fr(r, "st", 192 + 15, 288, 16), un16, 1.0, A.mult, A.subtract, t3)
            tg_ = climb(1, tg_)
        tb_ = step(0, tb_)
        if r == 0:
            tb16 = tt(mw[:, 0:16], ms[:, 0:16], ms[:, 32:48], A.max, tb)
            ta = fun(F.Abs, col(5), tau, 1.0, -2.0)
            fun(ID, col(24), r_, 2.0, -1.0)
            fun(ID, col(26), tau, 256.0, -1.0)
            tb = fun(ID, col(25), r_, 4.0, 1.0)
            fun(ID, col(21), col(9), 0.5 - 0.5 / LIFT, 0.5 + 0.5 / LIFT)
            tab["a"] = fun(F.Abs, col(6), col(5), 256.0, -256.0, ta)
            fun(ID, col(22), col(9), 1.0 - 1.0 / LIFT, 1.0 + 1.0 / LIFT)
            fun(ID, T.cc[:, 0:32], ci[:, 0:32], 1.0, col(24), g_c8, tb)
            fun(ID, T.cc[:, 32:64], ci[:, 0:32], 2.0, col(25))
            put("ra0", "c", fun, ID, col(27), col(0), 4.0, tau)
            put("ra0", "cc", fun, ID, col(23), col(6), -1.0, 256.0, "a")
        xk2 = T["xj%d" % r]

        def halves(a, b):
            tab["xk"] = act(xk[:, a:b], X[:].indirect(wr(r, "k4", a // 16, b // 16)), 0.5, v_k4, *x_done)
            if b == (1024 if r else 800):
                wait("y", tab["xk"])
                tab["xj"] = tab["xl"] = dma("y", "dxk", 16 * (r + 1), xk2[:, 0:b], xk[:, 0:b])
            elif b == 1024:
                wait("y", tab["xk"])
                tab["xl"] = dma("y", "dxl", 16, xk2[:, 800:b], xk[:, 800:b])
        if r == 0:
            halves(0, 448)
            a_m16 = act(m16[:, 0:64], mw[:, 0:16].indirect(T.oq[:, 0:4]), None, tb16)
            put("kk", "m16", act, m16[:, 64:192], mw[:, 0:16].indirect(T.oq[:, 0:8]), None)
        halves(0 if r else 448, 1024 if r else 672)

        def bits():
            t = fun(ID, fr(r, "f"), sg.indirect(k16[:, 0:8]) if r else fr(0, "kt", 0, 128), -1.0, 1.5, s, v_k16)
            put("bits" if r else "ra1", "f", fun, ID, fr(r, "f", 127, 128), q_, 0.0, 2.0, t)

        def back():
            tab["x"] = act(fr(r, "r0", 64, 128), fr(r, "t1").indirect(wr(r, "bl", 8, 12)), None, tab["x"])

        def place():
            tab["f1"] = act(fr(r, "f1"), fr(r, "sf", 3, 128, 4), col(21), tab["sf"])
            tab["dd"] = fun(ID, d0[:, 5:192:6], fr(r, "sf", 3, 128, 4), col(22), -3.0)

        def other():
            tab["u"] = act(fr(r, "u"), fr(r, "r0").indirect(wr(r, "sp")), None, tab["x"], tab["sp"])

        def none_lower():
            tab["g"] = act(d0[:, 1:192:3], fr(r, "g"), -1.0, tab["g"])

        def both(a, b):
            return tt(xk2[:, 1024 + a:1024 + b], xk[:, 4 * AHEAD:512].indirect(T.zl[:, a // 16:b // 16]), xk[:, 8 * AHEAD + a:8 * AHEAD + b],
                      A.add, tab["xk"], tab["zl"])
        third = (("x", tree, 2, "x"), ("x", climb, 2, "x"), ("x", top, 2, "x"), ("x", step, 2, "x"))
        behind = (("sp", tt, fr(r, "sp"), sg.indirect(k16[:, 0:4]), T.one[:, 0:128:2], A.add),
                  ("sp", scan, fr(r, "ss"), m16[:, 0:64], fr(r, "sp"), "sp"),
                  ("sp", ts, wr(r, "sp"), fr(r, "ss", 15, 64, 16), un16, 0.5, A.mult, A.subtract, "sp"))
        wrapu = (("u", scan, fr(r, "su"), m16[:, 0:64], fr(r, "u"), "u"), ("u", wrap, wr(r, "u"), fr(r, "su", 15, 64, 16), "u"))
        lower = ("g", tt, fr(r, "g"), fr(r, "m7"), T.ke[:], A.is_ge, "ke", "m")
        bit4 = ("sf", scan, fr(r, "sf"), m4, fr(r, "f"), "f")
        base4 = ("b", tt, d1[:, 5:192:6], fr(r, "f1"), T.cc[:, 0:32], A.add, "f1", "cc")
        if r == 0:
            put("t1", "z", ts, yc[:, 128:192], T.one[:].indirect(yl[:, 12:16]), 1.0, None, A.subtract, None)
            put("r0", "z", tt, wt[:, 192:256], sgn.indirect(T.oq[:, 0:4]), yc[:, 128:192], A.mult, "z", g_w2)
            tab["ba"] = ts(wr(r, "ba"), fr(r, "tm", 0, 4), 0.5, 0.25, A.mult, A.subtract)
            put("l0", "x", tree, 2, "z")
            for name, call in zip(("l1", "a1", "l2"), third[1:]):
                put(name, *call)
            for name, call in zip(("l1", "a1", "l2"), behind):
                put(name, *call)
            put("s0", "eq", ts, mw[:, 32:34], im[:, 1:3], col(0), None, A.is_equal, None)
            put("ra1", "c", fun, ID, col(28), col(23), 1.0 / 256, 0.0, "cc")
            put("ra1", "c", fun, ID, col(29), col(0), -2.0, r_)
            put("a2", *bit4)
            put("a2", "ol", ts, T.uo[:, 8:12], im[:, 1:5], 0.0, col(28), A.mult, A.add, "c")
            put("a2", "kf", ts, T.kf[:], T.cd[:, 0:128:2], col(29), None, A.add, None)
            put("l3", "ke", tt, T.ke[:], mw[:, 32:34].indirect(T.uo[:, 8:12]), T.kf[:], A.mult, "kf", "eq")
            put("a3", *wrapu[0])
            put("a3", *base4)
            put("a3", "ke", ts, T.ke[:, 0:1], T.ke[:, 0:1], col(17), None, A.mult, None, "ke")
            put("l4", *wrapu[1])
            side.update(t2=[lambda: halves(672, 736)], rb0=[bits, lambda: halves(736, 800)], rb1=[lambda: halves(800, 960)], ra2=[back], rb2=[other])
            side["ra3"] = [lambda: halves(960, 1024)]
            side["a2"].append(place)
            for b, name in zip((0, 2, 1, 3), ("f", "z2", "h1", "h2")):
                at = 528 * (b % 2) + 2 - b // 2 * 2
                put(name, "e", quant, T.eq[:, 128 * b:128 * b + 128], T.es[:, 128 * b:128 * b + 128], T.et[:, at:at + 512], g_e[b % 2])
            put("z1", "zl", ts, T.zl[:], ci[:, 0:32], col(27), None, A.add, None)
            put("z3", "fi", ts, fi[:, 24:30], yl[:, 0:6], 4.0, None, A.mult, None)
            put("z3", "fi", ts, fi[:, 30:42], fi[:, 6:18], 4.0, None, A.mult, None)
        else:
            zh = T["zh%d" % r]

            def twice(a, b):
                t = act(zh[:, a:b], xk[:, 512:768].indirect(T.zl[:, a // 16:b // 16]), None, tab["xk"])
                if b == 512:
                    wait("g", t)
                    g.dma_start(zh[:], xk[:, 0:512], accum_op=A.add).then_inc(T.sem["dz%d" % r], 16)
                return ("dz%d" % r, 16)
            bits()
            wait("g", act(xk2[:, 1024:1152], xk[:, 256:512].indirect(T.zl[:, 0:8]), None, tab["xk"]))
            g.dma_start(xk2[:, 1024:1152], xk[:, 512:640], accum_op=A.add).then_inc(T.sem["dy%d" % r], 16)
            gap("bits")
            for name, a, b in (("t2", 0, 64), ("ra0", 64, 128), ("rb0", 128, 288), ("ra1", 288, 352), ("rb1", 352, 512)):
                put(name, "zh", twice, a, b)
            tab["ba"] = ts(wr(r, "ba"), tsc[:, 19:80:20], 0.5, 0.25, A.mult, A.subtract)
            for name, call in zip(("t1", "r0", "s0", "s0"), third):
                put(name, *call)
            for name, call in zip(("l0", "l1", "a1"), behind):
                put(name, *call)
            put("a2", *bit4)
            put("a3", *wrapu[0])
            put("a3", *base4)
            put("l4", *wrapu[1])
            at = 128
            for name, n in (("r0", 32), ("l1", 32), ("a1", 32), ("l2", 96), ("a2", 32), ("l3", 96), ("f", 64)):
                put(name, "zc", both, at, at + n)
                at += n
            side.update(ra2=[back], rb2=[other])
            side["a2"].append(place)
        put("ra3", "kk", partner_list, r)
        put("l4", *lower)
        side["l4"] += [none_lower, lambda: tab.update(kk=read_by_own(r, tab["kk"], v_k16)), lambda: gap("kk")]
        tg_ = step(1, tg_)
        t = vcopy(fr(r, "t1"), T.cd[:].indirect(wr(r, "bl", 0, 4)), tb_, g_cd)
        gap("t1")
        v_r = vcopy(fr(r, "r0", 0, 64), fr(r, "t1").indirect(wr(r, "bl", 4, 8)), t, tg_)
        gap("r0")
        t = scan(fr(r, "s0", 0, 64), m16[:, 0:64], fr(r, "r0", 0, 64), v_r, a_m16)
        v_cp = vcopy(fr(r, "c0"), fr(r, "r0", 0, 64))
        gap("s0")
        v_l = wrap(wr(r, "l0", 0, 4), fr(r, "s0", 15, 64, 16), t, tab["un"])
        gap("l0")

        a_r, v_m = v_r, v_r
        rw = mn = fr(r, "r0", 0, 64)
        base = (fr(r, "c0"), mn)
        for lv in range(4):
            off = wr(r, "l%d" % lv)
            ra, rb, ma, mb = (fr(r, "%s%d" % (n, 2 * lv + i)) for n in "rm" for i in (1, 2))
            if lv == 0:
                t = act(fr(r, "t2"), rw.indirect(wr(r, "ba")), None, a_r, tab["ba"])
                gap("t2")
                a_ra = act(ra, fr(r, "t2").indirect(wr(r, "bl", 4, 8)), None, t)
                a_r = v_l
            else:
                a_ra = act(ra, rw.indirect(off), None, v_l, a_r)
            gap("ra%d" % lv)
            if lv < 3:
                a_r = act(rb, ra.indirect(off), None, a_ra, a_r)
                gap("rb%d" % lv)
            tab["m"] = v_m = tt(ma, mn.indirect(off), base[0], A.min, v_l, v_m, v_cp)
            gap("a%d" % lv)
            t = scan(fr(r, "s%d" % (lv + 1)), m16[:, 0:64], ra, a_ra)
            v_m = tt(mb, ma.indirect(off), base[1], A.min, v_m)
            v_l = wrap(wr(r, "l%d" % (lv + 1)), fr(r, "s%d" % (lv + 1), 15, 64, 16), t)
            gap("l%d" % (lv + 1))
            rw, mn, base = rb, mb, (ma, ma)
        off = wr(r, "l4")
        v_m = tt(fr(r, "m9"), mn.indirect(off), base[0], A.min, v_l, v_m)
        gap("m9")
        tt(d1[:, 0:192:3], mn.indirect(off), T.ke[:], A.is_equal)
        t = tt(d1[:, 1:192:3], fr(r, "m9").indirect(wr(r, "u")), T.ke[:], A.is_equal, v_m, tab["u"])
        gap("f")
        t = chain(fr(r, "so", 0, 192), d0[:, 0:192], d1[:, 0:192], t, tab["dd"], tab["b"], tab["g"], g_d)
        tc = fr(r, "so", 5, 192, 6)
        clo = ts(wr(r, "lo"), tc, 4.0, tau, A.mult, A.add, t)
        th = tt(fr(r, "hi"), T.cc[:, 32:64], tc, A.subtract)
        ctn = ts(wr(r, "tn"), tc, col(23), None, A.add, None)

        def new_list():
            return act(fr(r + 1, "nn"), fr(r, "kk").indirect(wr(r, "tn")), None, ctn, tab["kk"])


        def layer(qz, qzs, banks, tok):
            out = []
            for b in range(4):
                out.append(mm(banks[b], 128, T.wq[:, 128 * b:128 * b + 128], T.wqs[:, 128 * b:128 * b + 128], qz, qzs,
                              tok, t_wc, t_ws, *bankuse[banks[b]]))
            return out

        def scaled(on, out, bank, a, p):
            t = ts(out, psv(bank, a, 128), 0.03125, None, A.mult, None, p) if on == "v" else act(out, psv(bank, a, 128), 0.03125, p)
            bankuse[bank] = [t]
            return t

        def nm(s):
            return T["%s_%d" % (s, r)]
        pl = T["xs%d" % r]
        n1 = 4 * AHEAD if two else 512

        def rest(a, b):
            return tt(Z[:, a:b], xk[:].indirect(wr(r, "hi", a // 16 - 32, b // 16 - 32)), xk2[:, a:b], A.add, tab["xl"])
        z0 = None
        if two:
            z0 = act(Z[:, n1:512], xk2[:, 1024 - 8 * AHEAD:2048 - 8 * AHEAD].indirect(wr(r, "lo", n1 // 16, 32)), None, clo, tab["zc"], tab["xj"], ("dy%d" % r, 16))
        exchanged(r, 0, tab["kk"])
        z1 = tt(Z[:, 0:n1], xk[:].indirect(wr(r, "lo", 0, n1 // 16)), xk2[:, 0:n1], A.add, clo, tab["xk"], tab["xj"])
        chi = ts(wr(r, "hi"), fr(r, "hi"), 4.0, tau, A.mult, A.add, th)
        gap("z1")
        tq = quant(nm("qz")[:, 0:128], pl[:, 256:384], Z[:, 0:512], z0, z1)
        p1 = layer(nm("qz")[:, 0:128], pl[:, 256:384], (0, 1, 2, 3), tq)
        if two:
            z0 = act(Z[:, 608:768], zh[:].indirect(wr(r, "hi", 6, 16)), None, chi, tab["zh"])
            z2 = vcopy(Z[:, 512:608], zh[:].indirect(wr(r, "hi", 0, 6)), chi, tab["zh"])
        tab["kk"] = exchanged(r, 1)
        if two:
            h1 = [scaled("a", H[:, 0:512:4], 0, 0, p1[0])]
        else:
            a_n = new_list()
            z2 = tt(Z[:, 512:768], xk[:].indirect(wr(r, "hi", 0, 16)), xk2[:, 512:768], A.add, chi)
            h1 = [scaled("a", H[:, b:512:4], b, 0, p1[b]) for b in range(3)]
        gap("z2")
        tq = quant(nm("qz")[:, 128:256], pl[:, 640:768], Z[:, 256:768], z2, z0)
        p2 = layer(nm("qz")[:, 128:256], pl[:, 640:768], (4, 5, 6, 7), tq)
        if two:
            h1 += [scaled("va"[b - 1], H[:, b:512:4], b, 0, p1[b]) for b in (1, 2)]
        h1.append(scaled("v", H[:, 3:512:4], 3, 0, p1[3]))
        gap("h1")
        tq1 = quant(nm("qh")[:, 0:128], pl[:, 384:512], H[:, 0:512], *h1)
        h2 = [scaled("aavv"[b], H[:, 512 + b:768:4], 4 + b, 64, p2[b]) for b in range(4)]
        gap("h2")
        if two:
            rest(768, 832)
            a_n = new_list()
        tq2 = quant(nm("qh")[:, 128:256], pl[:, 512:640], H[:, 256:768], *h2)

        wait("g", tq1)
        na = remote(r, nm("cin")[:, 0:128].bitcast(dt.uint8), nm("qh")[:, 0:128].bitcast(dt.uint8), "ra%d" % r)
        na += remote(r, nm("la")[:, 0:128], pl[:, 384:512], "ra%d" % r)
        wait("g", tq2)
        nb = remote(r, nm("cin")[:, 128:192].bitcast(dt.uint8), nm("qh")[:, 192:256].bitcast(dt.uint8), "rb%d" % r)
        nb += remote(r, nm("la")[:, 128:192], pl[:, 576:640], "rb%d" % r)
        if r == 0:
            t_v = dma("g", "dv", 16, T.vt[:], T.v[:])

        z3 = rest(832 if r else 768, 1024)

        def latch():
            t16 = scan(fr(r + 1, "n16", 0, 128), m16[:, 0:128], half(r + 1, 0), a_n)
            t4 = four(r + 1, 1)
            return t16, (t4 if last else four(r + 1, 0))
        if r == 0:
            t16, t4 = latch()
        tq = quant(nm("qz")[:, 256:384], pl[:, 768:896], Z[:, 512:1024], z3)
        p = layer(nm("qz")[:, 256:384], pl[:, 768:896], (0, 1, 2, 3), tq)
        gap("z3")
        if r == 0:
            t = scan(T.pf[:, 96:192], m16[:, 0:96], T.pf[:, 0:96], g_pf)
            t2 = fill(T.tk[:, 80:160], 1.0)
        else:
            t16, t4 = latch()
        ts(wr(r + 1, "n8"), fr(r + 1, "n16", 15, 128, 16), un16, 1.0, A.mult, A.subtract, t16)
        v_n = ts(wr(r + 1, "n4"), fr(r + 1, "n4", 128 + 3, 256, 4), col(21), col(26), A.mult, A.add, t4)
        if not last:
            v_k4 = four_end(r + 1, t4)
        if r == 0:
            v_pf = ts(T.pl[:, 0:6], T.pf[:, 111:192:16], un16, 1.0, A.mult, A.subtract, t)
            v_tk = fill(T.tk[:, 80:160:20], 0.0, t2)
        bt = [[scaled("vava"[b], B[:, 256 * b + 192:256 * b + 256], b, 64, p[b])] for b in range(4)]
        if r == 1:
            v_v = quant(T.vq[:, 0:128], T.vqs[:, 0:128], T.vt[:], t_v)

        cin = nm("cin")
        p = []
        for b in range(4):
            p.append(mm(4 + b, 128, T.eq[:, 128 * b:128 * b + 128], T.es[:, 128 * b:128 * b + 128], cin[:, 0:128], nm("la")[:, 0:128],
                        ("ra%d" % r, na), tab["e"], *bankuse[4 + b]))
        for b in range(4):
            o, i = B[:, 256 * b:256 * b + 128], psv(4 + b, 0, 128)
            t = act(o, i, None, p[b]) if b % 2 else vcopy(o, i, p[b])
            bankuse[4 + b] = [t]
            bt[b].append(t)
        p = []
        for b in range(4):
            p.append(mm(b, 128, T.eq[:, 128 * b:128 * b + 128], T.es[:, 128 * b:128 * b + 128], cin[:, 64:192], nm("la")[:, 64:192],
                        ("rb%d" % r, nb), *bankuse[b]))
        for b in range(4):
            o, i = B[:, 256 * b + 128:256 * b + 192], psv(b, 64, 128)
            t = act(o, i, None, p[b]) if b else vcopy(o, i, p[b])
            bankuse[b] = [t]
            bt[b].append(t)

        nx = T["x%d" % (r + 1)]
        nq, ns = T["xq%d" % (r + 1)], T["xs%d" % (r + 1)]
        for b in range(4):
            g1 = tt(nx[:, b:512:4], B[:, 256 * b:256 * b + 256].indirect(wr(r + 1, "n8")), X[:, b:512:4], A.add, v_n, *bt[b])
        g2 = tt(nx[:, 512:1024], B[:].indirect(wr(r + 1, "n4")), X[:, 512:1024], A.add)
        if not last:
            t = act(fr(r + 1, "kt"), fr(r + 1, "nn").indirect(fi[:, 24:42]), None, a_n, tab["fi"])
            if r == 0:
                for a in range(3):
                    v_wt = act(T.w2[:, 96 * a:96 * a + 80], wt[:, 96 * a:96 * a + 80].indirect(T.pl[:, 0:5]), None, v_pf)
            for a in range(3):
                a_kt = act(fr(r + 1, "k2", 96 * a, 96 * a + 96), fr(r + 1, "kt", 96 * a, 96 * a + 96).indirect(T.pl[:, 0:6]), None, t)
        else:
            fun(ID, T.kyf[:, 0:128], half(r + 1, 0), 1.0, -1.0)
            a_ky = fun(ID, T.kyf[:, 128:256], half(r + 1, 1), 1.0, -1.0)
        v_q1 = quant(nq[:, 0:128], ns[:, 0:128], nx[:, 0:512], g1)
        v_q2 = quant(nq[:, 128:256], ns[:, 128:256], nx[:, 512:1024], g2)
        x_done = (g1, g2)
        if not last:
            tab["tl"] = scan(fr(r + 1, "st", 0, 192), m16, fr(r + 1, "k2", 0, 192), a_kt)
            tab["n16"] = scan(fr(r + 1, "n16", 128, 256), m16[:, 0:128], half(r + 1, 1))

    nd = [0]

    def out(q, o, i, *toks):
        wait(q, *toks)
        queues[q].dma_start(o, i).then_inc(T.sem.dout, 16)
        nd[0] += 16
    xq, xs = T["xq%d" % ROUNDS], T["xs%d" % ROUNDS]
    p1 = scores(T.vq, T.vqs, ROUNDS, 0, v_q1, v_v)
    p2 = scores(T.vq, T.vqs, ROUNDS, 1, v_q2)
    y1 = vcopy(T.yo[:, 0:128], psv(4, 0, 128), p1)
    y2 = vcopy(T.yo[:, 128:256], psv(5, 0, 128), p2)
    out("a", T.osc[0:4, :], xs[0:4, :], v_q2)
    out("a", T.osc[8:12, :], xs[64:68, :])
    out("y", T.kp[:], T.kyf[0:128:16, :], a_ky)
    out("y", T.oc[:], xq[:, 0:256].bitcast(dt.uint8), v_q2)
    out("y", T.osc[4:8, :], xs[32:36, :])
    out("y", T.osc[12:16, :], xs[96:100, :])
    out("a", T.y[:, 0:128], T.yo[:, 0:128], y1)
    out("y", T.y[:, 128:256], T.yo[:, 128:256], y2)

    wait("g", ("dout", nd[0]), ("loc", loc[0]), *[(s, n) for s, n in done.items()])
